import numpy as np
import ml_dtypes


def mxq(x, axis, fmt="e4m3"):
    dtype, down = {"e4m3": (ml_dtypes.float8_e4m3fn, 7), "e5m2": (ml_dtypes.float8_e5m2, 14)}[fmt]
    v = np.moveaxis(np.asarray(x, np.float32).astype(ml_dtypes.bfloat16).astype(np.float64), axis, -1)
    blocks = v.reshape(v.shape[:-1] + (-1, 32))
    amax = np.abs(blocks).max(-1, keepdims=True)
    byte = np.maximum(np.where(amax > 0, np.frexp(amax)[1] - 1 + 127, 0) - down, 1)
    scale = np.exp2(byte - 127.0)
    codes = (blocks / scale).astype(np.float32).astype(dtype).astype(np.float64)
    return np.moveaxis((codes * scale).reshape(v.shape), -1, axis)


WIDE = False


def mx_kscale(k):
    if not WIDE:
        return np.ones(k)
    levels = np.array([24, -24, 12, -12, 0])
    if k % 512:
        return np.exp2(np.random.permutation(np.resize(levels, k // 32))).repeat(32)
    a = np.empty((k // 512, 16))
    for p in range(k // 512):
        a[p, :8] = np.random.permutation(np.resize(levels, 8))
        for g in range(8):
            far = levels[np.abs(levels - a[p, g]) >= 10]
            a[p, g + 8] = far[np.random.randint(len(far))]
    return np.exp2(a.ravel()).repeat(32)


def f64(x):
    return np.asarray(x).astype(np.float64)


def striped(idx):
    return np.tile(idx.reshape(-1, 16).T, (8, 1)).astype(np.uint16)


def unstriped(offs):
    return offs[:16].T.reshape(-1).astype(np.int64)


E2M1 = np.array([0.0, 0.5, 1.0, 1.5, 2.0, 3.0, 4.0, 6.0, -0.0, -0.5, -1.0, -1.5, -2.0, -3.0, -4.0, -6.0])


def pack_weight(w, fmt):
    k, n = w.shape
    w = f64(np.asarray(w, np.float32).astype(ml_dtypes.bfloat16)).reshape(k // 32, 32, n)
    amax = np.abs(w).max(1)
    if fmt == "e4m3":
        byte = np.frexp(amax)[1] - 1 + 127 - 7
    else:
        mant, ex = np.frexp(amax / 6.0)
        byte = np.where(mant > 0.5, ex, ex - 1) + 127
    byte = np.clip(np.where(amax > 0, byte, 1), 1, 254)
    scaled = (w * np.exp2(127.0 - byte)[:, None, :]).reshape(k, n).astype(np.float32)
    by_word = np.ascontiguousarray(scaled.reshape(k // 512, 128, 4, n).transpose(0, 1, 3, 2))
    if fmt == "e4m3":
        words = by_word.astype(ml_dtypes.float8_e4m3fn).view(np.uint8)
    else:
        c = by_word.astype(ml_dtypes.float4_e2m1fn).view(np.uint8) & 0xF
        words = (c[..., 0::2] | (c[..., 1::2] << 4)).reshape(k // 512, 128, 2 * n)
    return np.ascontiguousarray(words), np.ascontiguousarray(byte.astype(np.uint8).reshape(k // 512, 16, n))


def unpack_weight(words, scales, fmt):
    g, _, n = scales.shape
    words = np.ascontiguousarray(words).reshape(g, 128, n, -1)
    if fmt == "e4m3":
        vals = words.view(ml_dtypes.float8_e4m3fn).astype(np.float64)
    else:
        nib = np.empty((g, 128, n, 4), np.uint8)
        nib[..., 0::2] = words & 0xF
        nib[..., 1::2] = words >> 4
        vals = E2M1[nib]
    vals = vals * np.repeat(np.exp2(scales.astype(np.float64) - 127.0), 8, axis=1)[..., None]
    return vals.transpose(0, 1, 3, 2).reshape(g * 512, n)


K, R, N, T, J = 1024, 1024, 512, 2048, 1024


def setup_inputs():
    n = np.random.standard_normal
    s = mx_kscale(K)[:, None]
    u = mx_kscale(R)[:, None]
    p_tab = pack_weight(n((K, T)) * s, "e4m3")
    p_ws = pack_weight(n((K, R)) / np.sqrt(2 * K) / s * u.T, "e4m3")
    p_wt = pack_weight(n((K, R)) / np.sqrt(2 * K) / s * u.T, "e2m1")
    p_wd = pack_weight(n((R, N)) / np.sqrt(R) / u, "e2m1")
    return {
        "tab_words": p_tab[0],
        "tab_scales": p_tab[1],
        "ws_words": p_ws[0],
        "ws_scales": p_ws[1],
        "wt_words": p_wt[0],
        "wt_scales": p_wt[1],
        "wd_words": p_wd[0],
        "wd_scales": p_wd[1],
        "wgo": np.tile(np.random.uniform(0.5, 2.0, J), (128, 1)).astype(np.float32),
        "offs": striped(np.random.permutation(T)[:J]),
        "offs2": striped(np.random.permutation(T)[:J]),
    }


def reference(tab_words, tab_scales, ws_words, ws_scales, wt_words, wt_scales, wd_words, wd_scales, wgo, offs, offs2):
    idx = unstriped(offs)
    idx2 = unstriped(offs2)
    tab_ = unpack_weight(tab_words, tab_scales, "e4m3")[:, idx]
    tabb_ = unpack_weight(tab_words, tab_scales, "e4m3")[:, idx2]
    ws_ = unpack_weight(ws_words, ws_scales, "e4m3")
    wt_ = unpack_weight(wt_words, wt_scales, "e2m1")
    a = ws_.T @ tab_ + wt_.T @ tabb_
    h = a
    h_ = mxq(h, 0, "e4m3")
    wd_ = unpack_weight(wd_words, wd_scales, "e2m1")
    y = wd_.T @ h_
    out = np.zeros((N, T))
    out[:, idx2] = f64(wgo)[0] * (y)
    return out

@@ -1,0 +1,216 @@
+from contextlib import ExitStack
+
+import concourse.mybir as mybir
+from concourse.masks import make_identity
+
+K, R, N, T, J = 1024, 1024, 512, 2048, 1024
+FLOPS = 2 * (2 * K * R * J + R * N * J)
+
+F32 = mybir.dt.float32
+BF16 = mybir.dt.bfloat16
+I32 = mybir.dt.int32
+U32 = mybir.dt.uint32
+U16 = mybir.dt.uint16
+U8 = mybir.dt.uint8
+FP8X4 = mybir.dt.float8_e4m3fn_x4
+FP4X4 = mybir.dt.float4_e2m1fn_x4
+
+P = 128
+BANK = 512
+CHUNK = 256
+CHUNKS = J // CHUNK
+BLOCKS = CHUNK // P
+N_TILES = N // P
+ALIGN = 64
+
+
+def tile_list_msg_none_none_kernel(
+    tc, tab_words, tab_scales, ws_words, ws_scales, wt_words, wt_scales, wd_words, wd_scales, wgo, offs, offs2, out
+):
+    nc = tc.nc
+    with ExitStack() as ctx:
+        keep = ctx.enter_context(tc.tile_pool(name="keep", bufs=1))
+        psum = ctx.enter_context(tc.psum_pool(name="psum", bufs=1))
+
+        src_list = keep.tile([P, J // 16], U16)
+        dst_list = keep.tile([P, J // 16], U16)
+        tab = keep.tile([P, 2, T], I32, align_bytes=ALIGN)
+        tab_sc = keep.tile([P, T // 4], I32, align_bytes=ALIGN)
+        ws = keep.tile([P, 2, R], I32, align_bytes=ALIGN)
+        ws_sc = keep.tile([P, R // 4], I32, align_bytes=ALIGN)
+        wt = keep.tile([P, 2, R // 2], I32, align_bytes=ALIGN)
+        wt_sc = keep.tile([P, 2, R // 4], I32, align_bytes=ALIGN)
+        wd = keep.tile([P, 2, N // 2], I32, align_bytes=ALIGN)
+        wd_sc = keep.tile([P, 2, N // 4], I32, align_bytes=ALIGN)
+        weight = keep.tile([P, J], F32)
+        src = [keep.tile([P, 2, CHUNK], U32, name="src%d" % a, align_bytes=ALIGN) for a in range(2)]
+        dst = [keep.tile([P, 2, CHUNK], U32, name="dst%d" % a, align_bytes=ALIGN) for a in range(2)]
+        src_sc = keep.tile([P, J], U8, align_bytes=ALIGN)
+        h_rows = keep.tile([P, BLOCKS, 2, BANK], BF16)
+        grouped = keep.tile([P, 2, 2, CHUNK, 2], F32, align_bytes=ALIGN)
+        h_codes = keep.tile([P, CHUNKS, 2, CHUNK], U32, align_bytes=ALIGN)
+        h_sc = keep.tile([P, CHUNKS, 2, CHUNK], U8, align_bytes=ALIGN)
+        acc_h = [[psum.tile([P, BANK], F32, name="acc_h%d%d" % (blk, b)) for b in range(2)] for blk in range(BLOCKS)]
+        side = [psum.tile([P, BANK], F32, name="side%d" % i) for i in range(4)]
+        dst_sc = keep.tile([P, J], U8, align_bytes=ALIGN)
+        dst_sc1 = keep.tile([P, J // 4], I32, align_bytes=ALIGN)
+        ident = keep.tile([P, P], F32)
+        y_sb = [keep.tile([P, J], F32, name="y%d" % t) for t in range(N_TILES)]
+        placed = [keep.tile([P, T], F32, name="placed%d" % t) for t in range(N_TILES)]
+
+        nc.vector.memset(tab_sc[:], 0)
+        nc.gpsimd.memset(wt_sc[:], 0)
+        nc.gpsimd.memset(ws_sc[:], 0)
+        nc.gpsimd.memset(dst_sc1[:], 0)
+        nc.gpsimd.memset(wd_sc[:], 0)
+        make_identity(nc, ident[:])
+        for t in range(N_TILES):
+            nc.gpsimd.memset(placed[t][:], 0.0)
+
+        def load_packed(plane, scales, q):
+            nc.sync.dma_start(out=plane[32 * q : 32 * q + 8, :], in_=scales.bitcast(I32)[:, 4 * q : 4 * q + 4, :])
+
+        def load_side_by_side(plane, scales, q):
+            nc.sync.dma_start(
+                out=plane[32 * q : 32 * q + 4, :, :],
+                in_=scales.bitcast(I32)[:, 4 * q : 4 * q + 4, :].rearrange("a r n -> r a n"),
+            )
+
+        def words8(w):
+            return w.rearrange("a p c i -> p a (c i)").bitcast(I32)
+
+        nc.sync.dma_start(dst_list[:], offs2)
+        for q in range(4):
+            load_packed(tab_sc, tab_scales, q)
+        nc.sync.dma_start(src_list[:], offs)
+        nc.sync.dma_start(out=wt[:], in_=wt_words.bitcast(I32).rearrange("a p c -> p a c"))
+        nc.sync.dma_start(out=tab[:], in_=words8(tab_words))
+        for q in range(4):
+            load_side_by_side(wt_sc, wt_scales, q)
+        for q in range(2):
+            load_packed(ws_sc, ws_scales, q)
+        nc.sync.dma_start(out=ws[:], in_=words8(ws_words))
+        for q in range(2, 4):
+            load_packed(ws_sc, ws_scales, q)
+        nc.sync.dma_start(out=wd[:], in_=wd_words.bitcast(I32).rearrange("a p c -> p a c"))
+        for q in range(4):
+            load_side_by_side(wd_sc, wd_scales, q)
+        nc.sync.dma_start(out=weight[:], in_=wgo)
+
+        def listed(offsets, c):
+            return offsets[:, c * CHUNK // 16 : (c + 1) * CHUNK // 16]
+
+        def gather_chunk(c):
+            for into, offsets in ((dst, dst_list), (src, src_list)):
+                for a in range(2):
+                    nc.vector.tensor_copy(into[a][:, c % 2, :], tab[:, a, :].bitcast(U32).indirect(listed(offsets, c)))
+
+        def first_pass(c, blk, b, step):
+            a = step % 2
+            cols = slice(blk * P, (blk + 1) * P)
+            edges = slice(c * CHUNK + blk * P, c * CHUNK + (blk + 1) * P)
+            if step < 2:
+                lhsT = dst[a][:, c % 2, cols].bitcast(FP8X4)
+                lhsT_scale = dst_sc[:, edges] if a == 0 else dst_sc1[:].bitcast(U8)[:, edges]
+                rhs = wt[:, a, :].bitcast(U8)[:, 2 * BANK * b : 2 * BANK * (b + 1)].bitcast(FP4X4)
+                rhs_scale = wt_sc[:, a, :].bitcast(U8)[:, BANK * b : BANK * (b + 1)]
+            else:
+                lhsT = src[a][:, c % 2, cols].bitcast(FP8X4)
+                lhsT_scale = src_sc[4 * a : P, edges]
+                rhs = ws[:, a, BANK * b : BANK * (b + 1)].bitcast(FP8X4)
+                rhs_scale = ws_sc[4 * a : P, :].bitcast(U8)[:, BANK * b : BANK * (b + 1)]
+            nc.tensor.matmul_mx(
+                out=acc_h[blk][b][:],
+                lhsT=lhsT,
+                lhsT_scale=lhsT_scale,
+                rhs=rhs,
+                rhs_scale=rhs_scale,
+                start=(step == 0),
+                stop=(step == 3),
+            )
+
+        def round_rows(blk):
+            for b in range(2):
+                nc.scalar.copy(
+                    out=h_rows[:, blk, b, :].rearrange("j (u p e) -> j u p e", u=2, e=2),
+                    in_=acc_h[blk][b][:].rearrange("j (p u e) -> j u p e", u=2, e=2),
+                )
+
+        def first_product(c, blk):
+            for step in range(4):
+                for b in range(2):
+                    first_pass(c, blk, b, step)
+            round_rows(blk)
+
+        def turn_and_quantise(c):
+            for blk in range(BLOCKS):
+                turned = side[blk][:].rearrange("p (b u j) -> p b u j", b=2, u=2)
+                words = h_rows[:, blk, :, :].rearrange("j b r -> j (b r)").bitcast(F32)
+                for b in (1, 0):
+                    for u in range(2):
+                        w0 = (2 * b + u) * P
+                        nc.tensor.transpose(turned[:, b, u, :], words[:, w0 : w0 + P], ident[:])
+                nc.scalar.copy(
+                    out=grouped[:, c % 2, :, blk * P : (blk + 1) * P, :], in_=turned.rearrange("p b u j -> p b j u")
+                )
+            nc.vector.quantize_mx(
+                out=h_codes[:, c, :, :].rearrange("p b j -> p (b j)").bitcast(FP8X4),
+                scales=h_sc[:, c, :, :].rearrange("p b j -> p (b j)"),
+                in_=grouped[:, c % 2, :, :, :].rearrange("p b j u -> p (b j u)").bitcast(BF16),
+            )
+
+        def second_product(c, pair, bank):
+            for i in range(2):
+                t = 2 * pair + i
+                for blk in range(BLOCKS):
+                    cols = slice(blk * P, (blk + 1) * P)
+                    for b in range(2):
+                        nc.tensor.matmul_mx(
+                            out=bank[:, i * CHUNK + blk * P : i * CHUNK + (blk + 1) * P],
+                            lhsT=wd[:, b, :].bitcast(U8)[:, 2 * P * t : 2 * P * (t + 1)].bitcast(FP4X4),
+                            lhsT_scale=wd_sc[:, b, :].bitcast(U8)[:, P * t : P * (t + 1)],
+                            rhs=h_codes[:, c, b, cols].bitcast(FP8X4),
+                            rhs_scale=h_sc[:, c, b, cols],
+                            start=(b == 0),
+                            stop=(b == 1),
+                        )
+            for i in range(2):
+                nc.scalar.copy(
+                    out=y_sb[2 * pair + i][:, c * CHUNK : (c + 1) * CHUNK], in_=bank[:, i * CHUNK : (i + 1) * CHUNK]
+                )
+
+        nc.vector.tensor_copy(dst_sc[:], tab_sc[:].bitcast(U8).indirect(dst_list[:]))
+        nc.scalar.dma_start(out=dst_sc1[0 : P - 4, :], in_=dst_sc[4:P, :].bitcast(I32))
+        nc.vector.tensor_copy(src_sc[:], tab_sc[:].bitcast(U8).indirect(src_list[:]))
+        gather_chunk(0)
+        gather_chunk(1)
+
+        for step in range(4):
+            for blk in range(BLOCKS):
+                for b in range(2):
+                    first_pass(0, blk, b, step)
+        for blk in range(BLOCKS):
+            round_rows(blk)
+        gather_chunk(2)
+
+        for c in range(CHUNKS):
+            turn_and_quantise(c)
+            if c > 0:
+                second_product(c - 1, 1, side[1])
+            if c + 1 < CHUNKS:
+                first_product(c + 1, 0)
+            second_product(c, 0, side[2])
+            if c + 1 < CHUNKS:
+                first_product(c + 1, 1)
+            if c == 0:
+                gather_chunk(3)
+        second_product(CHUNKS - 1, 1, side[3])
+
+        for c in range(CHUNKS):
+            for t in range(N_TILES):
+                cols = slice(c * CHUNK, (c + 1) * CHUNK)
+                nc.vector.tensor_tensor(
+                    placed[t][:].indirect(listed(dst_list, c)), y_sb[t][:, cols], weight[:, cols], mybir.AluOpType.mult
+                )
+                if c == CHUNKS - 1:
+                    nc.sync.dma_start(out=out[t * P : (t + 1) * P, :], in_=placed[t][:])

@@ -30,6 +30,7 @@ def tile_list_msg_none_none_kernel(
     nc = tc.nc
     with ExitStack() as ctx:
         keep = ctx.enter_context(tc.tile_pool(name="keep", bufs=1))
+        shared = ctx.enter_context(tc.tile_pool(name="shared", bufs=1))
         psum = ctx.enter_context(tc.psum_pool(name="psum", bufs=1))
 
         src_list = keep.tile([P, J // 16], U16)
@@ -56,16 +57,16 @@ def tile_list_msg_none_none_kernel(
         dst_sc1 = keep.tile([P, J // 4], I32, align_bytes=ALIGN)
         ident = keep.tile([P, P], F32)
         y_sb = [keep.tile([P, J], F32, name="y%d" % t) for t in range(N_TILES)]
-        placed = [keep.tile([P, T], F32, name="placed%d" % t) for t in range(N_TILES)]
+        placed = [keep.tile([P, T], F32, name="placed%d" % t) for t in range(2)]
+        first_rows = shared.tile([P, 2, BANK], BF16, offset=4 * T - 2 * BANK)
+        placed += [shared.tile([P, T], F32, name="placed%d" % t, offset=4 * T * (t - 2)) for t in range(2, 4)]
 
         nc.vector.memset(tab_sc[:], 0)
-        nc.gpsimd.memset(wt_sc[:], 0)
-        nc.gpsimd.memset(ws_sc[:], 0)
-        nc.gpsimd.memset(dst_sc1[:], 0)
-        nc.gpsimd.memset(wd_sc[:], 0)
+        nc.vector.memset(wt_sc[:], 0)
+        nc.vector.memset(ws_sc[:], 0)
+        nc.vector.memset(dst_sc1[:], 0)
+        nc.vector.memset(wd_sc[:], 0)
         make_identity(nc, ident[:])
-        for t in range(N_TILES):
-            nc.gpsimd.memset(placed[t][:], 0.0)
 
         def load_packed(plane, scales, q):
             nc.sync.dma_start(out=plane[32 * q : 32 * q + 8, :], in_=scales.bitcast(I32)[:, 4 * q : 4 * q + 4, :])
@@ -129,10 +130,13 @@ def tile_list_msg_none_none_kernel(
                 stop=(step == 3),
             )
 
-        def round_rows(blk):
+        def rows_of(c, blk):
+            return first_rows[:] if (c, blk) == (0, 0) else h_rows[:, blk, :, :]
+
+        def round_rows(c, blk):
             for b in range(2):
                 nc.scalar.copy(
-                    out=h_rows[:, blk, b, :].rearrange("j (u p e) -> j u p e", u=2, e=2),
+                    out=rows_of(c, blk)[:, b, :].rearrange("j (u p e) -> j u p e", u=2, e=2),
                     in_=acc_h[blk][b][:].rearrange("j (p u e) -> j u p e", u=2, e=2),
                 )
 
@@ -140,12 +144,12 @@ def tile_list_msg_none_none_kernel(
             for step in range(4):
                 for b in range(2):
                     first_pass(c, blk, b, step)
-            round_rows(blk)
+            round_rows(c, blk)
 
         def turn_and_quantise(c):
             for blk in range(BLOCKS):
                 turned = side[blk][:].rearrange("p (b u j) -> p b u j", b=2, u=2)
-                words = h_rows[:, blk, :, :].rearrange("j b r -> j (b r)").bitcast(F32)
+                words = rows_of(c, blk).rearrange("j b r -> j (b r)").bitcast(F32)
                 for b in (1, 0):
                     for u in range(2):
                         w0 = (2 * b + u) * P
@@ -159,9 +163,8 @@ def tile_list_msg_none_none_kernel(
                 in_=grouped[:, c % 2, :, :, :].rearrange("p b j u -> p (b j u)").bitcast(BF16),
             )
 
-        def second_product(c, pair, bank):
-            for i in range(2):
-                t = 2 * pair + i
+        def second_product(c, tiles, bank):
+            for i, t in enumerate(tiles):
                 for blk in range(BLOCKS):
                     cols = slice(blk * P, (blk + 1) * P)
                     for b in range(2):
@@ -174,14 +177,14 @@ def tile_list_msg_none_none_kernel(
                             start=(b == 0),
                             stop=(b == 1),
                         )
-            for i in range(2):
-                nc.scalar.copy(
-                    out=y_sb[2 * pair + i][:, c * CHUNK : (c + 1) * CHUNK], in_=bank[:, i * CHUNK : (i + 1) * CHUNK]
-                )
+            for i, t in enumerate(tiles):
+                nc.scalar.copy(out=y_sb[t][:, c * CHUNK : (c + 1) * CHUNK], in_=bank[:, i * CHUNK : (i + 1) * CHUNK])
 
         nc.vector.tensor_copy(dst_sc[:], tab_sc[:].bitcast(U8).indirect(dst_list[:]))
         nc.scalar.dma_start(out=dst_sc1[0 : P - 4, :], in_=dst_sc[4:P, :].bitcast(I32))
         nc.vector.tensor_copy(src_sc[:], tab_sc[:].bitcast(U8).indirect(src_list[:]))
+        for t in range(2):
+            nc.vector.memset(placed[t][:], 0.0)
         gather_chunk(0)
         gather_chunk(1)
 
@@ -190,27 +193,33 @@ def tile_list_msg_none_none_kernel(
                 for b in range(2):
                     first_pass(0, blk, b, step)
         for blk in range(BLOCKS):
-            round_rows(blk)
+            round_rows(0, blk)
         gather_chunk(2)
 
+        last = CHUNKS - 1
         for c in range(CHUNKS):
             turn_and_quantise(c)
-            if c > 0:
-                second_product(c - 1, 1, side[1])
-            if c + 1 < CHUNKS:
+            if c == 0:
+                for t in range(2, 4):
+                    nc.vector.memset(placed[t][:], 0.0)
+            else:
+                second_product(c - 1, (2, 3) if c < last else (2,), side[1])
+            if c < last:
                 first_product(c + 1, 0)
-            second_product(c, 0, side[2])
-            if c + 1 < CHUNKS:
+            second_product(c, (0, 1), side[2])
+            if c < last:
                 first_product(c + 1, 1)
             if c == 0:
                 gather_chunk(3)
-        second_product(CHUNKS - 1, 1, side[3])
+        second_product(last - 1, (3,), side[2])
+        second_product(last, (2, 3), side[3])
 
-        for c in range(CHUNKS):
-            for t in range(N_TILES):
-                cols = slice(c * CHUNK, (c + 1) * CHUNK)
-                nc.vector.tensor_tensor(
-                    placed[t][:].indirect(listed(dst_list, c)), y_sb[t][:, cols], weight[:, cols], mybir.AluOpType.mult
-                )
-                if c == CHUNKS - 1:
-                    nc.sync.dma_start(out=out[t * P : (t + 1) * P, :], in_=placed[t][:])
+        order = [(c, t) for c in range(last) for t in range(N_TILES)]
+        order = order[:-1] + [(last, 0), (last, 1), order[-1], (last, 2), (last, 3)]
+        for c, t in order:
+            cols = slice(c * CHUNK, (c + 1) * CHUNK)
+            nc.vector.tensor_tensor(
+                placed[t][:].indirect(listed(dst_list, c)), y_sb[t][:, cols], weight[:, cols], mybir.AluOpType.mult
+            )
+            if c == last:
+                nc.sync.dma_start(out=out[t * P : (t + 1) * P, :], in_=placed[t][:])

@@ -35,7 +35,7 @@ def tile_list_msg_none_none_kernel(
 
         src_list = keep.tile([P, J // 16], U16)
         dst_list = keep.tile([P, J // 16], U16)
-        tab = keep.tile([P, 2, T], I32, align_bytes=ALIGN)
+        tab = [keep.tile([P, T], I32, name="tab%d" % a, align_bytes=ALIGN) for a in range(2)]
         tab_sc = keep.tile([P, T // 4], I32, align_bytes=ALIGN)
         ws = keep.tile([P, 2, R], I32, align_bytes=ALIGN)
         ws_sc = keep.tile([P, R // 4], I32, align_bytes=ALIGN)
@@ -44,13 +44,14 @@ def tile_list_msg_none_none_kernel(
         wd = keep.tile([P, 2, N // 2], I32, align_bytes=ALIGN)
         wd_sc = keep.tile([P, 2, N // 4], I32, align_bytes=ALIGN)
         weight = keep.tile([P, J], F32)
-        src = [keep.tile([P, 2, CHUNK], U32, name="src%d" % a, align_bytes=ALIGN) for a in range(2)]
-        dst = [keep.tile([P, 2, CHUNK], U32, name="dst%d" % a, align_bytes=ALIGN) for a in range(2)]
+        early = keep.tile([P, 2, 4, CHUNK], U32, align_bytes=ALIGN)
         src_sc = keep.tile([P, J], U8, align_bytes=ALIGN)
         h_rows = keep.tile([P, BLOCKS, 2, BANK], BF16)
         grouped = keep.tile([P, 2, 2, CHUNK, 2], F32, align_bytes=ALIGN)
         h_codes = keep.tile([P, CHUNKS, 2, CHUNK], U32, align_bytes=ALIGN)
         h_sc = keep.tile([P, CHUNKS, 2, CHUNK], U8, align_bytes=ALIGN)
+        first_grouped = shared.tile([P, 2, CHUNK, 2], F32, offset=8 * T, align_bytes=ALIGN)
+        late = shared.tile([P, 2, 4, CHUNK], U32, offset=8 * T, align_bytes=ALIGN)
         acc_h = [[psum.tile([P, BANK], F32, name="acc_h%d%d" % (blk, b)) for b in range(2)] for blk in range(BLOCKS)]
         side = [psum.tile([P, BANK], F32, name="side%d" % i) for i in range(4)]
         dst_sc = keep.tile([P, J], U8, align_bytes=ALIGN)
@@ -77,46 +78,56 @@ def tile_list_msg_none_none_kernel(
                 in_=scales.bitcast(I32)[:, 4 * q : 4 * q + 4, :].rearrange("a r n -> r a n"),
             )
 
-        def words8(w):
-            return w.rearrange("a p c i -> p a (c i)").bitcast(I32)
+        def words8(w, a):
+            return w[a].rearrange("p c i -> p (c i)").bitcast(I32)
 
         nc.sync.dma_start(dst_list[:], offs2)
         for q in range(4):
             load_packed(tab_sc, tab_scales, q)
-        nc.sync.dma_start(src_list[:], offs)
         nc.sync.dma_start(out=wt[:], in_=wt_words.bitcast(I32).rearrange("a p c -> p a c"))
-        nc.sync.dma_start(out=tab[:], in_=words8(tab_words))
+        nc.sync.dma_start(out=tab[0][:], in_=words8(tab_words, 0))
         for q in range(4):
             load_side_by_side(wt_sc, wt_scales, q)
-        for q in range(2):
+        nc.sync.dma_start(out=tab[1][:], in_=words8(tab_words, 1))
+        nc.sync.dma_start(src_list[:], offs)
+        nc.sync.dma_start(out=ws[:, 0, :], in_=words8(ws_words, 0))
+        for q in range(4):
             load_packed(ws_sc, ws_scales, q)
-        nc.sync.dma_start(out=ws[:], in_=words8(ws_words))
-        for q in range(2, 4):
-            load_packed(ws_sc, ws_scales, q)
+        nc.sync.dma_start(out=ws[:, 1, :], in_=words8(ws_words, 1))
         nc.sync.dma_start(out=wd[:], in_=wd_words.bitcast(I32).rearrange("a p c -> p a c"))
         for q in range(4):
             load_side_by_side(wd_sc, wd_scales, q)
         nc.sync.dma_start(out=weight[:], in_=wgo)
 
-        def listed(offsets, c):
-            return offsets[:, c * CHUNK // 16 : (c + 1) * CHUNK // 16]
+        def listed(offsets, c, chunks=1):
+            return offsets[:, c * CHUNK // 16 : (c + chunks) * CHUNK // 16]
 
-        def gather_chunk(c):
-            for into, offsets in ((dst, dst_list), (src, src_list)):
-                for a in range(2):
-                    nc.vector.tensor_copy(into[a][:, c % 2, :], tab[:, a, :].bitcast(U32).indirect(listed(offsets, c)))
+        def picked(c, step):
+            return (early if c < 2 else late)[:, c % 2, step, :]
+
+        def gather_scales(c):
+            nc.vector.tensor_copy(
+                src_sc[:, c * CHUNK : (c + 1) * CHUNK], tab_sc[:].bitcast(U8).indirect(listed(src_list, c))
+            )
+
+        def gather_words(c, step):
+            offsets = dst_list if step < 2 else src_list
+            nc.vector.tensor_copy(picked(c, step), tab[step % 2][:].bitcast(U32).indirect(listed(offsets, c)))
+
+        def grouped_of(c):
+            return first_grouped[:] if c == 0 else grouped[:, c % 2, :, :, :]
 
         def first_pass(c, blk, b, step):
             a = step % 2
             cols = slice(blk * P, (blk + 1) * P)
             edges = slice(c * CHUNK + blk * P, c * CHUNK + (blk + 1) * P)
             if step < 2:
-                lhsT = dst[a][:, c % 2, cols].bitcast(FP8X4)
+                lhsT = picked(c, step)[:, cols].bitcast(FP8X4)
                 lhsT_scale = dst_sc[:, edges] if a == 0 else dst_sc1[:].bitcast(U8)[:, edges]
                 rhs = wt[:, a, :].bitcast(U8)[:, 2 * BANK * b : 2 * BANK * (b + 1)].bitcast(FP4X4)
                 rhs_scale = wt_sc[:, a, :].bitcast(U8)[:, BANK * b : BANK * (b + 1)]
             else:
-                lhsT = src[a][:, c % 2, cols].bitcast(FP8X4)
+                lhsT = picked(c, step)[:, cols].bitcast(FP8X4)
                 lhsT_scale = src_sc[4 * a : P, edges]
                 rhs = ws[:, a, BANK * b : BANK * (b + 1)].bitcast(FP8X4)
                 rhs_scale = ws_sc[4 * a : P, :].bitcast(U8)[:, BANK * b : BANK * (b + 1)]
@@ -155,12 +166,12 @@ def tile_list_msg_none_none_kernel(
                         w0 = (2 * b + u) * P
                         nc.tensor.transpose(turned[:, b, u, :], words[:, w0 : w0 + P], ident[:])
                 nc.scalar.copy(
-                    out=grouped[:, c % 2, :, blk * P : (blk + 1) * P, :], in_=turned.rearrange("p b u j -> p b j u")
+                    out=grouped_of(c)[:, :, blk * P : (blk + 1) * P, :], in_=turned.rearrange("p b u j -> p b j u")
                 )
             nc.vector.quantize_mx(
                 out=h_codes[:, c, :, :].rearrange("p b j -> p (b j)").bitcast(FP8X4),
                 scales=h_sc[:, c, :, :].rearrange("p b j -> p (b j)"),
-                in_=grouped[:, c % 2, :, :, :].rearrange("p b j u -> p (b j u)").bitcast(BF16),
+                in_=grouped_of(c).rearrange("p b j u -> p (b j u)").bitcast(BF16),
             )
 
         def second_product(c, tiles, bank):
@@ -181,12 +192,17 @@ def tile_list_msg_none_none_kernel(
                 nc.scalar.copy(out=y_sb[t][:, c * CHUNK : (c + 1) * CHUNK], in_=bank[:, i * CHUNK : (i + 1) * CHUNK])
 
         nc.vector.tensor_copy(dst_sc[:], tab_sc[:].bitcast(U8).indirect(dst_list[:]))
-        nc.scalar.dma_start(out=dst_sc1[0 : P - 4, :], in_=dst_sc[4:P, :].bitcast(I32))
-        nc.vector.tensor_copy(src_sc[:], tab_sc[:].bitcast(U8).indirect(src_list[:]))
-        for t in range(2):
-            nc.vector.memset(placed[t][:], 0.0)
-        gather_chunk(0)
-        gather_chunk(1)
+        nc.scalar.dma_start(out=dst_sc1[0:112, :], in_=dst_sc[4:116, :].bitcast(I32))
+        for c in range(2):
+            for step in range(4):
+                if step == 2:
+                    gather_scales(c)
+                gather_words(c, step)
+                if (c, step) == (0, 0):
+                    for t in range(2):
+                        nc.vector.memset(placed[t][:], 0.0)
+        for c in range(2, CHUNKS):
+            gather_scales(c)
 
         for step in range(4):
             for blk in range(BLOCKS):
@@ -194,7 +210,6 @@ def tile_list_msg_none_none_kernel(
                     first_pass(0, blk, b, step)
         for blk in range(BLOCKS):
             round_rows(0, blk)
-        gather_chunk(2)
 
         last = CHUNKS - 1
         for c in range(CHUNKS):
@@ -202,24 +217,27 @@ def tile_list_msg_none_none_kernel(
             if c == 0:
                 for t in range(2, 4):
                     nc.vector.memset(placed[t][:], 0.0)
+                for later in range(2, CHUNKS):
+                    for step in range(4):
+                        gather_words(later, step)
             else:
-                second_product(c - 1, (2, 3) if c < last else (2,), side[1])
+                second_product(c - 1, (2, 3), side[1])
             if c < last:
                 first_product(c + 1, 0)
             second_product(c, (0, 1), side[2])
             if c < last:
                 first_product(c + 1, 1)
-            if c == 0:
-                gather_chunk(3)
-        second_product(last - 1, (3,), side[2])
         second_product(last, (2, 3), side[3])
 
-        order = [(c, t) for c in range(last) for t in range(N_TILES)]
-        order = order[:-1] + [(last, 0), (last, 1), order[-1], (last, 2), (last, 3)]
-        for c, t in order:
-            cols = slice(c * CHUNK, (c + 1) * CHUNK)
+        order = [(c, t, 1) for c in range(CHUNKS) for t in range(N_TILES) if c < last - 1 or t < N_TILES - 1]
+        order.append((last - 1, N_TILES - 1, 2))
+        for c, t, chunks in order:
+            cols = slice(c * CHUNK, (c + chunks) * CHUNK)
             nc.vector.tensor_tensor(
-                placed[t][:].indirect(listed(dst_list, c)), y_sb[t][:, cols], weight[:, cols], mybir.AluOpType.mult
+                placed[t][:].indirect(listed(dst_list, c, chunks)),
+                y_sb[t][:, cols],
+                weight[:, cols],
+                mybir.AluOpType.mult,
             )
-            if c == last:
+            if c + chunks == CHUNKS:
                 nc.sync.dma_start(out=out[t * P : (t + 1) * P, :], in_=placed[t][:])

@@ -45,13 +45,15 @@ def tile_list_msg_none_none_kernel(
         wd_sc = keep.tile([P, 2, N // 4], I32, align_bytes=ALIGN)
         weight = keep.tile([P, J], F32)
         early = keep.tile([P, 2, 4, CHUNK], U32, align_bytes=ALIGN)
-        src_sc = keep.tile([P, J], U8, align_bytes=ALIGN)
+        early_sc = keep.tile([P, 2 * CHUNK], U8, align_bytes=ALIGN)
         h_rows = keep.tile([P, BLOCKS, 2, BANK], BF16)
         grouped = keep.tile([P, 2, 2, CHUNK, 2], F32, align_bytes=ALIGN)
         h_codes = keep.tile([P, CHUNKS, 2, CHUNK], U32, align_bytes=ALIGN)
         h_sc = keep.tile([P, CHUNKS, 2, CHUNK], U8, align_bytes=ALIGN)
-        first_grouped = shared.tile([P, 2, CHUNK, 2], F32, offset=8 * T, align_bytes=ALIGN)
-        late = shared.tile([P, 2, 4, CHUNK], U32, offset=8 * T, align_bytes=ALIGN)
+        first_grouped = shared.tile([P, 2, CHUNK, 2], F32, offset=9 * T - 8 * CHUNK, align_bytes=ALIGN)
+        fourth = shared.tile([P, 4, CHUNK], U32, offset=9 * T, align_bytes=ALIGN)
+        gate2 = shared.tile([P, CHUNK], U32, offset=11 * T, align_bytes=ALIGN)
+        third = shared.tile([P, 4, CHUNK], U32, offset=11 * T, align_bytes=ALIGN)
         acc_h = [[psum.tile([P, BANK], F32, name="acc_h%d%d" % (blk, b)) for b in range(2)] for blk in range(BLOCKS)]
         side = [psum.tile([P, BANK], F32, name="side%d" % i) for i in range(4)]
         dst_sc = keep.tile([P, J], U8, align_bytes=ALIGN)
@@ -59,8 +61,10 @@ def tile_list_msg_none_none_kernel(
         ident = keep.tile([P, P], F32)
         y_sb = [keep.tile([P, J], F32, name="y%d" % t) for t in range(N_TILES)]
         placed = [keep.tile([P, T], F32, name="placed%d" % t) for t in range(2)]
-        first_rows = shared.tile([P, 2, BANK], BF16, offset=4 * T - 2 * BANK)
-        placed += [shared.tile([P, T], F32, name="placed%d" % t, offset=4 * T * (t - 2)) for t in range(2, 4)]
+        gate = shared.tile([P, CHUNK], U32, offset=4 * T - CHUNK, align_bytes=ALIGN)
+        late_sc = shared.tile([P, 2 * CHUNK], U8, offset=4 * T, align_bytes=ALIGN)
+        placed.append(shared.tile([P, T], F32, name="placed2", offset=0))
+        placed.append(shared.tile([P, T], F32, name="placed3", offset=5 * T))
 
         nc.vector.memset(tab_sc[:], 0)
         nc.vector.memset(wt_sc[:], 0)
@@ -84,12 +88,12 @@ def tile_list_msg_none_none_kernel(
         nc.sync.dma_start(dst_list[:], offs2)
         for q in range(4):
             load_packed(tab_sc, tab_scales, q)
-        nc.sync.dma_start(out=wt[:], in_=wt_words.bitcast(I32).rearrange("a p c -> p a c"))
+        nc.sync.dma_start(src_list[:], offs)
         nc.sync.dma_start(out=tab[0][:], in_=words8(tab_words, 0))
+        nc.sync.dma_start(out=wt[:], in_=wt_words.bitcast(I32).rearrange("a p c -> p a c"))
         for q in range(4):
             load_side_by_side(wt_sc, wt_scales, q)
         nc.sync.dma_start(out=tab[1][:], in_=words8(tab_words, 1))
-        nc.sync.dma_start(src_list[:], offs)
         nc.sync.dma_start(out=ws[:, 0, :], in_=words8(ws_words, 0))
         for q in range(4):
             load_packed(ws_sc, ws_scales, q)
@@ -103,12 +107,14 @@ def tile_list_msg_none_none_kernel(
             return offsets[:, c * CHUNK // 16 : (c + chunks) * CHUNK // 16]
 
         def picked(c, step):
-            return (early if c < 2 else late)[:, c % 2, step, :]
+            if (c, step) == (0, 1):
+                return gate[:]
+            if (c, step) == (0, 2):
+                return gate2[:]
+            return early[:, c, step, :] if c < 2 else (third, fourth)[c - 2][:, step, :]
 
-        def gather_scales(c):
-            nc.vector.tensor_copy(
-                src_sc[:, c * CHUNK : (c + 1) * CHUNK], tab_sc[:].bitcast(U8).indirect(listed(src_list, c))
-            )
+        def src_scales(c):
+            return (early_sc if c < 2 else late_sc)[:, (c % 2) * CHUNK : (c % 2 + 1) * CHUNK]
 
         def gather_words(c, step):
             offsets = dst_list if step < 2 else src_list
@@ -128,7 +134,7 @@ def tile_list_msg_none_none_kernel(
                 rhs_scale = wt_sc[:, a, :].bitcast(U8)[:, BANK * b : BANK * (b + 1)]
             else:
                 lhsT = picked(c, step)[:, cols].bitcast(FP8X4)
-                lhsT_scale = src_sc[4 * a : P, edges]
+                lhsT_scale = src_scales(c)[4 * a : P, cols]
                 rhs = ws[:, a, BANK * b : BANK * (b + 1)].bitcast(FP8X4)
                 rhs_scale = ws_sc[4 * a : P, :].bitcast(U8)[:, BANK * b : BANK * (b + 1)]
             nc.tensor.matmul_mx(
@@ -141,26 +147,24 @@ def tile_list_msg_none_none_kernel(
                 stop=(step == 3),
             )
 
-        def rows_of(c, blk):
-            return first_rows[:] if (c, blk) == (0, 0) else h_rows[:, blk, :, :]
-
-        def round_rows(c, blk):
+        def round_rows(blk):
             for b in range(2):
                 nc.scalar.copy(
-                    out=rows_of(c, blk)[:, b, :].rearrange("j (u p e) -> j u p e", u=2, e=2),
+                    out=h_rows[:, blk, b, :].rearrange("j (u p e) -> j u p e", u=2, e=2),
                     in_=acc_h[blk][b][:].rearrange("j (p u e) -> j u p e", u=2, e=2),
                 )
 
-        def first_product(c, blk):
-            for step in range(4):
+        def first_product(c, blk, steps):
+            for step in steps:
                 for b in range(2):
                     first_pass(c, blk, b, step)
-            round_rows(c, blk)
+            if steps[-1] == 3:
+                round_rows(blk)
 
         def turn_and_quantise(c):
             for blk in range(BLOCKS):
                 turned = side[blk][:].rearrange("p (b u j) -> p b u j", b=2, u=2)
-                words = rows_of(c, blk).rearrange("j b r -> j (b r)").bitcast(F32)
+                words = h_rows[:, blk, :, :].rearrange("j b r -> j (b r)").bitcast(F32)
                 for b in (1, 0):
                     for u in range(2):
                         w0 = (2 * b + u) * P
@@ -193,40 +197,40 @@ def tile_list_msg_none_none_kernel(
 
         nc.vector.tensor_copy(dst_sc[:], tab_sc[:].bitcast(U8).indirect(dst_list[:]))
         nc.scalar.dma_start(out=dst_sc1[0:112, :], in_=dst_sc[4:116, :].bitcast(I32))
+        for t in range(2):
+            nc.vector.memset(placed[t][:].bitcast(I32), 0)
         for c in range(2):
             for step in range(4):
                 if step == 2:
-                    gather_scales(c)
+                    nc.vector.tensor_copy(src_scales(c), tab_sc[:].bitcast(U8).indirect(listed(src_list, c)))
                 gather_words(c, step)
-                if (c, step) == (0, 0):
-                    for t in range(2):
-                        nc.vector.memset(placed[t][:], 0.0)
-        for c in range(2, CHUNKS):
-            gather_scales(c)
 
         for step in range(4):
             for blk in range(BLOCKS):
                 for b in range(2):
                     first_pass(0, blk, b, step)
         for blk in range(BLOCKS):
-            round_rows(0, blk)
+            round_rows(blk)
+        nc.vector.tensor_copy(late_sc[:], tab_sc[:].bitcast(U8).indirect(listed(src_list, 2, 2)))
+        nc.vector.memset(placed[2][:].bitcast(I32), 0)
+        for step in range(4):
+            gather_words(2, step)
 
         last = CHUNKS - 1
         for c in range(CHUNKS):
             turn_and_quantise(c)
             if c == 0:
-                for t in range(2, 4):
-                    nc.vector.memset(placed[t][:], 0.0)
-                for later in range(2, CHUNKS):
-                    for step in range(4):
-                        gather_words(later, step)
+                for step in range(4):
+                    gather_words(last, step)
+                nc.vector.memset(placed[3][:].bitcast(I32), 0)
             else:
                 second_product(c - 1, (2, 3), side[1])
             if c < last:
-                first_product(c + 1, 0)
+                first_product(c + 1, 0, (0, 1, 2, 3))
+                first_product(c + 1, 1, (0, 1))
             second_product(c, (0, 1), side[2])
             if c < last:
-                first_product(c + 1, 1)
+                first_product(c + 1, 1, (2, 3))
         second_product(last, (2, 3), side[3])
 
         order = [(c, t, 1) for c in range(CHUNKS) for t in range(N_TILES) if c < last - 1 or t < N_TILES - 1]

@@ -37,34 +37,34 @@ def tile_list_msg_none_none_kernel(
         dst_list = keep.tile([P, J // 16], U16)
         tab = [keep.tile([P, T], I32, name="tab%d" % a, align_bytes=ALIGN) for a in range(2)]
         tab_sc = keep.tile([P, T // 4], I32, align_bytes=ALIGN)
-        ws = keep.tile([P, 2, R], I32, align_bytes=ALIGN)
-        ws_sc = keep.tile([P, R // 4], I32, align_bytes=ALIGN)
+        ws = [keep.tile([P, 2, BANK], I32, name="ws%d" % b, align_bytes=ALIGN) for b in range(2)]
         wt = keep.tile([P, 2, R // 2], I32, align_bytes=ALIGN)
         wt_sc = keep.tile([P, 2, R // 4], I32, align_bytes=ALIGN)
+        ws_sc = keep.tile([P, 2, R // 4], I32, align_bytes=ALIGN)
         wd = keep.tile([P, 2, N // 2], I32, align_bytes=ALIGN)
         wd_sc = keep.tile([P, 2, N // 4], I32, align_bytes=ALIGN)
         weight = keep.tile([P, J], F32)
-        early = keep.tile([P, 2, 4, CHUNK], U32, align_bytes=ALIGN)
-        early_sc = keep.tile([P, 2 * CHUNK], U8, align_bytes=ALIGN)
-        h_rows = keep.tile([P, BLOCKS, 2, BANK], BF16)
-        grouped = keep.tile([P, 2, 2, CHUNK, 2], F32, align_bytes=ALIGN)
+        early = keep.tile([P, 4, 2 * CHUNK], U32, align_bytes=ALIGN)
+        src_sc = [keep.tile([P, 2 * CHUNK], U8, name="src_sc0", align_bytes=ALIGN)]
+        gate = shared.tile([P, CHUNK], U32, offset=4 * T - CHUNK, align_bytes=ALIGN)
+        src_sc.append(shared.tile([P, 2 * CHUNK], U8, name="src_sc1", offset=4 * T, align_bytes=ALIGN))
+        third = shared.tile([P, 4, CHUNK], U32, offset=4 * T + 2 * CHUNK, align_bytes=ALIGN)
+        h_rows = [
+            [keep.tile([P, BANK], BF16, name="h_rows%d%d" % (blk, b)) for b in range(2)] for blk in range(CHUNKS * BLOCKS)
+        ]
+        grouped = [keep.tile([P, 2, CHUNK, 2], F32, name="grouped%d" % c, align_bytes=ALIGN) for c in range(1, CHUNKS)]
         h_codes = keep.tile([P, CHUNKS, 2, CHUNK], U32, align_bytes=ALIGN)
         h_sc = keep.tile([P, CHUNKS, 2, CHUNK], U8, align_bytes=ALIGN)
-        first_grouped = shared.tile([P, 2, CHUNK, 2], F32, offset=9 * T - 8 * CHUNK, align_bytes=ALIGN)
-        fourth = shared.tile([P, 4, CHUNK], U32, offset=9 * T, align_bytes=ALIGN)
-        gate2 = shared.tile([P, CHUNK], U32, offset=11 * T, align_bytes=ALIGN)
-        third = shared.tile([P, 4, CHUNK], U32, offset=11 * T, align_bytes=ALIGN)
-        acc_h = [[psum.tile([P, BANK], F32, name="acc_h%d%d" % (blk, b)) for b in range(2)] for blk in range(BLOCKS)]
-        side = [psum.tile([P, BANK], F32, name="side%d" % i) for i in range(4)]
+        grouped.insert(0, shared.tile([P, 2, CHUNK, 2], F32, name="grouped0", offset=10 * T, align_bytes=ALIGN))
+        late = shared.tile([P, 4, CHUNK], U32, offset=11 * T, align_bytes=ALIGN)
+        banks = [psum.tile([P, BANK], F32, name="bank%d" % i) for i in range(8)]
         dst_sc = keep.tile([P, J], U8, align_bytes=ALIGN)
         dst_sc1 = keep.tile([P, J // 4], I32, align_bytes=ALIGN)
         ident = keep.tile([P, P], F32)
         y_sb = [keep.tile([P, J], F32, name="y%d" % t) for t in range(N_TILES)]
         placed = [keep.tile([P, T], F32, name="placed%d" % t) for t in range(2)]
-        gate = shared.tile([P, CHUNK], U32, offset=4 * T - CHUNK, align_bytes=ALIGN)
-        late_sc = shared.tile([P, 2 * CHUNK], U8, offset=4 * T, align_bytes=ALIGN)
         placed.append(shared.tile([P, T], F32, name="placed2", offset=0))
-        placed.append(shared.tile([P, T], F32, name="placed3", offset=5 * T))
+        placed.append(shared.tile([P, T], F32, name="placed3", offset=7 * T))
 
         nc.vector.memset(tab_sc[:], 0)
         nc.vector.memset(wt_sc[:], 0)
@@ -85,97 +85,93 @@ def tile_list_msg_none_none_kernel(
         def words8(w, a):
             return w[a].rearrange("p c i -> p (c i)").bitcast(I32)
 
+        ws_columns = ws_words.rearrange("a p c i -> p a (c i)").bitcast(I32)
+        nc.sync.dma_start(out=tab[0][:], in_=words8(tab_words, 0))
         nc.sync.dma_start(dst_list[:], offs2)
         for q in range(4):
             load_packed(tab_sc, tab_scales, q)
         nc.sync.dma_start(src_list[:], offs)
-        nc.sync.dma_start(out=tab[0][:], in_=words8(tab_words, 0))
         nc.sync.dma_start(out=wt[:], in_=wt_words.bitcast(I32).rearrange("a p c -> p a c"))
         for q in range(4):
             load_side_by_side(wt_sc, wt_scales, q)
         nc.sync.dma_start(out=tab[1][:], in_=words8(tab_words, 1))
-        nc.sync.dma_start(out=ws[:, 0, :], in_=words8(ws_words, 0))
+        nc.sync.dma_start(out=ws[0][:], in_=ws_columns[:, :, 0:BANK])
         for q in range(4):
-            load_packed(ws_sc, ws_scales, q)
-        nc.sync.dma_start(out=ws[:, 1, :], in_=words8(ws_words, 1))
+            load_side_by_side(ws_sc, ws_scales, q)
+        nc.sync.dma_start(out=ws[1][:], in_=ws_columns[:, :, BANK:R])
         nc.sync.dma_start(out=wd[:], in_=wd_words.bitcast(I32).rearrange("a p c -> p a c"))
         for q in range(4):
             load_side_by_side(wd_sc, wd_scales, q)
         nc.sync.dma_start(out=weight[:], in_=wgo)
 
+        last = CHUNKS - 1
+
         def listed(offsets, c, chunks=1):
             return offsets[:, c * CHUNK // 16 : (c + chunks) * CHUNK // 16]
 
-        def picked(c, step):
+        def picked(c, step, chunks=1):
             if (c, step) == (0, 1):
                 return gate[:]
-            if (c, step) == (0, 2):
-                return gate2[:]
-            return early[:, c, step, :] if c < 2 else (third, fourth)[c - 2][:, step, :]
+            if c >= 2:
+                return (third, late)[c - 2][:, step, :]
+            return early[:, step, c * CHUNK : (c + chunks) * CHUNK]
 
-        def src_scales(c):
-            return (early_sc if c < 2 else late_sc)[:, (c % 2) * CHUNK : (c % 2 + 1) * CHUNK]
-
-        def gather_words(c, step):
+        def gather_words(c, step, chunks=1):
             offsets = dst_list if step < 2 else src_list
-            nc.vector.tensor_copy(picked(c, step), tab[step % 2][:].bitcast(U32).indirect(listed(offsets, c)))
-
-        def grouped_of(c):
-            return first_grouped[:] if c == 0 else grouped[:, c % 2, :, :, :]
-
-        def first_pass(c, blk, b, step):
-            a = step % 2
-            cols = slice(blk * P, (blk + 1) * P)
-            edges = slice(c * CHUNK + blk * P, c * CHUNK + (blk + 1) * P)
-            if step < 2:
-                lhsT = picked(c, step)[:, cols].bitcast(FP8X4)
-                lhsT_scale = dst_sc[:, edges] if a == 0 else dst_sc1[:].bitcast(U8)[:, edges]
-                rhs = wt[:, a, :].bitcast(U8)[:, 2 * BANK * b : 2 * BANK * (b + 1)].bitcast(FP4X4)
-                rhs_scale = wt_sc[:, a, :].bitcast(U8)[:, BANK * b : BANK * (b + 1)]
-            else:
-                lhsT = picked(c, step)[:, cols].bitcast(FP8X4)
-                lhsT_scale = src_scales(c)[4 * a : P, cols]
-                rhs = ws[:, a, BANK * b : BANK * (b + 1)].bitcast(FP8X4)
-                rhs_scale = ws_sc[4 * a : P, :].bitcast(U8)[:, BANK * b : BANK * (b + 1)]
-            nc.tensor.matmul_mx(
-                out=acc_h[blk][b][:],
-                lhsT=lhsT,
-                lhsT_scale=lhsT_scale,
-                rhs=rhs,
-                rhs_scale=rhs_scale,
-                start=(step == 0),
-                stop=(step == 3),
+            nc.vector.tensor_copy(
+                picked(c, step, chunks), tab[step % 2][:].bitcast(U32).indirect(listed(offsets, c, chunks))
             )
 
-        def round_rows(blk):
-            for b in range(2):
+        def gather_src_scales(c):
+            nc.vector.tensor_copy(
+                src_sc[c // 2][:], tab_sc[:].bitcast(U8).indirect(listed(src_list, c, 2))
+            )
+
+        def first_product(blk, b, steps=(0, 1, 2, 3)):
+            c = blk // BLOCKS
+            cols = slice((blk % BLOCKS) * P, (blk % BLOCKS + 1) * P)
+            edges = slice(blk * P, (blk + 1) * P)
+            acc = banks[2 * (blk % 2) + b]
+            for step in steps:
+                a = step % 2
+                if step < 2:
+                    lhsT_scale = dst_sc[:, edges] if a == 0 else dst_sc1[:].bitcast(U8)[:, edges]
+                    rhs = wt[:, a, :].bitcast(U8)[:, 2 * BANK * b : 2 * BANK * (b + 1)].bitcast(FP4X4)
+                    rhs_scale = wt_sc[:, a, :].bitcast(U8)[:, BANK * b : BANK * (b + 1)]
+                else:
+                    lhsT_scale = src_sc[blk // 4][4 * a : P, (blk % 4) * P : (blk % 4 + 1) * P]
+                    rhs = ws[b][:, a, :].bitcast(FP8X4)
+                    rhs_scale = ws_sc[:, a, :].bitcast(U8)[:, BANK * b : BANK * (b + 1)]
+                nc.tensor.matmul_mx(
+                    out=acc[:],
+                    lhsT=picked(c, step)[:, cols].bitcast(FP8X4),
+                    lhsT_scale=lhsT_scale,
+                    rhs=rhs,
+                    rhs_scale=rhs_scale,
+                    start=(step == 0),
+                    stop=(step == 3),
+                )
+            if steps[-1] == 3:
                 nc.scalar.copy(
-                    out=h_rows[:, blk, b, :].rearrange("j (u p e) -> j u p e", u=2, e=2),
-                    in_=acc_h[blk][b][:].rearrange("j (p u e) -> j u p e", u=2, e=2),
+                    out=h_rows[blk][b][:].rearrange("j (u p e) -> j u p e", u=2, e=2),
+                    in_=acc[:].rearrange("j (p u e) -> j u p e", u=2, e=2),
                 )
 
-        def first_product(c, blk, steps):
-            for step in steps:
-                for b in range(2):
-                    first_pass(c, blk, b, step)
-            if steps[-1] == 3:
-                round_rows(blk)
-
         def turn_and_quantise(c):
-            for blk in range(BLOCKS):
-                turned = side[blk][:].rearrange("p (b u j) -> p b u j", b=2, u=2)
-                words = h_rows[:, blk, :, :].rearrange("j b r -> j (b r)").bitcast(F32)
-                for b in (1, 0):
+            for b in range(2):
+                turned = banks[4 + b][:].rearrange("p (i u j) -> p i u j", i=2, u=2)
+                for i in range(BLOCKS):
+                    words = h_rows[c * BLOCKS + i][b][:].bitcast(F32)
                     for u in range(2):
-                        w0 = (2 * b + u) * P
-                        nc.tensor.transpose(turned[:, b, u, :], words[:, w0 : w0 + P], ident[:])
+                        nc.tensor.transpose(turned[:, i, u, :], words[:, u * P : (u + 1) * P], ident[:])
                 nc.scalar.copy(
-                    out=grouped_of(c)[:, :, blk * P : (blk + 1) * P, :], in_=turned.rearrange("p b u j -> p b j u")
+                    out=grouped[c][:, b, :, :].rearrange("p (i j) u -> p i j u", i=2),
+                    in_=turned.rearrange("p i u j -> p i j u"),
                 )
             nc.vector.quantize_mx(
                 out=h_codes[:, c, :, :].rearrange("p b j -> p (b j)").bitcast(FP8X4),
                 scales=h_sc[:, c, :, :].rearrange("p b j -> p (b j)"),
-                in_=grouped_of(c).rearrange("p b j u -> p (b j u)").bitcast(BF16),
+                in_=grouped[c][:].rearrange("p b j u -> p (b j u)").bitcast(BF16),
             )
 
         def second_product(c, tiles, bank):
@@ -195,43 +191,47 @@ def tile_list_msg_none_none_kernel(
             for i, t in enumerate(tiles):
                 nc.scalar.copy(out=y_sb[t][:, c * CHUNK : (c + 1) * CHUNK], in_=bank[:, i * CHUNK : (i + 1) * CHUNK])
 
+        gather_words(0, 0, 2)
         nc.vector.tensor_copy(dst_sc[:], tab_sc[:].bitcast(U8).indirect(dst_list[:]))
         nc.scalar.dma_start(out=dst_sc1[0:112, :], in_=dst_sc[4:116, :].bitcast(I32))
+        gather_words(0, 2, 2)
+        gather_src_scales(0)
+        for c in range(2):
+            gather_words(c, 1)
+            gather_words(c, 3)
         for t in range(2):
             nc.vector.memset(placed[t][:].bitcast(I32), 0)
-        for c in range(2):
-            for step in range(4):
-                if step == 2:
-                    nc.vector.tensor_copy(src_scales(c), tab_sc[:].bitcast(U8).indirect(listed(src_list, c)))
-                gather_words(c, step)
 
-        for step in range(4):
+        for step in range(2):
             for blk in range(BLOCKS):
                 for b in range(2):
-                    first_pass(0, blk, b, step)
-        for blk in range(BLOCKS):
-            round_rows(blk)
-        nc.vector.tensor_copy(late_sc[:], tab_sc[:].bitcast(U8).indirect(listed(src_list, 2, 2)))
-        nc.vector.memset(placed[2][:].bitcast(I32), 0)
+                    first_product(blk, b, (step,))
+        gather_src_scales(2)
         for step in range(4):
             gather_words(2, step)
-
-        last = CHUNKS - 1
+        nc.vector.memset(placed[2][:].bitcast(I32), 0)
+        for b in range(2):
+            for blk in range(BLOCKS):
+                first_product(blk, b, (2, 3))
         for c in range(CHUNKS):
+            ahead = 2 * c + 2
+            if c < last:
+                first_product(ahead, 0)
             turn_and_quantise(c)
             if c == 0:
                 for step in range(4):
                     gather_words(last, step)
                 nc.vector.memset(placed[3][:].bitcast(I32), 0)
-            else:
-                second_product(c - 1, (2, 3), side[1])
             if c < last:
-                first_product(c + 1, 0, (0, 1, 2, 3))
-                first_product(c + 1, 1, (0, 1))
-            second_product(c, (0, 1), side[2])
+                first_product(ahead, 1)
+            if c > 0:
+                second_product(c - 1, (2, 3), banks[4])
             if c < last:
-                first_product(c + 1, 1, (2, 3))
-        second_product(last, (2, 3), side[3])
+                first_product(ahead + 1, 0)
+            second_product(c, (0, 1), banks[6])
+            if c < last:
+                first_product(ahead + 1, 1)
+        second_product(last, (2, 3), banks[7])
 
         order = [(c, t, 1) for c in range(CHUNKS) for t in range(N_TILES) if c < last - 1 or t < N_TILES - 1]
         order.append((last - 1, N_TILES - 1, 2))

@@ -98,11 +98,6 @@ def tile_list_msg_none_none_kernel(
         nc.sync.dma_start(out=ws[0][:], in_=ws_columns[:, :, 0:BANK])
         for q in range(4):
             load_side_by_side(ws_sc, ws_scales, q)
-        nc.sync.dma_start(out=ws[1][:], in_=ws_columns[:, :, BANK:R])
-        nc.sync.dma_start(out=wd[:], in_=wd_words.bitcast(I32).rearrange("a p c -> p a c"))
-        for q in range(4):
-            load_side_by_side(wd_sc, wd_scales, q)
-        nc.sync.dma_start(out=weight[:], in_=wgo)
 
         last = CHUNKS - 1
 
@@ -127,7 +122,7 @@ def tile_list_msg_none_none_kernel(
                 src_sc[c // 2][:], tab_sc[:].bitcast(U8).indirect(listed(src_list, c, 2))
             )
 
-        def first_product(blk, b, steps=(0, 1, 2, 3)):
+        def first_product(blk, b, steps, closes=False):
             c = blk // BLOCKS
             cols = slice((blk % BLOCKS) * P, (blk % BLOCKS + 1) * P)
             edges = slice(blk * P, (blk + 1) * P)
@@ -149,13 +144,16 @@ def tile_list_msg_none_none_kernel(
                     rhs=rhs,
                     rhs_scale=rhs_scale,
                     start=(step == 0),
-                    stop=(step == 3),
+                    stop=(closes and step == steps[-1]),
                 )
-            if steps[-1] == 3:
+            if closes:
                 nc.scalar.copy(
                     out=h_rows[blk][b][:].rearrange("j (u p e) -> j u p e", u=2, e=2),
                     in_=acc[:].rearrange("j (p u e) -> j u p e", u=2, e=2),
                 )
+
+        def whole_half(blk, b):
+            first_product(blk, b, (0, 1, 2, 3), closes=True)
 
         def turn_and_quantise(c):
             for b in range(2):
@@ -193,44 +191,52 @@ def tile_list_msg_none_none_kernel(
 
         gather_words(0, 0, 2)
         nc.vector.tensor_copy(dst_sc[:], tab_sc[:].bitcast(U8).indirect(dst_list[:]))
-        nc.scalar.dma_start(out=dst_sc1[0:112, :], in_=dst_sc[4:116, :].bitcast(I32))
+        nc.sync.dma_start(out=dst_sc1[0:112, :], in_=dst_sc[4:116, :].bitcast(I32))
+        nc.sync.dma_start(out=ws[1][:], in_=ws_columns[:, :, BANK:R])
+        nc.sync.dma_start(out=wd[:], in_=wd_words.bitcast(I32).rearrange("a p c -> p a c"))
+        for q in range(4):
+            load_side_by_side(wd_sc, wd_scales, q)
+        nc.sync.dma_start(out=weight[:], in_=wgo)
         gather_words(0, 2, 2)
         gather_src_scales(0)
         for c in range(2):
-            gather_words(c, 1)
             gather_words(c, 3)
+            gather_words(c, 1)
         for t in range(2):
             nc.vector.memset(placed[t][:].bitcast(I32), 0)
 
-        for step in range(2):
+        for blk in range(BLOCKS):
+            for b in range(2):
+                first_product(blk, b, (0,))
+        for blk in range(BLOCKS):
+            first_product(blk, 0, (2, 3))
+        for b in range(2):
             for blk in range(BLOCKS):
-                for b in range(2):
-                    first_product(blk, b, (step,))
+                first_product(blk, b, (1,), closes=(b == 0))
         gather_src_scales(2)
         for step in range(4):
             gather_words(2, step)
         nc.vector.memset(placed[2][:].bitcast(I32), 0)
-        for b in range(2):
-            for blk in range(BLOCKS):
-                first_product(blk, b, (2, 3))
+        for blk in range(BLOCKS):
+            first_product(blk, 1, (2, 3), closes=True)
         for c in range(CHUNKS):
             ahead = 2 * c + 2
             if c < last:
-                first_product(ahead, 0)
+                whole_half(ahead, 0)
             turn_and_quantise(c)
             if c == 0:
                 for step in range(4):
                     gather_words(last, step)
                 nc.vector.memset(placed[3][:].bitcast(I32), 0)
             if c < last:
-                first_product(ahead, 1)
+                whole_half(ahead, 1)
             if c > 0:
                 second_product(c - 1, (2, 3), banks[4])
             if c < last:
-                first_product(ahead + 1, 0)
+                whole_half(ahead + 1, 0)
             second_product(c, (0, 1), banks[6])
             if c < last:
-                first_product(ahead + 1, 1)
+                whole_half(ahead + 1, 1)
         second_product(last, (2, 3), banks[7])
 
         order = [(c, t, 1) for c in range(CHUNKS) for t in range(N_TILES) if c < last - 1 or t < N_TILES - 1]

@@ -35,7 +35,10 @@ def tile_list_msg_none_none_kernel(
 
         src_list = keep.tile([P, J // 16], U16)
         dst_list = keep.tile([P, J // 16], U16)
-        tab = [keep.tile([P, T], I32, name="tab%d" % a, align_bytes=ALIGN) for a in range(2)]
+        tab = [
+            shared.tile([P, T], I32, name="tab0", offset=13 * T, align_bytes=ALIGN),
+            keep.tile([P, T], I32, name="tab1", align_bytes=ALIGN),
+        ]
         tab_sc = keep.tile([P, T // 4], I32, align_bytes=ALIGN)
         ws = [keep.tile([P, 2, BANK], I32, name="ws%d" % b, align_bytes=ALIGN) for b in range(2)]
         wt = keep.tile([P, 2, R // 2], I32, align_bytes=ALIGN)
@@ -62,15 +65,18 @@ def tile_list_msg_none_none_kernel(
         dst_sc1 = keep.tile([P, J // 4], I32, align_bytes=ALIGN)
         ident = keep.tile([P, P], F32)
         y_sb = [keep.tile([P, J], F32, name="y%d" % t) for t in range(N_TILES)]
-        placed = [keep.tile([P, T], F32, name="placed%d" % t) for t in range(2)]
-        placed.append(shared.tile([P, T], F32, name="placed2", offset=0))
-        placed.append(shared.tile([P, T], F32, name="placed3", offset=7 * T))
+        placed = [keep.tile([P, T], F32, name="placed%d" % t) for t in range(3)]
+        placed.append(shared.tile([P, T], F32, name="placed3", offset=13 * T))
 
-        nc.vector.memset(tab_sc[:], 0)
-        nc.vector.memset(wt_sc[:], 0)
-        nc.vector.memset(ws_sc[:], 0)
-        nc.vector.memset(dst_sc1[:], 0)
-        nc.vector.memset(wd_sc[:], 0)
+        nc.gpsimd.memset(tab_sc[:], 0)
+        nc.gpsimd.memset(wt_sc[:], 0)
+        nc.gpsimd.memset(ws_sc[:], 0)
+        nc.gpsimd.memset(dst_sc1[:], 0)
+        nc.gpsimd.memset(wd_sc[:], 0)
+        nc.gpsimd.memset(placed[2][:].bitcast(I32), 0)
+        for t in range(2):
+            nc.vector.memset(placed[t][:, 0 : T - 1].bitcast(I32), 0)
+            nc.vector.memset(placed[t][:, T - 1 : T].bitcast(I32), 0)
         make_identity(nc, ident[:])
 
         def load_packed(plane, scales, q):
@@ -202,8 +208,6 @@ def tile_list_msg_none_none_kernel(
         for c in range(2):
             gather_words(c, 3)
             gather_words(c, 1)
-        for t in range(2):
-            nc.vector.memset(placed[t][:].bitcast(I32), 0)
 
         for blk in range(BLOCKS):
             for b in range(2):
@@ -216,7 +220,6 @@ def tile_list_msg_none_none_kernel(
         gather_src_scales(2)
         for step in range(4):
             gather_words(2, step)
-        nc.vector.memset(placed[2][:].bitcast(I32), 0)
         for blk in range(BLOCKS):
             first_product(blk, 1, (2, 3), closes=True)
         for c in range(CHUNKS):
@@ -225,9 +228,9 @@ def tile_list_msg_none_none_kernel(
                 whole_half(ahead, 0)
             turn_and_quantise(c)
             if c == 0:
-                for step in range(4):
+                for step in (0, 2, 1, 3):
                     gather_words(last, step)
-                nc.vector.memset(placed[3][:].bitcast(I32), 0)
+                nc.gpsimd.memset(placed[3][:].bitcast(I32), 0)
             if c < last:
                 whole_half(ahead, 1)
             if c > 0:

@@ -37,7 +37,7 @@ def tile_list_msg_none_none_kernel(
         dst_list = keep.tile([P, J // 16], U16)
         tab = [
             shared.tile([P, T], I32, name="tab0", offset=13 * T, align_bytes=ALIGN),
-            keep.tile([P, T], I32, name="tab1", align_bytes=ALIGN),
+            shared.tile([P, T], I32, name="tab1", offset=17 * T, align_bytes=ALIGN),
         ]
         tab_sc = keep.tile([P, T // 4], I32, align_bytes=ALIGN)
         ws = [keep.tile([P, 2, BANK], I32, name="ws%d" % b, align_bytes=ALIGN) for b in range(2)]
@@ -61,22 +61,25 @@ def tile_list_msg_none_none_kernel(
         grouped.insert(0, shared.tile([P, 2, CHUNK, 2], F32, name="grouped0", offset=10 * T, align_bytes=ALIGN))
         late = shared.tile([P, 4, CHUNK], U32, offset=11 * T, align_bytes=ALIGN)
         banks = [psum.tile([P, BANK], F32, name="bank%d" % i) for i in range(8)]
-        dst_sc = keep.tile([P, J], U8, align_bytes=ALIGN)
+        dst_sc = [
+            keep.tile([P, 2 * CHUNK], U8, name="dst_sc0", align_bytes=ALIGN),
+            shared.tile([P, 2 * CHUNK], U8, name="dst_sc2", offset=4 * T - 2 * CHUNK, align_bytes=ALIGN),
+        ]
         dst_sc1 = keep.tile([P, J // 4], I32, align_bytes=ALIGN)
         ident = keep.tile([P, P], F32)
         y_sb = [keep.tile([P, J], F32, name="y%d" % t) for t in range(N_TILES)]
-        placed = [keep.tile([P, T], F32, name="placed%d" % t) for t in range(3)]
-        placed.append(shared.tile([P, T], F32, name="placed3", offset=13 * T))
+        placed = [keep.tile([P, T], F32, name="placed%d" % t) for t in range(2)]
+        placed.append(shared.tile([P, T], F32, name="placed2", offset=15 * T))
+        placed.append(shared.tile([P, T], F32, name="placed3", offset=19 * T))
 
         nc.gpsimd.memset(tab_sc[:], 0)
         nc.gpsimd.memset(wt_sc[:], 0)
         nc.gpsimd.memset(ws_sc[:], 0)
         nc.gpsimd.memset(dst_sc1[:], 0)
         nc.gpsimd.memset(wd_sc[:], 0)
-        nc.gpsimd.memset(placed[2][:].bitcast(I32), 0)
-        for t in range(2):
-            nc.vector.memset(placed[t][:, 0 : T - 1].bitcast(I32), 0)
-            nc.vector.memset(placed[t][:, T - 1 : T].bitcast(I32), 0)
+        nc.vector.memset(placed[0][:, 0 : T - 1].bitcast(I32), 0)
+        nc.vector.memset(placed[0][:, T - 1 : T].bitcast(I32), 0)
+        nc.vector.memset(placed[1][:].bitcast(I32), 0)
         make_identity(nc, ident[:])
 
         def load_packed(plane, scales, q):
@@ -128,6 +131,12 @@ def tile_list_msg_none_none_kernel(
                 src_sc[c // 2][:], tab_sc[:].bitcast(U8).indirect(listed(src_list, c, 2))
             )
 
+        def gather_dst_scales(c):
+            nc.vector.tensor_copy(dst_sc[c // 2][:], tab_sc[:].bitcast(U8).indirect(listed(dst_list, c, 2)))
+            nc.sync.dma_start(
+                out=dst_sc1[0:112, c * CHUNK // 4 : (c + 2) * CHUNK // 4], in_=dst_sc[c // 2][4:116, :].bitcast(I32)
+            )
+
         def first_product(blk, b, steps, closes=False):
             c = blk // BLOCKS
             cols = slice((blk % BLOCKS) * P, (blk % BLOCKS + 1) * P)
@@ -136,7 +145,7 @@ def tile_list_msg_none_none_kernel(
             for step in steps:
                 a = step % 2
                 if step < 2:
-                    lhsT_scale = dst_sc[:, edges] if a == 0 else dst_sc1[:].bitcast(U8)[:, edges]
+                    lhsT_scale = dst_sc[blk // 4][:, (blk % 4) * P : (blk % 4 + 1) * P] if a == 0 else dst_sc1[:].bitcast(U8)[:, edges]
                     rhs = wt[:, a, :].bitcast(U8)[:, 2 * BANK * b : 2 * BANK * (b + 1)].bitcast(FP4X4)
                     rhs_scale = wt_sc[:, a, :].bitcast(U8)[:, BANK * b : BANK * (b + 1)]
                 else:
@@ -195,33 +204,32 @@ def tile_list_msg_none_none_kernel(
             for i, t in enumerate(tiles):
                 nc.scalar.copy(out=y_sb[t][:, c * CHUNK : (c + 1) * CHUNK], in_=bank[:, i * CHUNK : (i + 1) * CHUNK])
 
-        gather_words(0, 0, 2)
-        nc.vector.tensor_copy(dst_sc[:], tab_sc[:].bitcast(U8).indirect(dst_list[:]))
-        nc.sync.dma_start(out=dst_sc1[0:112, :], in_=dst_sc[4:116, :].bitcast(I32))
+        gather_words(0, 0)
+        gather_dst_scales(0)
         nc.sync.dma_start(out=ws[1][:], in_=ws_columns[:, :, BANK:R])
         nc.sync.dma_start(out=wd[:], in_=wd_words.bitcast(I32).rearrange("a p c -> p a c"))
         for q in range(4):
             load_side_by_side(wd_sc, wd_scales, q)
         nc.sync.dma_start(out=weight[:], in_=wgo)
-        gather_words(0, 2, 2)
+        gather_words(0, 2)
         gather_src_scales(0)
+        gather_words(1, 0)
+        gather_words(1, 2)
         for c in range(2):
-            gather_words(c, 3)
             gather_words(c, 1)
+            gather_words(c, 3)
 
-        for blk in range(BLOCKS):
-            for b in range(2):
-                first_product(blk, b, (0,))
-        for blk in range(BLOCKS):
-            first_product(blk, 0, (2, 3))
-        for b in range(2):
+        for step in range(2):
             for blk in range(BLOCKS):
-                first_product(blk, b, (1,), closes=(b == 0))
+                for b in range(2):
+                    first_product(blk, b, (step,))
+        gather_dst_scales(2)
         gather_src_scales(2)
         for step in range(4):
             gather_words(2, step)
-        for blk in range(BLOCKS):
-            first_product(blk, 1, (2, 3), closes=True)
+        for b in range(2):
+            for blk in range(BLOCKS):
+                first_product(blk, b, (2, 3), closes=True)
         for c in range(CHUNKS):
             ahead = 2 * c + 2
             if c < last:
@@ -230,7 +238,9 @@ def tile_list_msg_none_none_kernel(
             if c == 0:
                 for step in (0, 2, 1, 3):
                     gather_words(last, step)
-                nc.gpsimd.memset(placed[3][:].bitcast(I32), 0)
+                nc.gpsimd.memset(placed[2][:].bitcast(I32), 0)
+                for half in range(2):
+                    nc.gpsimd.memset(placed[3][:, half * T // 2 : (half + 1) * T // 2].bitcast(I32), 0)
             if c < last:
                 whole_half(ahead, 1)
             if c > 0:

@@ -22,6 +22,7 @@ CHUNKS = J // CHUNK
 BLOCKS = CHUNK // P
 N_TILES = N // P
 ALIGN = 64
+SPLIT = 1536
 
 
 def tile_list_msg_none_none_kernel(
@@ -35,10 +36,7 @@ def tile_list_msg_none_none_kernel(
 
         src_list = keep.tile([P, J // 16], U16)
         dst_list = keep.tile([P, J // 16], U16)
-        tab = [
-            shared.tile([P, T], I32, name="tab0", offset=13 * T, align_bytes=ALIGN),
-            shared.tile([P, T], I32, name="tab1", offset=17 * T, align_bytes=ALIGN),
-        ]
+        tab = [keep.tile([P, T], I32, name="tab%d" % a, align_bytes=ALIGN) for a in range(2)]
         tab_sc = keep.tile([P, T // 4], I32, align_bytes=ALIGN)
         ws = [keep.tile([P, 2, BANK], I32, name="ws%d" % b, align_bytes=ALIGN) for b in range(2)]
         wt = keep.tile([P, 2, R // 2], I32, align_bytes=ALIGN)
@@ -68,18 +66,18 @@ def tile_list_msg_none_none_kernel(
         dst_sc1 = keep.tile([P, J // 4], I32, align_bytes=ALIGN)
         ident = keep.tile([P, P], F32)
         y_sb = [keep.tile([P, J], F32, name="y%d" % t) for t in range(N_TILES)]
-        placed = [keep.tile([P, T], F32, name="placed%d" % t) for t in range(2)]
-        placed.append(shared.tile([P, T], F32, name="placed2", offset=15 * T))
-        placed.append(shared.tile([P, T], F32, name="placed3", offset=19 * T))
+        placed = [keep.tile([P, T], F32, name="placed%d" % t) for t in range(N_TILES)]
 
         nc.gpsimd.memset(tab_sc[:], 0)
         nc.gpsimd.memset(wt_sc[:], 0)
         nc.gpsimd.memset(ws_sc[:], 0)
         nc.gpsimd.memset(dst_sc1[:], 0)
         nc.gpsimd.memset(wd_sc[:], 0)
-        nc.vector.memset(placed[0][:, 0 : T - 1].bitcast(I32), 0)
-        nc.vector.memset(placed[0][:, T - 1 : T].bitcast(I32), 0)
-        nc.vector.memset(placed[1][:].bitcast(I32), 0)
+        nc.gpsimd.memset(placed[2][:].bitcast(I32), 0)
+        nc.gpsimd.memset(placed[3][:, SPLIT:T].bitcast(I32), 0)
+        for t, width in ((0, T), (1, T), (3, SPLIT)):
+            nc.vector.memset(placed[t][:, 0 : width - 1].bitcast(I32), 0)
+            nc.vector.memset(placed[t][:, width - 1 : width].bitcast(I32), 0)
         make_identity(nc, ident[:])
 
         def load_packed(plane, scales, q):
@@ -204,8 +202,8 @@ def tile_list_msg_none_none_kernel(
             for i, t in enumerate(tiles):
                 nc.scalar.copy(out=y_sb[t][:, c * CHUNK : (c + 1) * CHUNK], in_=bank[:, i * CHUNK : (i + 1) * CHUNK])
 
-        gather_words(0, 0)
         gather_dst_scales(0)
+        gather_words(0, 0)
         nc.sync.dma_start(out=ws[1][:], in_=ws_columns[:, :, BANK:R])
         nc.sync.dma_start(out=wd[:], in_=wd_words.bitcast(I32).rearrange("a p c -> p a c"))
         for q in range(4):
@@ -236,11 +234,8 @@ def tile_list_msg_none_none_kernel(
                 whole_half(ahead, 0)
             turn_and_quantise(c)
             if c == 0:
-                for step in (0, 2, 1, 3):
+                for step in range(4):
                     gather_words(last, step)
-                nc.gpsimd.memset(placed[2][:].bitcast(I32), 0)
-                for half in range(2):
-                    nc.gpsimd.memset(placed[3][:, half * T // 2 : (half + 1) * T // 2].bitcast(I32), 0)
             if c < last:
                 whole_half(ahead, 1)
             if c > 0:

@@ -185,13 +185,13 @@ def tile_list_msg_none_none_kernel(
                 in_=grouped[c][:].rearrange("p b j u -> p (b j u)").bitcast(BF16),
             )
 
-        def second_product(c, tiles, bank):
-            for i, t in enumerate(tiles):
+        def second_product(c, tiles, accs):
+            for t, acc in zip(tiles, accs):
                 for blk in range(BLOCKS):
                     cols = slice(blk * P, (blk + 1) * P)
                     for b in range(2):
                         nc.tensor.matmul_mx(
-                            out=bank[:, i * CHUNK + blk * P : i * CHUNK + (blk + 1) * P],
+                            out=acc[:, cols],
                             lhsT=wd[:, b, :].bitcast(U8)[:, 2 * P * t : 2 * P * (t + 1)].bitcast(FP4X4),
                             lhsT_scale=wd_sc[:, b, :].bitcast(U8)[:, P * t : P * (t + 1)],
                             rhs=h_codes[:, c, b, cols].bitcast(FP8X4),
@@ -199,8 +199,8 @@ def tile_list_msg_none_none_kernel(
                             start=(b == 0),
                             stop=(b == 1),
                         )
-            for i, t in enumerate(tiles):
-                nc.scalar.copy(out=y_sb[t][:, c * CHUNK : (c + 1) * CHUNK], in_=bank[:, i * CHUNK : (i + 1) * CHUNK])
+            for t, acc in zip(tiles, accs):
+                nc.scalar.copy(out=y_sb[t][:, c * CHUNK : (c + 1) * CHUNK], in_=acc)
 
         gather_dst_scales(0)
         gather_words(0, 0)
@@ -237,15 +237,17 @@ def tile_list_msg_none_none_kernel(
                 for step in range(4):
                     gather_words(last, step)
             if c < last:
-                whole_half(ahead, 1)
+                first_product(ahead, 1, (0, 1))
             if c > 0:
-                second_product(c - 1, (2, 3), banks[4])
+                second_product(c - 1, (2, 3), (banks[4][:, 0:CHUNK], banks[4][:, CHUNK:BANK]))
+            if c < last:
+                first_product(ahead, 1, (2, 3), closes=True)
             if c < last:
                 whole_half(ahead + 1, 0)
-            second_product(c, (0, 1), banks[6])
+            second_product(c, (0, 1), (banks[6][:, 0:CHUNK], banks[7][:, 0:CHUNK]))
             if c < last:
                 whole_half(ahead + 1, 1)
-        second_product(last, (2, 3), banks[7])
+        second_product(last, (2, 3), (banks[0][:, 0:CHUNK], banks[1][:, 0:CHUNK]))
 
         order = [(c, t, 1) for c in range(CHUNKS) for t in range(N_TILES) if c < last - 1 or t < N_TILES - 1]
         order.append((last - 1, N_TILES - 1, 2))

@@ -45,11 +45,11 @@ def tile_list_msg_none_none_kernel(
         wd = keep.tile([P, 2, N // 2], I32, align_bytes=ALIGN)
         wd_sc = keep.tile([P, 2, N // 4], I32, align_bytes=ALIGN)
         weight = keep.tile([P, J], F32)
-        early = keep.tile([P, 4, 2 * CHUNK], U32, align_bytes=ALIGN)
+        early = keep.tile([P, 3, CHUNK], U32, align_bytes=ALIGN)
         src_sc = [keep.tile([P, 2 * CHUNK], U8, name="src_sc0", align_bytes=ALIGN)]
         gate = shared.tile([P, CHUNK], U32, offset=4 * T - CHUNK, align_bytes=ALIGN)
         src_sc.append(shared.tile([P, 2 * CHUNK], U8, name="src_sc1", offset=4 * T, align_bytes=ALIGN))
-        third = shared.tile([P, 4, CHUNK], U32, offset=4 * T + 2 * CHUNK, align_bytes=ALIGN)
+        middle = shared.tile([P, 8, CHUNK], U32, offset=4 * T + 2 * CHUNK, align_bytes=ALIGN)
         h_rows = [
             [keep.tile([P, BANK], BF16, name="h_rows%d%d" % (blk, b)) for b in range(2)] for blk in range(CHUNKS * BLOCKS)
         ]
@@ -71,10 +71,10 @@ def tile_list_msg_none_none_kernel(
         nc.gpsimd.memset(tab_sc[:], 0)
         nc.gpsimd.memset(wt_sc[:], 0)
         nc.gpsimd.memset(ws_sc[:], 0)
-        nc.gpsimd.memset(dst_sc1[:], 0)
         nc.gpsimd.memset(wd_sc[:], 0)
         nc.gpsimd.memset(placed[2][:].bitcast(I32), 0)
         nc.gpsimd.memset(placed[3][:, SPLIT:T].bitcast(I32), 0)
+        nc.gpsimd.memset(dst_sc1[:], 0)
         for t, width in ((0, T), (1, T), (3, SPLIT)):
             nc.vector.memset(placed[t][:, 0 : width - 1].bitcast(I32), 0)
             nc.vector.memset(placed[t][:, width - 1 : width].bitcast(I32), 0)
@@ -83,28 +83,26 @@ def tile_list_msg_none_none_kernel(
         def load_packed(plane, scales, q):
             nc.sync.dma_start(out=plane[32 * q : 32 * q + 8, :], in_=scales.bitcast(I32)[:, 4 * q : 4 * q + 4, :])
 
-        def load_side_by_side(plane, scales, q):
-            nc.sync.dma_start(
+        def load_side_by_side(queue, plane, scales, q):
+            queue.dma_start(
                 out=plane[32 * q : 32 * q + 4, :, :],
                 in_=scales.bitcast(I32)[:, 4 * q : 4 * q + 4, :].rearrange("a r n -> r a n"),
             )
 
-        def words8(w, a):
-            return w[a].rearrange("p c i -> p (c i)").bitcast(I32)
-
         ws_columns = ws_words.rearrange("a p c i -> p a (c i)").bitcast(I32)
-        nc.sync.dma_start(out=tab[0][:], in_=words8(tab_words, 0))
+        tab_columns = tab_words.rearrange("a p c i -> a p (c i)").bitcast(I32)
         nc.sync.dma_start(dst_list[:], offs2)
+        for a in range(2):
+            nc.sync.dma_start(out=wt[:, a, :], in_=wt_words[a].bitcast(I32))
+        nc.sync.dma_start(out=ws[0][:, 0, :], in_=ws_columns[:, 0, 0:BANK])
         for q in range(4):
             load_packed(tab_sc, tab_scales, q)
+        nc.sync.dma_start(out=tab[0][:], in_=tab_columns[0])
         nc.sync.dma_start(src_list[:], offs)
-        nc.sync.dma_start(out=wt[:], in_=wt_words.bitcast(I32).rearrange("a p c -> p a c"))
+        nc.sync.dma_start(out=tab[1][:], in_=tab_columns[1])
         for q in range(4):
-            load_side_by_side(wt_sc, wt_scales, q)
-        nc.sync.dma_start(out=tab[1][:], in_=words8(tab_words, 1))
-        nc.sync.dma_start(out=ws[0][:], in_=ws_columns[:, :, 0:BANK])
-        for q in range(4):
-            load_side_by_side(ws_sc, ws_scales, q)
+            load_side_by_side(nc.sync, wt_sc, wt_scales, q)
+        nc.sync.dma_start(out=ws[0][:, 1, :], in_=ws_columns[:, 1, 0:BANK])
 
         last = CHUNKS - 1
 
@@ -112,11 +110,11 @@ def tile_list_msg_none_none_kernel(
             return offsets[:, c * CHUNK // 16 : (c + chunks) * CHUNK // 16]
 
         def picked(c, step, chunks=1):
-            if (c, step) == (0, 1):
-                return gate[:]
-            if c >= 2:
-                return (third, late)[c - 2][:, step, :]
-            return early[:, step, c * CHUNK : (c + chunks) * CHUNK]
+            if c == 0:
+                return gate[:] if step == 0 else early[:, step - 1, :]
+            if c == last:
+                return late[:, step, :]
+            return middle[:, 4 * (c - 1) + step, :]
 
         def gather_words(c, step, chunks=1):
             offsets = dst_list if step < 2 else src_list
@@ -203,36 +201,39 @@ def tile_list_msg_none_none_kernel(
                 nc.scalar.copy(out=y_sb[t][:, c * CHUNK : (c + 1) * CHUNK], in_=acc)
 
         gather_dst_scales(0)
-        gather_words(0, 0)
         nc.sync.dma_start(out=ws[1][:], in_=ws_columns[:, :, BANK:R])
+        for q in range(4):
+            load_side_by_side(nc.sync, ws_sc, ws_scales, q)
         nc.sync.dma_start(out=wd[:], in_=wd_words.bitcast(I32).rearrange("a p c -> p a c"))
         for q in range(4):
-            load_side_by_side(wd_sc, wd_scales, q)
+            load_side_by_side(nc.sync, wd_sc, wd_scales, q)
         nc.sync.dma_start(out=weight[:], in_=wgo)
-        gather_words(0, 2)
+        gather_words(0, 0)
         gather_src_scales(0)
-        gather_words(1, 0)
-        gather_words(1, 2)
-        for c in range(2):
-            gather_words(c, 1)
-            gather_words(c, 3)
-
-        for step in range(2):
-            for blk in range(BLOCKS):
-                for b in range(2):
-                    first_product(blk, b, (step,))
+        for step in (2, 3, 1):
+            gather_words(0, step)
+        for blk in range(BLOCKS):
+            for b in range(2):
+                first_product(blk, b, (0,))
+        for step in range(4):
+            gather_words(1, step)
         gather_dst_scales(2)
         gather_src_scales(2)
         for step in range(4):
             gather_words(2, step)
         for b in range(2):
+            for step in (2, 3):
+                for blk in range(BLOCKS):
+                    first_product(blk, b, (step,))
             for blk in range(BLOCKS):
-                first_product(blk, b, (2, 3), closes=True)
+                first_product(blk, b, (1,), closes=True)
         for c in range(CHUNKS):
             ahead = 2 * c + 2
             if c < last:
-                whole_half(ahead, 0)
+                first_product(ahead, 0, (0, 1, 2))
             turn_and_quantise(c)
+            if c < last:
+                first_product(ahead, 0, (3,), closes=True)
             if c == 0:
                 for step in range(4):
                     gather_words(last, step)

@@ -22,7 +22,7 @@ CHUNKS = J // CHUNK
 BLOCKS = CHUNK // P
 N_TILES = N // P
 ALIGN = 64
-SPLIT = 1536
+SPLIT = 1280
 
 
 def tile_list_msg_none_none_kernel(
@@ -38,18 +38,18 @@ def tile_list_msg_none_none_kernel(
         dst_list = keep.tile([P, J // 16], U16)
         tab = [keep.tile([P, T], I32, name="tab%d" % a, align_bytes=ALIGN) for a in range(2)]
         tab_sc = keep.tile([P, T // 4], I32, align_bytes=ALIGN)
-        ws = [keep.tile([P, 2, BANK], I32, name="ws%d" % b, align_bytes=ALIGN) for b in range(2)]
+        ws = [keep.tile([P, R], I32, name="ws%d" % a, align_bytes=ALIGN) for a in range(2)]
         wt = keep.tile([P, 2, R // 2], I32, align_bytes=ALIGN)
         wt_sc = keep.tile([P, 2, R // 4], I32, align_bytes=ALIGN)
         ws_sc = keep.tile([P, 2, R // 4], I32, align_bytes=ALIGN)
-        wd = keep.tile([P, 2, N // 2], I32, align_bytes=ALIGN)
         wd_sc = keep.tile([P, 2, N // 4], I32, align_bytes=ALIGN)
-        weight = keep.tile([P, J], F32)
-        early = keep.tile([P, 3, CHUNK], U32, align_bytes=ALIGN)
+        early = keep.tile([P, 7, CHUNK], U32, align_bytes=ALIGN)
         src_sc = [keep.tile([P, 2 * CHUNK], U8, name="src_sc0", align_bytes=ALIGN)]
         gate = shared.tile([P, CHUNK], U32, offset=4 * T - CHUNK, align_bytes=ALIGN)
         src_sc.append(shared.tile([P, 2 * CHUNK], U8, name="src_sc1", offset=4 * T, align_bytes=ALIGN))
-        middle = shared.tile([P, 8, CHUNK], U32, offset=4 * T + 2 * CHUNK, align_bytes=ALIGN)
+        third = shared.tile([P, 4, CHUNK], U32, offset=4 * T + 2 * CHUNK, align_bytes=ALIGN)
+        wd = keep.tile([P, 2, N // 2], I32, align_bytes=ALIGN)
+        weight = keep.tile([P, J], F32)
         h_rows = [
             [keep.tile([P, BANK], BF16, name="h_rows%d%d" % (blk, b)) for b in range(2)] for blk in range(CHUNKS * BLOCKS)
         ]
@@ -68,17 +68,19 @@ def tile_list_msg_none_none_kernel(
         y_sb = [keep.tile([P, J], F32, name="y%d" % t) for t in range(N_TILES)]
         placed = [keep.tile([P, T], F32, name="placed%d" % t) for t in range(N_TILES)]
 
-        nc.gpsimd.memset(tab_sc[:], 0)
+        nc.gpsimd.memset(tab_sc[:, T // 8 :], 0)
+        nc.vector.memset(tab_sc[:, 0 : T // 8 - 1], 0)
+        nc.vector.memset(tab_sc[:, T // 8 - 1 : T // 8], 0)
         nc.gpsimd.memset(wt_sc[:], 0)
         nc.gpsimd.memset(ws_sc[:], 0)
         nc.gpsimd.memset(wd_sc[:], 0)
+        make_identity(nc, ident[:])
         nc.gpsimd.memset(placed[2][:].bitcast(I32), 0)
         nc.gpsimd.memset(placed[3][:, SPLIT:T].bitcast(I32), 0)
         nc.gpsimd.memset(dst_sc1[:], 0)
         for t, width in ((0, T), (1, T), (3, SPLIT)):
             nc.vector.memset(placed[t][:, 0 : width - 1].bitcast(I32), 0)
             nc.vector.memset(placed[t][:, width - 1 : width].bitcast(I32), 0)
-        make_identity(nc, ident[:])
 
         def load_packed(plane, scales, q):
             nc.sync.dma_start(out=plane[32 * q : 32 * q + 8, :], in_=scales.bitcast(I32)[:, 4 * q : 4 * q + 4, :])
@@ -89,20 +91,23 @@ def tile_list_msg_none_none_kernel(
                 in_=scales.bitcast(I32)[:, 4 * q : 4 * q + 4, :].rearrange("a r n -> r a n"),
             )
 
-        ws_columns = ws_words.rearrange("a p c i -> p a (c i)").bitcast(I32)
-        tab_columns = tab_words.rearrange("a p c i -> a p (c i)").bitcast(I32)
+        def words8(w, a):
+            return w[a].rearrange("p c i -> p (c i)").bitcast(I32)
+
         nc.sync.dma_start(dst_list[:], offs2)
+        nc.sync.dma_start(out=tab[0][:], in_=words8(tab_words, 0))
         for a in range(2):
             nc.sync.dma_start(out=wt[:, a, :], in_=wt_words[a].bitcast(I32))
-        nc.sync.dma_start(out=ws[0][:, 0, :], in_=ws_columns[:, 0, 0:BANK])
         for q in range(4):
             load_packed(tab_sc, tab_scales, q)
-        nc.sync.dma_start(out=tab[0][:], in_=tab_columns[0])
-        nc.sync.dma_start(src_list[:], offs)
-        nc.sync.dma_start(out=tab[1][:], in_=tab_columns[1])
+        nc.sync.dma_start(out=ws[0][:], in_=words8(ws_words, 0))
         for q in range(4):
             load_side_by_side(nc.sync, wt_sc, wt_scales, q)
-        nc.sync.dma_start(out=ws[0][:, 1, :], in_=ws_columns[:, 1, 0:BANK])
+        nc.sync.dma_start(src_list[:], offs)
+        nc.sync.dma_start(out=tab[1][:], in_=words8(tab_words, 1))
+        for q in range(4):
+            load_side_by_side(nc.sync, ws_sc, ws_scales, q)
+        nc.sync.dma_start(out=ws[1][:], in_=words8(ws_words, 1))
 
         last = CHUNKS - 1
 
@@ -110,11 +115,11 @@ def tile_list_msg_none_none_kernel(
             return offsets[:, c * CHUNK // 16 : (c + chunks) * CHUNK // 16]
 
         def picked(c, step, chunks=1):
-            if c == 0:
-                return gate[:] if step == 0 else early[:, step - 1, :]
-            if c == last:
-                return late[:, step, :]
-            return middle[:, 4 * (c - 1) + step, :]
+            if (c, step) == (0, 2):
+                return gate[:]
+            if c >= 2:
+                return (third, late)[c - 2][:, step, :]
+            return early[:, 3 * c + step - (c == 0 and step == 3), :]
 
         def gather_words(c, step, chunks=1):
             offsets = dst_list if step < 2 else src_list
@@ -146,7 +151,7 @@ def tile_list_msg_none_none_kernel(
                     rhs_scale = wt_sc[:, a, :].bitcast(U8)[:, BANK * b : BANK * (b + 1)]
                 else:
                     lhsT_scale = src_sc[blk // 4][4 * a : P, (blk % 4) * P : (blk % 4 + 1) * P]
-                    rhs = ws[b][:, a, :].bitcast(FP8X4)
+                    rhs = ws[a][:, BANK * b : BANK * (b + 1)].bitcast(FP8X4)
                     rhs_scale = ws_sc[:, a, :].bitcast(U8)[:, BANK * b : BANK * (b + 1)]
                 nc.tensor.matmul_mx(
                     out=acc[:],
@@ -200,33 +205,31 @@ def tile_list_msg_none_none_kernel(
             for t, acc in zip(tiles, accs):
                 nc.scalar.copy(out=y_sb[t][:, c * CHUNK : (c + 1) * CHUNK], in_=acc)
 
+        gather_words(0, 0)
         gather_dst_scales(0)
-        nc.sync.dma_start(out=ws[1][:], in_=ws_columns[:, :, BANK:R])
-        for q in range(4):
-            load_side_by_side(nc.sync, ws_sc, ws_scales, q)
         nc.sync.dma_start(out=wd[:], in_=wd_words.bitcast(I32).rearrange("a p c -> p a c"))
         for q in range(4):
             load_side_by_side(nc.sync, wd_sc, wd_scales, q)
         nc.sync.dma_start(out=weight[:], in_=wgo)
-        gather_words(0, 0)
+        gather_words(0, 2)
         gather_src_scales(0)
-        for step in (2, 3, 1):
-            gather_words(0, step)
-        for blk in range(BLOCKS):
+        gather_words(1, 0)
+        gather_words(1, 2)
+        for c in range(2):
+            gather_words(c, 3)
+            gather_words(c, 1)
+
+        for step in (0, 2):
             for b in range(2):
-                first_product(blk, b, (0,))
-        for step in range(4):
-            gather_words(1, step)
+                for blk in range(BLOCKS):
+                    first_product(blk, b, (step,))
         gather_dst_scales(2)
         gather_src_scales(2)
         for step in range(4):
             gather_words(2, step)
         for b in range(2):
-            for step in (2, 3):
-                for blk in range(BLOCKS):
-                    first_product(blk, b, (step,))
             for blk in range(BLOCKS):
-                first_product(blk, b, (1,), closes=True)
+                first_product(blk, b, (3, 1), closes=True)
         for c in range(CHUNKS):
             ahead = 2 * c + 2
             if c < last:

@@ -22,7 +22,9 @@ CHUNKS = J // CHUNK
 BLOCKS = CHUNK // P
 N_TILES = N // P
 ALIGN = 64
-SPLIT = 1280
+SPLIT = 896
+PIECE = 256
+PAD = 16
 
 
 def tile_list_msg_none_none_kernel(
@@ -36,57 +38,66 @@ def tile_list_msg_none_none_kernel(
 
         src_list = keep.tile([P, J // 16], U16)
         dst_list = keep.tile([P, J // 16], U16)
-        tab = [keep.tile([P, T], I32, name="tab%d" % a, align_bytes=ALIGN) for a in range(2)]
+        tab = keep.tile([P, 2 * T], I32, align_bytes=ALIGN)
         tab_sc = keep.tile([P, T // 4], I32, align_bytes=ALIGN)
         ws = [keep.tile([P, R], I32, name="ws%d" % a, align_bytes=ALIGN) for a in range(2)]
-        wt = keep.tile([P, 2, R // 2], I32, align_bytes=ALIGN)
+        wt = [keep.tile([P, R // 2], I32, name="wt%d" % a, align_bytes=ALIGN) for a in range(2)]
         wt_sc = keep.tile([P, 2, R // 4], I32, align_bytes=ALIGN)
-        ws_sc = keep.tile([P, 2, R // 4], I32, align_bytes=ALIGN)
+        ws_sc = keep.tile([P, R // 4], I32, align_bytes=ALIGN)
         wd_sc = keep.tile([P, 2, N // 4], I32, align_bytes=ALIGN)
-        early = keep.tile([P, 7, CHUNK], U32, align_bytes=ALIGN)
-        src_sc = [keep.tile([P, 2 * CHUNK], U8, name="src_sc0", align_bytes=ALIGN)]
-        gate = shared.tile([P, CHUNK], U32, offset=4 * T - CHUNK, align_bytes=ALIGN)
-        src_sc.append(shared.tile([P, 2 * CHUNK], U8, name="src_sc1", offset=4 * T, align_bytes=ALIGN))
-        third = shared.tile([P, 4, CHUNK], U32, offset=4 * T + 2 * CHUNK, align_bytes=ALIGN)
+        src_sc = [
+            shared.tile([P, CHUNK], U8, name="src_sc0", offset=8192 + 384, align_bytes=ALIGN),
+            keep.tile([P, CHUNK], U8, name="src_sc1", align_bytes=ALIGN),
+            shared.tile([P, 2 * CHUNK], U8, name="src_sc2", offset=8192 + 512, align_bytes=ALIGN),
+        ]
+        dst_sc = [
+            keep.tile([P, J // 2], U8, name="dst_sc0", align_bytes=ALIGN),
+            shared.tile([P, J // 2], U8, name="dst_sc1", offset=8192, align_bytes=ALIGN),
+        ]
+        moved_sc = [keep.tile([P, J // 8], I32, name="moved_sc%d" % half, align_bytes=ALIGN) for half in range(2)]
         wd = keep.tile([P, 2, N // 2], I32, align_bytes=ALIGN)
         weight = keep.tile([P, J], F32)
+        reused = {(0, 0): 4096, (0, 1): 6144, (1, 1): 7168, (2, 0): 6144, (2, 1): 7168}
         h_rows = [
-            [keep.tile([P, BANK], BF16, name="h_rows%d%d" % (blk, b)) for b in range(2)] for blk in range(CHUNKS * BLOCKS)
+            [
+                shared.tile([P, BANK], BF16, name="h_rows%d%d" % (blk, b), offset=reused[blk, b])
+                if (blk, b) in reused
+                else keep.tile([P, BANK], BF16, name="h_rows%d%d" % (blk, b))
+                for b in range(2)
+            ]
+            for blk in range(CHUNKS * BLOCKS)
         ]
         grouped = [keep.tile([P, 2, CHUNK, 2], F32, name="grouped%d" % c, align_bytes=ALIGN) for c in range(1, CHUNKS)]
+        grouped.insert(0, shared.tile([P, 2, CHUNK, 2], F32, name="grouped0", offset=0, align_bytes=ALIGN))
+        late = [
+            shared.tile([P, CHUNK], U32, name="late%d" % step, offset=1024 * (step or 4), align_bytes=ALIGN)
+            for step in range(4)
+        ]
         h_codes = keep.tile([P, CHUNKS, 2, CHUNK], U32, align_bytes=ALIGN)
         h_sc = keep.tile([P, CHUNKS, 2, CHUNK], U8, align_bytes=ALIGN)
-        grouped.insert(0, shared.tile([P, 2, CHUNK, 2], F32, name="grouped0", offset=10 * T, align_bytes=ALIGN))
-        late = shared.tile([P, 4, CHUNK], U32, offset=11 * T, align_bytes=ALIGN)
         banks = [psum.tile([P, BANK], F32, name="bank%d" % i) for i in range(8)]
-        dst_sc = [
-            keep.tile([P, 2 * CHUNK], U8, name="dst_sc0", align_bytes=ALIGN),
-            shared.tile([P, 2 * CHUNK], U8, name="dst_sc2", offset=4 * T - 2 * CHUNK, align_bytes=ALIGN),
-        ]
-        dst_sc1 = keep.tile([P, J // 4], I32, align_bytes=ALIGN)
         ident = keep.tile([P, P], F32)
         y_sb = [keep.tile([P, J], F32, name="y%d" % t) for t in range(N_TILES)]
         placed = [keep.tile([P, T], F32, name="placed%d" % t) for t in range(N_TILES)]
 
-        nc.gpsimd.memset(tab_sc[:, T // 8 :], 0)
-        nc.vector.memset(tab_sc[:, 0 : T // 8 - 1], 0)
-        nc.vector.memset(tab_sc[:, T // 8 - 1 : T // 8], 0)
+        nc.gpsimd.memset(tab_sc[:], 0)
         nc.gpsimd.memset(wt_sc[:], 0)
+        nc.gpsimd.memset(moved_sc[0][:], 0)
         nc.gpsimd.memset(ws_sc[:], 0)
-        nc.gpsimd.memset(wd_sc[:], 0)
         make_identity(nc, ident[:])
-        nc.gpsimd.memset(placed[2][:].bitcast(I32), 0)
-        nc.gpsimd.memset(placed[3][:, SPLIT:T].bitcast(I32), 0)
-        nc.gpsimd.memset(dst_sc1[:], 0)
-        for t, width in ((0, T), (1, T), (3, SPLIT)):
+        nc.gpsimd.memset(wd_sc[:], 0)
+        nc.gpsimd.memset(moved_sc[1][:], 0)
+        for t, width in ((0, T), (1, SPLIT)):
             nc.vector.memset(placed[t][:, 0 : width - 1].bitcast(I32), 0)
             nc.vector.memset(placed[t][:, width - 1 : width].bitcast(I32), 0)
 
-        def load_packed(plane, scales, q):
-            nc.sync.dma_start(out=plane[32 * q : 32 * q + 8, :], in_=scales.bitcast(I32)[:, 4 * q : 4 * q + 4, :])
+        def load_packed(plane, first, scales, q):
+            nc.sync.dma_start(
+                out=plane[32 * q + first : 32 * q + first + 8, :], in_=scales.bitcast(I32)[:, 4 * q : 4 * q + 4, :]
+            )
 
-        def load_side_by_side(queue, plane, scales, q):
-            queue.dma_start(
+        def load_side_by_side(plane, scales, q):
+            nc.sync.dma_start(
                 out=plane[32 * q : 32 * q + 4, :, :],
                 in_=scales.bitcast(I32)[:, 4 * q : 4 * q + 4, :].rearrange("a r n -> r a n"),
             )
@@ -95,67 +106,62 @@ def tile_list_msg_none_none_kernel(
             return w[a].rearrange("p c i -> p (c i)").bitcast(I32)
 
         nc.sync.dma_start(dst_list[:], offs2)
-        nc.sync.dma_start(out=tab[0][:], in_=words8(tab_words, 0))
-        for a in range(2):
-            nc.sync.dma_start(out=wt[:, a, :], in_=wt_words[a].bitcast(I32))
-        for q in range(4):
-            load_packed(tab_sc, tab_scales, q)
-        nc.sync.dma_start(out=ws[0][:], in_=words8(ws_words, 0))
-        for q in range(4):
-            load_side_by_side(nc.sync, wt_sc, wt_scales, q)
         nc.sync.dma_start(src_list[:], offs)
-        nc.sync.dma_start(out=tab[1][:], in_=words8(tab_words, 1))
+        nc.sync.dma_start(out=wt[0][:], in_=wt_words[0].bitcast(I32))
+        nc.sync.dma_start(out=ws[0][:, 0:P], in_=words8(ws_words, 0)[:, 0:P])
         for q in range(4):
-            load_side_by_side(nc.sync, ws_sc, ws_scales, q)
+            load_packed(tab_sc, 0, tab_scales, q)
+        nc.sync.dma_start(out=tab[:, 0:T], in_=words8(tab_words, 0))
+        for q in range(4):
+            load_side_by_side(wt_sc, wt_scales, q)
+        nc.sync.dma_start(out=tab[:, T : 2 * T], in_=words8(tab_words, 1))
+        nc.sync.dma_start(out=ws[0][:, P:R], in_=words8(ws_words, 0)[:, P:R])
+        for q in range(4):
+            load_packed(ws_sc, 8, ws_scales, q)
         nc.sync.dma_start(out=ws[1][:], in_=words8(ws_words, 1))
+        nc.sync.dma_start(out=wt[1][:], in_=wt_words[1].bitcast(I32))
 
         last = CHUNKS - 1
+        picked = {}
 
-        def listed(offsets, c, chunks=1):
-            return offsets[:, c * CHUNK // 16 : (c + chunks) * CHUNK // 16]
+        def listed(offsets, first, count):
+            return offsets[:, first * P // 16 : (first + count) * P // 16]
 
-        def picked(c, step, chunks=1):
-            if (c, step) == (0, 2):
-                return gate[:]
-            if c >= 2:
-                return (third, late)[c - 2][:, step, :]
-            return early[:, 3 * c + step - (c == 0 and step == 3), :]
-
-        def gather_words(c, step, chunks=1):
+        def gather_words(step, first, count, spare=0):
             offsets = dst_list if step < 2 else src_list
+            a = step % 2
+            if count % 2:
+                rows = keep.tile([P, count, P + PAD], U32, name="picked%d%d" % (step, first), align_bytes=ALIGN)
+                target = rows[:, :, 0:P]
+                for i in range(count):
+                    picked[step, first + i] = rows[:, i, 0:P]
+            else:
+                target = late[step][:]
+                for i in range(count):
+                    picked[step, first + i] = target[:, i * P : (i + 1) * P]
             nc.vector.tensor_copy(
-                picked(c, step, chunks), tab[step % 2][:].bitcast(U32).indirect(listed(offsets, c, chunks))
-            )
-
-        def gather_src_scales(c):
-            nc.vector.tensor_copy(
-                src_sc[c // 2][:], tab_sc[:].bitcast(U8).indirect(listed(src_list, c, 2))
-            )
-
-        def gather_dst_scales(c):
-            nc.vector.tensor_copy(dst_sc[c // 2][:], tab_sc[:].bitcast(U8).indirect(listed(dst_list, c, 2)))
-            nc.sync.dma_start(
-                out=dst_sc1[0:112, c * CHUNK // 4 : (c + 2) * CHUNK // 4], in_=dst_sc[c // 2][4:116, :].bitcast(I32)
+                target, tab[:, a * T : (a + 1) * T + spare].bitcast(U32).indirect(listed(offsets, first, count))
             )
 
         def first_product(blk, b, steps, closes=False):
-            c = blk // BLOCKS
-            cols = slice((blk % BLOCKS) * P, (blk % BLOCKS + 1) * P)
-            edges = slice(blk * P, (blk + 1) * P)
-            acc = banks[2 * (blk % 2) + b]
+            within = slice(blk % 4 * P, (blk % 4 + 1) * P)
+            pair = 2 if blk == 2 else blk % 2
+            acc = banks[2 * pair + b]
             for step in steps:
                 a = step % 2
                 if step < 2:
-                    lhsT_scale = dst_sc[blk // 4][:, (blk % 4) * P : (blk % 4 + 1) * P] if a == 0 else dst_sc1[:].bitcast(U8)[:, edges]
-                    rhs = wt[:, a, :].bitcast(U8)[:, 2 * BANK * b : 2 * BANK * (b + 1)].bitcast(FP4X4)
+                    lhsT_scale = dst_sc[blk // 4][:, within] if a == 0 else moved_sc[blk // 4][:].bitcast(U8)[:, within]
+                    rhs = wt[a][:].bitcast(U8)[:, 2 * BANK * b : 2 * BANK * (b + 1)].bitcast(FP4X4)
                     rhs_scale = wt_sc[:, a, :].bitcast(U8)[:, BANK * b : BANK * (b + 1)]
                 else:
-                    lhsT_scale = src_sc[blk // 4][4 * a : P, (blk % 4) * P : (blk % 4 + 1) * P]
+                    part = min(blk // BLOCKS, 2)
+                    col = (blk - part * BLOCKS) * P
+                    lhsT_scale = src_sc[part][4 * a : P, col : col + P]
                     rhs = ws[a][:, BANK * b : BANK * (b + 1)].bitcast(FP8X4)
-                    rhs_scale = ws_sc[:, a, :].bitcast(U8)[:, BANK * b : BANK * (b + 1)]
+                    rhs_scale = ws_sc[:].bitcast(U8)[8 + 4 * a : P, BANK * b : BANK * (b + 1)]
                 nc.tensor.matmul_mx(
                     out=acc[:],
-                    lhsT=picked(c, step)[:, cols].bitcast(FP8X4),
+                    lhsT=picked[step, blk].bitcast(FP8X4),
                     lhsT_scale=lhsT_scale,
                     rhs=rhs,
                     rhs_scale=rhs_scale,
@@ -169,19 +175,20 @@ def tile_list_msg_none_none_kernel(
                 )
 
         def whole_half(blk, b):
-            first_product(blk, b, (0, 1, 2, 3), closes=True)
+            first_product(blk, b, (0, 2, 3, 1), closes=True)
 
-        def turn_and_quantise(c):
-            for b in range(2):
-                turned = banks[4 + b][:].rearrange("p (i u j) -> p i u j", i=2, u=2)
-                for i in range(BLOCKS):
-                    words = h_rows[c * BLOCKS + i][b][:].bitcast(F32)
-                    for u in range(2):
-                        nc.tensor.transpose(turned[:, i, u, :], words[:, u * P : (u + 1) * P], ident[:])
-                nc.scalar.copy(
-                    out=grouped[c][:, b, :, :].rearrange("p (i j) u -> p i j u", i=2),
-                    in_=turned.rearrange("p i u j -> p i j u"),
-                )
+        def turn(c, b, bank):
+            turned = bank[:].rearrange("p (i u j) -> p i u j", i=2, u=2)
+            for i in range(BLOCKS):
+                words = h_rows[c * BLOCKS + i][b][:].bitcast(F32)
+                for u in range(2):
+                    nc.tensor.transpose(turned[:, i, u, :], words[:, u * P : (u + 1) * P], ident[:])
+            nc.scalar.copy(
+                out=grouped[c][:, b, :, :].rearrange("p (i j) u -> p i j u", i=2),
+                in_=turned.rearrange("p i u j -> p i j u"),
+            )
+
+        def quantise(c):
             nc.vector.quantize_mx(
                 out=h_codes[:, c, :, :].rearrange("p b j -> p (b j)").bitcast(FP8X4),
                 scales=h_sc[:, c, :, :].rearrange("p b j -> p (b j)"),
@@ -205,48 +212,79 @@ def tile_list_msg_none_none_kernel(
             for t, acc in zip(tiles, accs):
                 nc.scalar.copy(out=y_sb[t][:, c * CHUNK : (c + 1) * CHUNK], in_=acc)
 
-        gather_words(0, 0)
-        gather_dst_scales(0)
+        def gather_scales(plane, offsets, first, count):
+            nc.vector.tensor_copy(plane[:], tab_sc[:].bitcast(U8).indirect(listed(offsets, first, count)))
+
+        def move_plane(queue, half):
+            queue.dma_start(
+                out=moved_sc[half][0:112, :], in_=dst_sc[half][4:116, :].bitcast(I32)
+            )
+
+        gather_scales(dst_sc[0], dst_list, 0, 4)
+        move_plane(nc.gpsimd, 0)
+        for t, first in ((1, SPLIT), (2, 0), (3, 0)):
+            for col in range(first, T, PIECE):
+                nc.gpsimd.memset(placed[t][:, col : min(col + PIECE, T)].bitcast(I32), 0)
         nc.sync.dma_start(out=wd[:], in_=wd_words.bitcast(I32).rearrange("a p c -> p a c"))
         for q in range(4):
-            load_side_by_side(nc.sync, wd_sc, wd_scales, q)
+            load_side_by_side(wd_sc, wd_scales, q)
         nc.sync.dma_start(out=weight[:], in_=wgo)
-        gather_words(0, 2)
-        gather_src_scales(0)
-        gather_words(1, 0)
-        gather_words(1, 2)
-        for c in range(2):
-            gather_words(c, 3)
-            gather_words(c, 1)
+        gather_scales(src_sc[0], src_list, 0, 2)
+        gather_scales(src_sc[1], src_list, 2, 2)
+        for plane, bank in ((dst_sc[0], banks[6]), (dst_sc[0], banks[7]), (src_sc[1], banks[6]), (src_sc[1], banks[7])):
+            nc.tensor.matmul_mx(
+                out=bank[:],
+                lhsT=ws[0][:, 0:P].bitcast(FP8X4),
+                lhsT_scale=plane[:, 0:P],
+                rhs=wt[0][:].bitcast(U8)[:, 0 : 2 * BANK].bitcast(FP4X4),
+                rhs_scale=dst_sc[0][:],
+                start=True,
+                stop=True,
+            )
+        gather_words(0, 0, 3)
+        gather_words(2, 0, 3)
+        gather_words(3, 0, 3)
+        gather_words(1, 0, 3)
+        gather_words(0, 3, 3, spare=8)
+        gather_words(2, 3, 3, spare=8)
+        gather_words(3, 3, 3)
+        gather_words(1, 3, 3)
 
         for step in (0, 2):
             for b in range(2):
                 for blk in range(BLOCKS):
                     first_product(blk, b, (step,))
-        gather_dst_scales(2)
-        gather_src_scales(2)
-        for step in range(4):
-            gather_words(2, step)
         for b in range(2):
-            for blk in range(BLOCKS):
-                first_product(blk, b, (3, 1), closes=True)
-        for c in range(CHUNKS):
+            for step in (3, 1):
+                for blk in range(BLOCKS):
+                    first_product(blk, b, (step,), closes=(step == 1))
+        gather_scales(dst_sc[1], dst_list, 4, 4)
+        move_plane(nc.sync, 1)
+        gather_scales(src_sc[2], src_list, 4, 4)
+        for b in range(2):
+            turn(0, b, banks[2 + b])
+        gather_words(0, 6, 2)
+        quantise(0)
+        gather_words(2, 6, 2)
+        gather_words(3, 6, 2)
+        gather_words(1, 6, 2)
+        second_product(0, (0, 1), (banks[0][:, 0:CHUNK], banks[1][:, 0:CHUNK]))
+        for blk in (2, 3):
+            for b in range(2):
+                whole_half(blk, b)
+        for c in range(1, CHUNKS):
             ahead = 2 * c + 2
             if c < last:
-                first_product(ahead, 0, (0, 1, 2))
-            turn_and_quantise(c)
+                first_product(ahead, 0, (0, 2, 3))
+            for b in range(2):
+                turn(c, b, banks[4 + b])
+            quantise(c)
             if c < last:
-                first_product(ahead, 0, (3,), closes=True)
-            if c == 0:
-                for step in range(4):
-                    gather_words(last, step)
+                first_product(ahead, 0, (1,), closes=True)
+                first_product(ahead, 1, (0, 2))
+            second_product(c - 1, (2, 3), (banks[4][:, 0:CHUNK], banks[4][:, CHUNK:BANK]))
             if c < last:
-                first_product(ahead, 1, (0, 1))
-            if c > 0:
-                second_product(c - 1, (2, 3), (banks[4][:, 0:CHUNK], banks[4][:, CHUNK:BANK]))
-            if c < last:
-                first_product(ahead, 1, (2, 3), closes=True)
-            if c < last:
+                first_product(ahead, 1, (3, 1), closes=True)
                 whole_half(ahead + 1, 0)
             second_product(c, (0, 1), (banks[6][:, 0:CHUNK], banks[7][:, 0:CHUNK]))
             if c < last:
@@ -258,7 +296,7 @@ def tile_list_msg_none_none_kernel(
         for c, t, chunks in order:
             cols = slice(c * CHUNK, (c + chunks) * CHUNK)
             nc.vector.tensor_tensor(
-                placed[t][:].indirect(listed(dst_list, c, chunks)),
+                placed[t][:].indirect(listed(dst_list, c * BLOCKS, chunks * BLOCKS)),
                 y_sb[t][:, cols],
                 weight[:, cols],
                 mybir.AluOpType.mult,

@@ -23,7 +23,7 @@ BLOCKS = CHUNK // P
 N_TILES = N // P
 ALIGN = 64
 SPLIT = 896
-PIECE = 256
+PIECE = 512
 PAD = 16
 
 
@@ -77,6 +77,7 @@ def tile_list_msg_none_none_kernel(
         h_sc = keep.tile([P, CHUNKS, 2, CHUNK], U8, align_bytes=ALIGN)
         banks = [psum.tile([P, BANK], F32, name="bank%d" % i) for i in range(8)]
         ident = keep.tile([P, P], F32)
+        ident_made = keep.tile([P, P], F32)
         y_sb = [keep.tile([P, J], F32, name="y%d" % t) for t in range(N_TILES)]
         placed = [keep.tile([P, T], F32, name="placed%d" % t) for t in range(N_TILES)]
 
@@ -84,7 +85,8 @@ def tile_list_msg_none_none_kernel(
         nc.gpsimd.memset(wt_sc[:], 0)
         nc.gpsimd.memset(moved_sc[0][:], 0)
         nc.gpsimd.memset(ws_sc[:], 0)
-        make_identity(nc, ident[:])
+        make_identity(nc, ident_made[:])
+        nc.scalar.copy(out=ident[:], in_=ident_made[:])
         nc.gpsimd.memset(wd_sc[:], 0)
         nc.gpsimd.memset(moved_sc[1][:], 0)
         for t, width in ((0, T), (1, SPLIT)):
@@ -108,14 +110,13 @@ def tile_list_msg_none_none_kernel(
         nc.sync.dma_start(dst_list[:], offs2)
         nc.sync.dma_start(src_list[:], offs)
         nc.sync.dma_start(out=wt[0][:], in_=wt_words[0].bitcast(I32))
-        nc.sync.dma_start(out=ws[0][:, 0:P], in_=words8(ws_words, 0)[:, 0:P])
         for q in range(4):
             load_packed(tab_sc, 0, tab_scales, q)
         nc.sync.dma_start(out=tab[:, 0:T], in_=words8(tab_words, 0))
         for q in range(4):
             load_side_by_side(wt_sc, wt_scales, q)
         nc.sync.dma_start(out=tab[:, T : 2 * T], in_=words8(tab_words, 1))
-        nc.sync.dma_start(out=ws[0][:, P:R], in_=words8(ws_words, 0)[:, P:R])
+        nc.sync.dma_start(out=ws[0][:], in_=words8(ws_words, 0))
         for q in range(4):
             load_packed(ws_sc, 8, ws_scales, q)
         nc.sync.dma_start(out=ws[1][:], in_=words8(ws_words, 1))
@@ -220,6 +221,8 @@ def tile_list_msg_none_none_kernel(
                 out=moved_sc[half][0:112, :], in_=dst_sc[half][4:116, :].bitcast(I32)
             )
 
+        gather_scales(src_sc[0], src_list, 0, 2)
+        gather_scales(src_sc[1], src_list, 2, 2)
         gather_scales(dst_sc[0], dst_list, 0, 4)
         move_plane(nc.gpsimd, 0)
         for t, first in ((1, SPLIT), (2, 0), (3, 0)):
@@ -229,18 +232,6 @@ def tile_list_msg_none_none_kernel(
         for q in range(4):
             load_side_by_side(wd_sc, wd_scales, q)
         nc.sync.dma_start(out=weight[:], in_=wgo)
-        gather_scales(src_sc[0], src_list, 0, 2)
-        gather_scales(src_sc[1], src_list, 2, 2)
-        for plane, bank in ((dst_sc[0], banks[6]), (dst_sc[0], banks[7]), (src_sc[1], banks[6]), (src_sc[1], banks[7])):
-            nc.tensor.matmul_mx(
-                out=bank[:],
-                lhsT=ws[0][:, 0:P].bitcast(FP8X4),
-                lhsT_scale=plane[:, 0:P],
-                rhs=wt[0][:].bitcast(U8)[:, 0 : 2 * BANK].bitcast(FP4X4),
-                rhs_scale=dst_sc[0][:],
-                start=True,
-                stop=True,
-            )
         gather_words(0, 0, 3)
         gather_words(2, 0, 3)
         gather_words(3, 0, 3)

@@ -22,7 +22,7 @@ CHUNKS = J // CHUNK
 BLOCKS = CHUNK // P
 N_TILES = N // P
 ALIGN = 64
-SPLIT = 896
+SPLIT = 1024
 PIECE = 512
 PAD = 16
 
@@ -146,7 +146,7 @@ def tile_list_msg_none_none_kernel(
 
         def first_product(blk, b, steps, closes=False):
             within = slice(blk % 4 * P, (blk % 4 + 1) * P)
-            pair = 2 if blk == 2 else blk % 2
+            pair = blk if blk < 4 else blk % 2
             acc = banks[2 * pair + b]
             for step in steps:
                 a = step % 2
@@ -236,14 +236,14 @@ def tile_list_msg_none_none_kernel(
         gather_words(2, 0, 3)
         gather_words(3, 0, 3)
         gather_words(1, 0, 3)
-        gather_words(0, 3, 3, spare=8)
+        gather_words(0, 3, 3)
         gather_words(2, 3, 3, spare=8)
         gather_words(3, 3, 3)
         gather_words(1, 3, 3)
 
-        for step in (0, 2):
+        for blks, step in (((0, 1), 0), ((2, 3), 0), ((0, 1), 2)):
             for b in range(2):
-                for blk in range(BLOCKS):
+                for blk in blks:
                     first_product(blk, b, (step,))
         for b in range(2):
             for step in (3, 1):
@@ -262,7 +262,7 @@ def tile_list_msg_none_none_kernel(
         second_product(0, (0, 1), (banks[0][:, 0:CHUNK], banks[1][:, 0:CHUNK]))
         for blk in (2, 3):
             for b in range(2):
-                whole_half(blk, b)
+                first_product(blk, b, (2, 3, 1), closes=True)
         for c in range(1, CHUNKS):
             ahead = 2 * c + 2
             if c < last:
@@ -277,9 +277,8 @@ def tile_list_msg_none_none_kernel(
             if c < last:
                 first_product(ahead, 1, (3, 1), closes=True)
                 whole_half(ahead + 1, 0)
-            second_product(c, (0, 1), (banks[6][:, 0:CHUNK], banks[7][:, 0:CHUNK]))
-            if c < last:
                 whole_half(ahead + 1, 1)
+            second_product(c, (0, 1), (banks[6][:, 0:CHUNK], banks[7][:, 0:CHUNK]))
         second_product(last, (2, 3), (banks[0][:, 0:CHUNK], banks[1][:, 0:CHUNK]))
 
         order = [(c, t, 1) for c in range(CHUNKS) for t in range(N_TILES) if c < last - 1 or t < N_TILES - 1]

@@ -22,7 +22,7 @@ CHUNKS = J // CHUNK
 BLOCKS = CHUNK // P
 N_TILES = N // P
 ALIGN = 64
-SPLIT = 1024
+SPLIT = 1280
 PIECE = 512
 PAD = 16
 
@@ -81,20 +81,8 @@ def tile_list_msg_none_none_kernel(
         y_sb = [keep.tile([P, J], F32, name="y%d" % t) for t in range(N_TILES)]
         placed = [keep.tile([P, T], F32, name="placed%d" % t) for t in range(N_TILES)]
 
-        nc.gpsimd.memset(tab_sc[:], 0)
-        nc.gpsimd.memset(wt_sc[:], 0)
-        nc.gpsimd.memset(moved_sc[0][:], 0)
-        nc.gpsimd.memset(ws_sc[:], 0)
-        make_identity(nc, ident_made[:])
-        nc.scalar.copy(out=ident[:], in_=ident_made[:])
-        nc.gpsimd.memset(wd_sc[:], 0)
-        nc.gpsimd.memset(moved_sc[1][:], 0)
-        for t, width in ((0, T), (1, SPLIT)):
-            nc.vector.memset(placed[t][:, 0 : width - 1].bitcast(I32), 0)
-            nc.vector.memset(placed[t][:, width - 1 : width].bitcast(I32), 0)
-
-        def load_packed(plane, first, scales, q):
-            nc.sync.dma_start(
+        def load_packed(queue, plane, first, scales, q):
+            queue.dma_start(
                 out=plane[32 * q + first : 32 * q + first + 8, :], in_=scales.bitcast(I32)[:, 4 * q : 4 * q + 4, :]
             )
 
@@ -107,18 +95,32 @@ def tile_list_msg_none_none_kernel(
         def words8(w, a):
             return w[a].rearrange("p c i -> p (c i)").bitcast(I32)
 
+        nc.gpsimd.memset(tab_sc[:], 0)
+        nc.gpsimd.memset(wt_sc[:], 0)
+        nc.gpsimd.memset(moved_sc[0][:], 0)
+        nc.gpsimd.memset(ws_sc[:], 0)
+        for q in (0, 1):
+            load_packed(nc.gpsimd, ws_sc, 8, ws_scales, q)
+        make_identity(nc, ident_made[:])
+        nc.scalar.copy(out=ident[:], in_=ident_made[:])
+        nc.gpsimd.memset(wd_sc[:], 0)
+        nc.gpsimd.memset(moved_sc[1][:], 0)
+        for t, width in ((0, T), (1, SPLIT)):
+            nc.vector.memset(placed[t][:, 0 : width - 1].bitcast(I32), 0)
+            nc.vector.memset(placed[t][:, width - 1 : width].bitcast(I32), 0)
+
         nc.sync.dma_start(dst_list[:], offs2)
         nc.sync.dma_start(src_list[:], offs)
         nc.sync.dma_start(out=wt[0][:], in_=wt_words[0].bitcast(I32))
         for q in range(4):
-            load_packed(tab_sc, 0, tab_scales, q)
+            load_packed(nc.sync, tab_sc, 0, tab_scales, q)
         nc.sync.dma_start(out=tab[:, 0:T], in_=words8(tab_words, 0))
         for q in range(4):
             load_side_by_side(wt_sc, wt_scales, q)
         nc.sync.dma_start(out=tab[:, T : 2 * T], in_=words8(tab_words, 1))
+        for q in (2, 3):
+            load_packed(nc.sync, ws_sc, 8, ws_scales, q)
         nc.sync.dma_start(out=ws[0][:], in_=words8(ws_words, 0))
-        for q in range(4):
-            load_packed(ws_sc, 8, ws_scales, q)
         nc.sync.dma_start(out=ws[1][:], in_=words8(ws_words, 1))
         nc.sync.dma_start(out=wt[1][:], in_=wt_words[1].bitcast(I32))
 
@@ -146,7 +148,7 @@ def tile_list_msg_none_none_kernel(
 
         def first_product(blk, b, steps, closes=False):
             within = slice(blk % 4 * P, (blk % 4 + 1) * P)
-            pair = blk if blk < 4 else blk % 2
+            pair = 2 if blk == 2 else blk % 2
             acc = banks[2 * pair + b]
             for step in steps:
                 a = step % 2
@@ -241,7 +243,7 @@ def tile_list_msg_none_none_kernel(
         gather_words(3, 3, 3)
         gather_words(1, 3, 3)
 
-        for blks, step in (((0, 1), 0), ((2, 3), 0), ((0, 1), 2)):
+        for blks, step in (((0, 1), 0), ((2,), 0), ((0, 1), 2)):
             for b in range(2):
                 for blk in blks:
                     first_product(blk, b, (step,))
@@ -260,9 +262,10 @@ def tile_list_msg_none_none_kernel(
         gather_words(3, 6, 2)
         gather_words(1, 6, 2)
         second_product(0, (0, 1), (banks[0][:, 0:CHUNK], banks[1][:, 0:CHUNK]))
-        for blk in (2, 3):
-            for b in range(2):
-                first_product(blk, b, (2, 3, 1), closes=True)
+        for b in range(2):
+            first_product(2, b, (2, 3, 1), closes=True)
+        for b in range(2):
+            whole_half(3, b)
         for c in range(1, CHUNKS):
             ahead = 2 * c + 2
             if c < last:
@@ -277,8 +280,9 @@ def tile_list_msg_none_none_kernel(
             if c < last:
                 first_product(ahead, 1, (3, 1), closes=True)
                 whole_half(ahead + 1, 0)
-                whole_half(ahead + 1, 1)
             second_product(c, (0, 1), (banks[6][:, 0:CHUNK], banks[7][:, 0:CHUNK]))
+            if c < last:
+                whole_half(ahead + 1, 1)
         second_product(last, (2, 3), (banks[0][:, 0:CHUNK], banks[1][:, 0:CHUNK]))
 
         order = [(c, t, 1) for c in range(CHUNKS) for t in range(N_TILES) if c < last - 1 or t < N_TILES - 1]

@@ -22,7 +22,6 @@ CHUNKS = J // CHUNK
 BLOCKS = CHUNK // P
 N_TILES = N // P
 ALIGN = 64
-SPLIT = 1280
 PIECE = 512
 PAD = 16
 
@@ -40,24 +39,24 @@ def tile_list_msg_none_none_kernel(
         dst_list = keep.tile([P, J // 16], U16)
         tab = keep.tile([P, 2 * T], I32, align_bytes=ALIGN)
         tab_sc = keep.tile([P, T // 4], I32, align_bytes=ALIGN)
-        ws = [keep.tile([P, R], I32, name="ws%d" % a, align_bytes=ALIGN) for a in range(2)]
+        ws_first = [keep.tile([P, BANK], I32, name="ws0%d" % b, align_bytes=ALIGN) for b in range(2)]
+        ws_second = keep.tile([P, R], I32, align_bytes=ALIGN)
         wt = [keep.tile([P, R // 2], I32, name="wt%d" % a, align_bytes=ALIGN) for a in range(2)]
         wt_sc = keep.tile([P, 2, R // 4], I32, align_bytes=ALIGN)
         ws_sc = keep.tile([P, R // 4], I32, align_bytes=ALIGN)
         wd_sc = keep.tile([P, 2, N // 4], I32, align_bytes=ALIGN)
         src_sc = [
-            shared.tile([P, CHUNK], U8, name="src_sc0", offset=8192 + 384, align_bytes=ALIGN),
-            keep.tile([P, CHUNK], U8, name="src_sc1", align_bytes=ALIGN),
-            shared.tile([P, 2 * CHUNK], U8, name="src_sc2", offset=8192 + 512, align_bytes=ALIGN),
+            keep.tile([P, J // 2], U8, name="src_sc0", align_bytes=ALIGN),
+            shared.tile([P, J // 2], U8, name="src_sc1", offset=0, align_bytes=ALIGN),
         ]
         dst_sc = [
             keep.tile([P, J // 2], U8, name="dst_sc0", align_bytes=ALIGN),
-            shared.tile([P, J // 2], U8, name="dst_sc1", offset=8192, align_bytes=ALIGN),
+            shared.tile([P, J // 2], U8, name="dst_sc1", offset=4096, align_bytes=ALIGN),
         ]
         moved_sc = [keep.tile([P, J // 8], I32, name="moved_sc%d" % half, align_bytes=ALIGN) for half in range(2)]
         wd = keep.tile([P, 2, N // 2], I32, align_bytes=ALIGN)
         weight = keep.tile([P, J], F32)
-        reused = {(0, 0): 4096, (0, 1): 6144, (1, 1): 7168, (2, 0): 6144, (2, 1): 7168}
+        reused = {(0, 0): 4096, (0, 1): 5120, (1, 1): 6144, (2, 0): 5120, (2, 1): 6144}
         h_rows = [
             [
                 shared.tile([P, BANK], BF16, name="h_rows%d%d" % (blk, b), offset=reused[blk, b])
@@ -69,10 +68,6 @@ def tile_list_msg_none_none_kernel(
         ]
         grouped = [keep.tile([P, 2, CHUNK, 2], F32, name="grouped%d" % c, align_bytes=ALIGN) for c in range(1, CHUNKS)]
         grouped.insert(0, shared.tile([P, 2, CHUNK, 2], F32, name="grouped0", offset=0, align_bytes=ALIGN))
-        late = [
-            shared.tile([P, CHUNK], U32, name="late%d" % step, offset=1024 * (step or 4), align_bytes=ALIGN)
-            for step in range(4)
-        ]
         h_codes = keep.tile([P, CHUNKS, 2, CHUNK], U32, align_bytes=ALIGN)
         h_sc = keep.tile([P, CHUNKS, 2, CHUNK], U8, align_bytes=ALIGN)
         banks = [psum.tile([P, BANK], F32, name="bank%d" % i) for i in range(8)]
@@ -86,8 +81,8 @@ def tile_list_msg_none_none_kernel(
                 out=plane[32 * q + first : 32 * q + first + 8, :], in_=scales.bitcast(I32)[:, 4 * q : 4 * q + 4, :]
             )
 
-        def load_side_by_side(plane, scales, q):
-            nc.sync.dma_start(
+        def load_side_by_side(queue, plane, scales, q):
+            queue.dma_start(
                 out=plane[32 * q : 32 * q + 4, :, :],
                 in_=scales.bitcast(I32)[:, 4 * q : 4 * q + 4, :].rearrange("a r n -> r a n"),
             )
@@ -95,33 +90,33 @@ def tile_list_msg_none_none_kernel(
         def words8(w, a):
             return w[a].rearrange("p c i -> p (c i)").bitcast(I32)
 
+        def clear_on_vector(words):
+            width = words.shape[1]
+            nc.vector.memset(words[:, 0 : width // 2 + 1], 0)
+            nc.vector.memset(words[:, width // 2 + 1 : width], 0)
+
         nc.gpsimd.memset(tab_sc[:], 0)
-        nc.gpsimd.memset(wt_sc[:], 0)
-        nc.gpsimd.memset(moved_sc[0][:], 0)
-        nc.gpsimd.memset(ws_sc[:], 0)
-        for q in (0, 1):
-            load_packed(nc.gpsimd, ws_sc, 8, ws_scales, q)
-        make_identity(nc, ident_made[:])
-        nc.scalar.copy(out=ident[:], in_=ident_made[:])
-        nc.gpsimd.memset(wd_sc[:], 0)
-        nc.gpsimd.memset(moved_sc[1][:], 0)
-        for t, width in ((0, T), (1, SPLIT)):
-            nc.vector.memset(placed[t][:, 0 : width - 1].bitcast(I32), 0)
-            nc.vector.memset(placed[t][:, width - 1 : width].bitcast(I32), 0)
+        clear_on_vector(wt_sc[:].rearrange("p a n -> p (a n)"))
+        for q in (0, 2):
+            load_side_by_side(nc.gpsimd, wt_sc, wt_scales, q)
+        clear_on_vector(ws_sc[:])
+        clear_on_vector(moved_sc[0][:])
+        clear_on_vector(placed[0][:].bitcast(I32))
 
         nc.sync.dma_start(dst_list[:], offs2)
         nc.sync.dma_start(src_list[:], offs)
-        nc.sync.dma_start(out=wt[0][:], in_=wt_words[0].bitcast(I32))
+        nc.sync.dma_start(out=ws_first[0][:], in_=words8(ws_words, 0)[:, 0:BANK])
         for q in range(4):
             load_packed(nc.sync, tab_sc, 0, tab_scales, q)
         nc.sync.dma_start(out=tab[:, 0:T], in_=words8(tab_words, 0))
         for q in range(4):
-            load_side_by_side(wt_sc, wt_scales, q)
-        nc.sync.dma_start(out=tab[:, T : 2 * T], in_=words8(tab_words, 1))
-        for q in (2, 3):
             load_packed(nc.sync, ws_sc, 8, ws_scales, q)
-        nc.sync.dma_start(out=ws[0][:], in_=words8(ws_words, 0))
-        nc.sync.dma_start(out=ws[1][:], in_=words8(ws_words, 1))
+        nc.sync.dma_start(out=ws_first[1][:], in_=words8(ws_words, 0)[:, BANK:R])
+        nc.sync.dma_start(out=tab[:, T : 2 * T], in_=words8(tab_words, 1))
+        for q in (1, 3):
+            load_side_by_side(nc.sync, wt_sc, wt_scales, q)
+        nc.sync.dma_start(out=wt[0][:], in_=wt_words[0].bitcast(I32))
+        nc.sync.dma_start(out=ws_second[:], in_=words8(ws_words, 1))
         nc.sync.dma_start(out=wt[1][:], in_=wt_words[1].bitcast(I32))
 
         last = CHUNKS - 1
@@ -133,23 +128,20 @@ def tile_list_msg_none_none_kernel(
         def gather_words(step, first, count, spare=0):
             offsets = dst_list if step < 2 else src_list
             a = step % 2
-            if count % 2:
-                rows = keep.tile([P, count, P + PAD], U32, name="picked%d%d" % (step, first), align_bytes=ALIGN)
-                target = rows[:, :, 0:P]
-                for i in range(count):
-                    picked[step, first + i] = rows[:, i, 0:P]
-            else:
-                target = late[step][:]
-                for i in range(count):
-                    picked[step, first + i] = target[:, i * P : (i + 1) * P]
+            rows = keep.tile([P, count, P + PAD], U32, name="picked%d%d" % (step, first), align_bytes=ALIGN)
+            target = rows[:, :, 0:P]
+            for i in range(count):
+                picked[step, first + i] = rows[:, i, 0:P]
             nc.vector.tensor_copy(
                 target, tab[:, a * T : (a + 1) * T + spare].bitcast(U32).indirect(listed(offsets, first, count))
             )
 
+        def steps_of(blk):
+            return (2, 0, 3, 1) if blk < 4 else (0, 2, 3, 1)
+
         def first_product(blk, b, steps, closes=False):
             within = slice(blk % 4 * P, (blk % 4 + 1) * P)
-            pair = 2 if blk == 2 else blk % 2
-            acc = banks[2 * pair + b]
+            acc = banks[2 * (blk % 2) + b]
             for step in steps:
                 a = step % 2
                 if step < 2:
@@ -157,10 +149,9 @@ def tile_list_msg_none_none_kernel(
                     rhs = wt[a][:].bitcast(U8)[:, 2 * BANK * b : 2 * BANK * (b + 1)].bitcast(FP4X4)
                     rhs_scale = wt_sc[:, a, :].bitcast(U8)[:, BANK * b : BANK * (b + 1)]
                 else:
-                    part = min(blk // BLOCKS, 2)
-                    col = (blk - part * BLOCKS) * P
-                    lhsT_scale = src_sc[part][4 * a : P, col : col + P]
-                    rhs = ws[a][:, BANK * b : BANK * (b + 1)].bitcast(FP8X4)
+                    lhsT_scale = src_sc[blk // 4][4 * a : P, within]
+                    words = ws_first[b][:] if a == 0 else ws_second[:, BANK * b : BANK * (b + 1)]
+                    rhs = words.bitcast(FP8X4)
                     rhs_scale = ws_sc[:].bitcast(U8)[8 + 4 * a : P, BANK * b : BANK * (b + 1)]
                 nc.tensor.matmul_mx(
                     out=acc[:],
@@ -168,7 +159,7 @@ def tile_list_msg_none_none_kernel(
                     lhsT_scale=lhsT_scale,
                     rhs=rhs,
                     rhs_scale=rhs_scale,
-                    start=(step == 0),
+                    start=(step == steps_of(blk)[0]),
                     stop=(closes and step == steps[-1]),
                 )
             if closes:
@@ -178,7 +169,7 @@ def tile_list_msg_none_none_kernel(
                 )
 
         def whole_half(blk, b):
-            first_product(blk, b, (0, 2, 3, 1), closes=True)
+            first_product(blk, b, steps_of(blk), closes=True)
 
         def turn(c, b, bank):
             turned = bank[:].rearrange("p (i u j) -> p i u j", i=2, u=2)
@@ -223,62 +214,57 @@ def tile_list_msg_none_none_kernel(
                 out=moved_sc[half][0:112, :], in_=dst_sc[half][4:116, :].bitcast(I32)
             )
 
-        gather_scales(src_sc[0], src_list, 0, 2)
-        gather_scales(src_sc[1], src_list, 2, 2)
         gather_scales(dst_sc[0], dst_list, 0, 4)
         move_plane(nc.gpsimd, 0)
-        for t, first in ((1, SPLIT), (2, 0), (3, 0)):
-            for col in range(first, T, PIECE):
-                nc.gpsimd.memset(placed[t][:, col : min(col + PIECE, T)].bitcast(I32), 0)
+        gather_scales(src_sc[0], src_list, 0, 4)
+        make_identity(nc, ident_made[:])
+        nc.scalar.copy(out=ident[:], in_=ident_made[:])
+        nc.gpsimd.memset(wd_sc[:], 0)
+        nc.gpsimd.memset(moved_sc[1][:], 0)
+        for t in range(1, N_TILES):
+            for col in range(0, T, PIECE):
+                nc.gpsimd.memset(placed[t][:, col : col + PIECE].bitcast(I32), 0)
         nc.sync.dma_start(out=wd[:], in_=wd_words.bitcast(I32).rearrange("a p c -> p a c"))
         for q in range(4):
-            load_side_by_side(wd_sc, wd_scales, q)
+            load_side_by_side(nc.sync, wd_sc, wd_scales, q)
         nc.sync.dma_start(out=weight[:], in_=wgo)
-        gather_words(0, 0, 3)
         gather_words(2, 0, 3)
+        gather_words(0, 0, 3)
+        gather_words(2, 3, 5)
         gather_words(3, 0, 3)
         gather_words(1, 0, 3)
-        gather_words(0, 3, 3)
-        gather_words(2, 3, 3, spare=8)
-        gather_words(3, 3, 3)
-        gather_words(1, 3, 3)
+        gather_words(0, 3, 5, spare=8)
+        gather_words(3, 3, 5)
+        gather_words(1, 3, 5)
 
-        for blks, step in (((0, 1), 0), ((2,), 0), ((0, 1), 2)):
+        for step in (2, 0):
             for b in range(2):
-                for blk in blks:
+                for blk in range(BLOCKS):
                     first_product(blk, b, (step,))
         for b in range(2):
             for step in (3, 1):
                 for blk in range(BLOCKS):
                     first_product(blk, b, (step,), closes=(step == 1))
-        gather_scales(dst_sc[1], dst_list, 4, 4)
-        move_plane(nc.sync, 1)
-        gather_scales(src_sc[2], src_list, 4, 4)
-        for b in range(2):
-            turn(0, b, banks[2 + b])
-        gather_words(0, 6, 2)
-        quantise(0)
-        gather_words(2, 6, 2)
-        gather_words(3, 6, 2)
-        gather_words(1, 6, 2)
-        second_product(0, (0, 1), (banks[0][:, 0:CHUNK], banks[1][:, 0:CHUNK]))
-        for b in range(2):
-            first_product(2, b, (2, 3, 1), closes=True)
-        for b in range(2):
-            whole_half(3, b)
-        for c in range(1, CHUNKS):
+        for c in range(CHUNKS):
             ahead = 2 * c + 2
+            steps = steps_of(ahead)
             if c < last:
-                first_product(ahead, 0, (0, 2, 3))
+                first_product(ahead, 0, steps[0:3])
             for b in range(2):
                 turn(c, b, banks[4 + b])
+            if c == 0:
+                gather_scales(dst_sc[1], dst_list, 4, 4)
+                move_plane(nc.sync, 1)
             quantise(c)
+            if c == 0:
+                gather_scales(src_sc[1], src_list, 4, 4)
             if c < last:
-                first_product(ahead, 0, (1,), closes=True)
-                first_product(ahead, 1, (0, 2))
-            second_product(c - 1, (2, 3), (banks[4][:, 0:CHUNK], banks[4][:, CHUNK:BANK]))
+                first_product(ahead, 0, steps[3:4], closes=True)
+                first_product(ahead, 1, steps[0:2])
+            if c > 0:
+                second_product(c - 1, (2, 3), (banks[4][:, 0:CHUNK], banks[4][:, CHUNK:BANK]))
             if c < last:
-                first_product(ahead, 1, (3, 1), closes=True)
+                first_product(ahead, 1, steps[2:4], closes=True)
                 whole_half(ahead + 1, 0)
             second_product(c, (0, 1), (banks[6][:, 0:CHUNK], banks[7][:, 0:CHUNK]))
             if c < last:

@@ -24,6 +24,7 @@ N_TILES = N // P
 ALIGN = 64
 PIECE = 512
 PAD = 16
+STEPS = (0, 2, 3, 1)
 
 
 def tile_list_msg_none_none_kernel(
@@ -39,8 +40,7 @@ def tile_list_msg_none_none_kernel(
         dst_list = keep.tile([P, J // 16], U16)
         tab = keep.tile([P, 2 * T], I32, align_bytes=ALIGN)
         tab_sc = keep.tile([P, T // 4], I32, align_bytes=ALIGN)
-        ws_first = [keep.tile([P, BANK], I32, name="ws0%d" % b, align_bytes=ALIGN) for b in range(2)]
-        ws_second = keep.tile([P, R], I32, align_bytes=ALIGN)
+        ws = [[keep.tile([P, BANK], I32, name="ws%d%d" % (a, b), align_bytes=ALIGN) for b in range(2)] for a in range(2)]
         wt = [keep.tile([P, R // 2], I32, name="wt%d" % a, align_bytes=ALIGN) for a in range(2)]
         wt_sc = keep.tile([P, 2, R // 4], I32, align_bytes=ALIGN)
         ws_sc = keep.tile([P, R // 4], I32, align_bytes=ALIGN)
@@ -96,27 +96,28 @@ def tile_list_msg_none_none_kernel(
             nc.vector.memset(words[:, width // 2 + 1 : width], 0)
 
         nc.gpsimd.memset(tab_sc[:], 0)
-        clear_on_vector(wt_sc[:].rearrange("p a n -> p (a n)"))
-        for q in (0, 2):
-            load_side_by_side(nc.gpsimd, wt_sc, wt_scales, q)
         clear_on_vector(ws_sc[:])
+        for q in (0, 2):
+            load_packed(nc.gpsimd, ws_sc, 8, ws_scales, q)
+        clear_on_vector(wt_sc[:].rearrange("p a n -> p (a n)"))
         clear_on_vector(moved_sc[0][:])
         clear_on_vector(placed[0][:].bitcast(I32))
 
         nc.sync.dma_start(dst_list[:], offs2)
         nc.sync.dma_start(src_list[:], offs)
-        nc.sync.dma_start(out=ws_first[0][:], in_=words8(ws_words, 0)[:, 0:BANK])
-        for q in range(4):
+        nc.sync.dma_start(out=ws[0][0][:], in_=words8(ws_words, 0)[:, 0:BANK])
+        for q in (0, 2, 1, 3):
             load_packed(nc.sync, tab_sc, 0, tab_scales, q)
         nc.sync.dma_start(out=tab[:, 0:T], in_=words8(tab_words, 0))
-        for q in range(4):
-            load_packed(nc.sync, ws_sc, 8, ws_scales, q)
-        nc.sync.dma_start(out=ws_first[1][:], in_=words8(ws_words, 0)[:, BANK:R])
-        nc.sync.dma_start(out=tab[:, T : 2 * T], in_=words8(tab_words, 1))
-        for q in (1, 3):
+        for q in (0, 2, 1, 3):
             load_side_by_side(nc.sync, wt_sc, wt_scales, q)
         nc.sync.dma_start(out=wt[0][:], in_=wt_words[0].bitcast(I32))
-        nc.sync.dma_start(out=ws_second[:], in_=words8(ws_words, 1))
+        nc.sync.dma_start(out=tab[:, T : 2 * T], in_=words8(tab_words, 1))
+        for q in (1, 3):
+            load_packed(nc.sync, ws_sc, 8, ws_scales, q)
+        nc.sync.dma_start(out=ws[0][1][:], in_=words8(ws_words, 0)[:, BANK:R])
+        for b in range(2):
+            nc.sync.dma_start(out=ws[1][b][:], in_=words8(ws_words, 1)[:, BANK * b : BANK * (b + 1)])
         nc.sync.dma_start(out=wt[1][:], in_=wt_words[1].bitcast(I32))
 
         last = CHUNKS - 1
@@ -136,12 +137,9 @@ def tile_list_msg_none_none_kernel(
                 target, tab[:, a * T : (a + 1) * T + spare].bitcast(U32).indirect(listed(offsets, first, count))
             )
 
-        def steps_of(blk):
-            return (2, 0, 3, 1) if blk < 4 else (0, 2, 3, 1)
-
         def first_product(blk, b, steps, closes=False):
             within = slice(blk % 4 * P, (blk % 4 + 1) * P)
-            acc = banks[2 * (blk % 2) + b]
+            acc = banks[2 * (2 if blk == 2 else blk % 2) + b]
             for step in steps:
                 a = step % 2
                 if step < 2:
@@ -150,8 +148,7 @@ def tile_list_msg_none_none_kernel(
                     rhs_scale = wt_sc[:, a, :].bitcast(U8)[:, BANK * b : BANK * (b + 1)]
                 else:
                     lhsT_scale = src_sc[blk // 4][4 * a : P, within]
-                    words = ws_first[b][:] if a == 0 else ws_second[:, BANK * b : BANK * (b + 1)]
-                    rhs = words.bitcast(FP8X4)
+                    rhs = ws[a][b][:].bitcast(FP8X4)
                     rhs_scale = ws_sc[:].bitcast(U8)[8 + 4 * a : P, BANK * b : BANK * (b + 1)]
                 nc.tensor.matmul_mx(
                     out=acc[:],
@@ -159,7 +156,7 @@ def tile_list_msg_none_none_kernel(
                     lhsT_scale=lhsT_scale,
                     rhs=rhs,
                     rhs_scale=rhs_scale,
-                    start=(step == steps_of(blk)[0]),
+                    start=(step == STEPS[0]),
                     stop=(closes and step == steps[-1]),
                 )
             if closes:
@@ -169,7 +166,7 @@ def tile_list_msg_none_none_kernel(
                 )
 
         def whole_half(blk, b):
-            first_product(blk, b, steps_of(blk), closes=True)
+            first_product(blk, b, STEPS, closes=True)
 
         def turn(c, b, bank):
             turned = bank[:].rearrange("p (i u j) -> p i u j", i=2, u=2)
@@ -182,11 +179,11 @@ def tile_list_msg_none_none_kernel(
                 in_=turned.rearrange("p i u j -> p i j u"),
             )
 
-        def quantise(c):
+        def quantise(c, halves):
             nc.vector.quantize_mx(
-                out=h_codes[:, c, :, :].rearrange("p b j -> p (b j)").bitcast(FP8X4),
-                scales=h_sc[:, c, :, :].rearrange("p b j -> p (b j)"),
-                in_=grouped[c][:].rearrange("p b j u -> p (b j u)").bitcast(BF16),
+                out=h_codes[:, c, halves, :].rearrange("p b j -> p (b j)").bitcast(FP8X4),
+                scales=h_sc[:, c, halves, :].rearrange("p b j -> p (b j)"),
+                in_=grouped[c][:, halves, :, :].rearrange("p b j u -> p (b j u)").bitcast(BF16),
             )
 
         def second_product(c, tiles, accs):
@@ -228,46 +225,66 @@ def tile_list_msg_none_none_kernel(
         for q in range(4):
             load_side_by_side(nc.sync, wd_sc, wd_scales, q)
         nc.sync.dma_start(out=weight[:], in_=wgo)
-        gather_words(2, 0, 3)
+        for plane in 3 * [tab_sc[:].bitcast(U8)] + 2 * [src_sc[0][:]]:
+            nc.tensor.matmul_mx(
+                out=banks[6][:],
+                lhsT=ws[0][0][:, 0:P].bitcast(FP8X4),
+                lhsT_scale=plane[:, 0:P],
+                rhs=ws[0][0][:].bitcast(FP8X4),
+                rhs_scale=plane[:, 0:BANK],
+                start=True,
+                stop=True,
+            )
         gather_words(0, 0, 3)
-        gather_words(2, 3, 5)
+        gather_words(2, 0, 5)
+        gather_words(2, 5, 3)
         gather_words(3, 0, 3)
         gather_words(1, 0, 3)
         gather_words(0, 3, 5, spare=8)
         gather_words(3, 3, 5)
         gather_words(1, 3, 5)
 
-        for step in (2, 0):
+        for step in (0, 2):
             for b in range(2):
-                for blk in range(BLOCKS):
+                for blk in range(BLOCKS + 1):
                     first_product(blk, b, (step,))
         for b in range(2):
-            for step in (3, 1):
-                for blk in range(BLOCKS):
-                    first_product(blk, b, (step,), closes=(step == 1))
+            for blk in range(BLOCKS):
+                first_product(blk, b, (3,))
+        for b in range(2):
+            for blk in range(BLOCKS):
+                first_product(blk, b, (1,), closes=True)
         for c in range(CHUNKS):
             ahead = 2 * c + 2
-            steps = steps_of(ahead)
+            steps = STEPS
+            begun, before_turn = {0: (2, 3), 1: (0, 1)}.get(c, (0, 3))
             if c < last:
-                first_product(ahead, 0, steps[0:3])
+                first_product(ahead, 0, steps[begun:before_turn])
             for b in range(2):
-                turn(c, b, banks[4 + b])
+                turn(c, b, banks[(6 if c == 0 else 4) + b])
             if c == 0:
                 gather_scales(dst_sc[1], dst_list, 4, 4)
                 move_plane(nc.sync, 1)
-            quantise(c)
             if c == 0:
+                quantise(c, slice(0, 1))
+                quantise(c, slice(1, 2))
                 gather_scales(src_sc[1], src_list, 4, 4)
+            else:
+                quantise(c, slice(0, 2))
             if c < last:
-                first_product(ahead, 0, steps[3:4], closes=True)
-                first_product(ahead, 1, steps[0:2])
+                first_product(ahead, 0, steps[before_turn:4], closes=True)
+                first_product(ahead, 1, steps[begun:2])
             if c > 0:
                 second_product(c - 1, (2, 3), (banks[4][:, 0:CHUNK], banks[4][:, CHUNK:BANK]))
             if c < last:
                 first_product(ahead, 1, steps[2:4], closes=True)
                 whole_half(ahead + 1, 0)
+            if c == 0:
+                first_product(ahead + 1, 1, steps[0:2])
             second_product(c, (0, 1), (banks[6][:, 0:CHUNK], banks[7][:, 0:CHUNK]))
-            if c < last:
+            if c == 0:
+                first_product(ahead + 1, 1, steps[2:4], closes=True)
+            elif c < last:
                 whole_half(ahead + 1, 1)
         second_product(last, (2, 3), (banks[0][:, 0:CHUNK], banks[1][:, 0:CHUNK]))
 

@@ -25,6 +25,7 @@ ALIGN = 64
 PIECE = 512
 PAD = 16
 STEPS = (0, 2, 3, 1)
+CUTS = ((2, 2, 10), (1, 4, 12), (3, 6, 12), (0, 0, 0))
 
 
 def tile_list_msg_none_none_kernel(
@@ -44,7 +45,7 @@ def tile_list_msg_none_none_kernel(
         wt = [keep.tile([P, R // 2], I32, name="wt%d" % a, align_bytes=ALIGN) for a in range(2)]
         wt_sc = keep.tile([P, 2, R // 4], I32, align_bytes=ALIGN)
         ws_sc = keep.tile([P, R // 4], I32, align_bytes=ALIGN)
-        wd_sc = keep.tile([P, 2, N // 4], I32, align_bytes=ALIGN)
+        wd_sc = shared.tile([P, 2, N // 4], I32, name="wd_sc", offset=10240 + 512, align_bytes=ALIGN)
         src_sc = [
             keep.tile([P, J // 2], U8, name="src_sc0", align_bytes=ALIGN),
             shared.tile([P, J // 2], U8, name="src_sc1", offset=0, align_bytes=ALIGN),
@@ -54,8 +55,8 @@ def tile_list_msg_none_none_kernel(
             shared.tile([P, J // 2], U8, name="dst_sc1", offset=4096, align_bytes=ALIGN),
         ]
         moved_sc = [keep.tile([P, J // 8], I32, name="moved_sc%d" % half, align_bytes=ALIGN) for half in range(2)]
-        wd = keep.tile([P, 2, N // 2], I32, align_bytes=ALIGN)
-        weight = keep.tile([P, J], F32)
+        wd = shared.tile([P, 2, N // 2], I32, name="wd", offset=10240 - 1536, align_bytes=ALIGN)
+        weight = shared.tile([P, J], F32, name="weight", offset=10240 + 1536, align_bytes=ALIGN)
         reused = {(0, 0): 4096, (0, 1): 5120, (1, 1): 6144, (2, 0): 5120, (2, 1): 6144}
         h_rows = [
             [
@@ -68,6 +69,7 @@ def tile_list_msg_none_none_kernel(
         ]
         grouped = [keep.tile([P, 2, CHUNK, 2], F32, name="grouped%d" % c, align_bytes=ALIGN) for c in range(1, CHUNKS)]
         grouped.insert(0, shared.tile([P, 2, CHUNK, 2], F32, name="grouped0", offset=0, align_bytes=ALIGN))
+        late = shared.tile([P, CHUNK], U32, name="late", offset=1024, align_bytes=ALIGN)
         h_codes = keep.tile([P, CHUNKS, 2, CHUNK], U32, align_bytes=ALIGN)
         h_sc = keep.tile([P, CHUNKS, 2, CHUNK], U8, align_bytes=ALIGN)
         banks = [psum.tile([P, BANK], F32, name="bank%d" % i) for i in range(8)]
@@ -116,9 +118,9 @@ def tile_list_msg_none_none_kernel(
         for q in (1, 3):
             load_packed(nc.sync, ws_sc, 8, ws_scales, q)
         nc.sync.dma_start(out=ws[0][1][:], in_=words8(ws_words, 0)[:, BANK:R])
-        for b in range(2):
-            nc.sync.dma_start(out=ws[1][b][:], in_=words8(ws_words, 1)[:, BANK * b : BANK * (b + 1)])
+        nc.sync.dma_start(out=ws[1][0][:], in_=words8(ws_words, 1)[:, 0:BANK])
         nc.sync.dma_start(out=wt[1][:], in_=wt_words[1].bitcast(I32))
+        nc.sync.dma_start(out=ws[1][1][:], in_=words8(ws_words, 1)[:, BANK:R])
 
         last = CHUNKS - 1
         picked = {}
@@ -129,18 +131,34 @@ def tile_list_msg_none_none_kernel(
         def gather_words(step, first, count, spare=0):
             offsets = dst_list if step < 2 else src_list
             a = step % 2
-            rows = keep.tile([P, count, P + PAD], U32, name="picked%d%d" % (step, first), align_bytes=ALIGN)
-            target = rows[:, :, 0:P]
-            for i in range(count):
-                picked[step, first + i] = rows[:, i, 0:P]
+            if count % 2:
+                shape, name = [P, count, P + PAD], "picked%d%d" % (step, first)
+                if (step, first) == (0, 0):
+                    rows = shared.tile(shape, U32, name=name, offset=10240, align_bytes=ALIGN)
+                else:
+                    rows = keep.tile(shape, U32, name=name, align_bytes=ALIGN)
+                target = rows[:, :, 0:P]
+                for i in range(count):
+                    picked[step, first + i] = rows[:, i, 0:P]
+            else:
+                target = late[:]
+                for i in range(count):
+                    picked[step, first + i] = target[:, i * P : (i + 1) * P]
             nc.vector.tensor_copy(
                 target, tab[:, a * T : (a + 1) * T + spare].bitcast(U32).indirect(listed(offsets, first, count))
             )
 
-        def first_product(blk, b, steps, closes=False):
-            within = slice(blk % 4 * P, (blk % 4 + 1) * P)
-            acc = banks[2 * (2 if blk == 2 else blk % 2) + b]
-            for step in steps:
+        def steps_of(blk, b):
+            if b == 1 and blk < BLOCKS:
+                return (0, 2, 1, 3)
+            if blk == BLOCKS:
+                return (0, 1, 2, 3)
+            return STEPS
+
+        def first_passes(passes):
+            for blk, b, step in passes:
+                within = slice(blk % 4 * P, (blk % 4 + 1) * P)
+                acc = banks[2 * (2 if blk == BLOCKS else blk % 2) + b]
                 a = step % 2
                 if step < 2:
                     lhsT_scale = dst_sc[blk // 4][:, within] if a == 0 else moved_sc[blk // 4][:].bitcast(U8)[:, within]
@@ -157,26 +175,24 @@ def tile_list_msg_none_none_kernel(
                     rhs=rhs,
                     rhs_scale=rhs_scale,
                     start=(step == STEPS[0]),
-                    stop=(closes and step == steps[-1]),
+                    stop=(step == steps_of(blk, b)[-1]),
                 )
-            if closes:
-                nc.scalar.copy(
-                    out=h_rows[blk][b][:].rearrange("j (u p e) -> j u p e", u=2, e=2),
-                    in_=acc[:].rearrange("j (p u e) -> j u p e", u=2, e=2),
-                )
+                if step == steps_of(blk, b)[-1]:
+                    nc.scalar.copy(
+                        out=h_rows[blk][b][:].rearrange("j (u p e) -> j u p e", u=2, e=2),
+                        in_=acc[:].rearrange("j (p u e) -> j u p e", u=2, e=2),
+                    )
 
-        def whole_half(blk, b):
-            first_product(blk, b, STEPS, closes=True)
-
-        def turn(c, b, bank):
+        def turn(c, b, bank, blocks=range(BLOCKS)):
             turned = bank[:].rearrange("p (i u j) -> p i u j", i=2, u=2)
-            for i in range(BLOCKS):
+            for i in blocks:
                 words = h_rows[c * BLOCKS + i][b][:].bitcast(F32)
                 for u in range(2):
                     nc.tensor.transpose(turned[:, i, u, :], words[:, u * P : (u + 1) * P], ident[:])
+            within = slice(blocks.start, blocks.stop)
             nc.scalar.copy(
-                out=grouped[c][:, b, :, :].rearrange("p (i j) u -> p i j u", i=2),
-                in_=turned.rearrange("p i u j -> p i j u"),
+                out=grouped[c][:, b, :, :].rearrange("p (i j) u -> p i j u", i=2)[:, within],
+                in_=turned.rearrange("p i u j -> p i j u")[:, within],
             )
 
         def quantise(c, halves):
@@ -216,15 +232,10 @@ def tile_list_msg_none_none_kernel(
         gather_scales(src_sc[0], src_list, 0, 4)
         make_identity(nc, ident_made[:])
         nc.scalar.copy(out=ident[:], in_=ident_made[:])
-        nc.gpsimd.memset(wd_sc[:], 0)
         nc.gpsimd.memset(moved_sc[1][:], 0)
         for t in range(1, N_TILES):
             for col in range(0, T, PIECE):
                 nc.gpsimd.memset(placed[t][:, col : col + PIECE].bitcast(I32), 0)
-        nc.sync.dma_start(out=wd[:], in_=wd_words.bitcast(I32).rearrange("a p c -> p a c"))
-        for q in range(4):
-            load_side_by_side(nc.sync, wd_sc, wd_scales, q)
-        nc.sync.dma_start(out=weight[:], in_=wgo)
         for plane in 3 * [tab_sc[:].bitcast(U8)] + 2 * [src_sc[0][:]]:
             nc.tensor.matmul_mx(
                 out=banks[6][:],
@@ -236,56 +247,49 @@ def tile_list_msg_none_none_kernel(
                 stop=True,
             )
         gather_words(0, 0, 3)
-        gather_words(2, 0, 5)
-        gather_words(2, 5, 3)
+        gather_words(2, 0, 3)
+        gather_words(0, 3, 3)
         gather_words(3, 0, 3)
         gather_words(1, 0, 3)
-        gather_words(0, 3, 5, spare=8)
+        gather_words(2, 3, 5, spare=8)
         gather_words(3, 3, 5)
         gather_words(1, 3, 5)
 
-        for step in (0, 2):
-            for b in range(2):
-                for blk in range(BLOCKS + 1):
-                    first_product(blk, b, (step,))
-        for b in range(2):
-            for blk in range(BLOCKS):
-                first_product(blk, b, (3,))
-        for b in range(2):
-            for blk in range(BLOCKS):
-                first_product(blk, b, (1,), closes=True)
+        early = [(blk, b, STEPS[0]) for b in range(2) for blk in range(BLOCKS + 1)]
+        early.extend((blk, b, STEPS[1]) for b in range(2) for blk in range(BLOCKS))
+        first_passes(early)
+        nc.gpsimd.memset(wd_sc[:], 0)
+        for q in (0, 2, 1, 3):
+            load_side_by_side(nc.sync, wd_sc, wd_scales, q)
+        nc.sync.dma_start(out=wd[:], in_=wd_words.bitcast(I32).rearrange("a p c -> p a c"))
+        nc.sync.dma_start(out=weight[:], in_=wgo)
+        first_passes([(blk, b, step) for b in range(2) for step in steps_of(0, b)[2:4] for blk in range(BLOCKS)])
         for c in range(CHUNKS):
-            ahead = 2 * c + 2
-            steps = STEPS
-            begun, before_turn = {0: (2, 3), 1: (0, 1)}.get(c, (0, 3))
-            if c < last:
-                first_product(ahead, 0, steps[begun:before_turn])
-            for b in range(2):
-                turn(c, b, banks[(6 if c == 0 else 4) + b])
-            if c == 0:
+            blocks_ahead = range((c + 1) * BLOCKS, (c + 2) * BLOCKS) if c < last else ()
+            ahead = [(blk, b, step) for blk in blocks_ahead for b in range(2) for step in steps_of(blk, b)]
+            ahead = [one for one in ahead if one not in early]
+            to_turn, to_late_tiles, to_early_tiles = CUTS[c]
+            first_passes(ahead[0:to_turn])
+            if c > 0:
+                for b in range(2):
+                    turn(c, b, banks[4 + b])
+                quantise(c, slice(0, 2))
+            else:
+                turn(c, 0, banks[6])
+                turn(c, 1, banks[7], range(0, 1))
+                turn(c, 1, banks[0], range(1, 2))
                 gather_scales(dst_sc[1], dst_list, 4, 4)
                 move_plane(nc.sync, 1)
-            if c == 0:
                 quantise(c, slice(0, 1))
                 quantise(c, slice(1, 2))
                 gather_scales(src_sc[1], src_list, 4, 4)
-            else:
-                quantise(c, slice(0, 2))
-            if c < last:
-                first_product(ahead, 0, steps[before_turn:4], closes=True)
-                first_product(ahead, 1, steps[begun:2])
+                gather_words(0, 6, 2)
+            first_passes(ahead[to_turn:to_late_tiles])
             if c > 0:
                 second_product(c - 1, (2, 3), (banks[4][:, 0:CHUNK], banks[4][:, CHUNK:BANK]))
-            if c < last:
-                first_product(ahead, 1, steps[2:4], closes=True)
-                whole_half(ahead + 1, 0)
-            if c == 0:
-                first_product(ahead + 1, 1, steps[0:2])
+            first_passes(ahead[to_late_tiles:to_early_tiles])
             second_product(c, (0, 1), (banks[6][:, 0:CHUNK], banks[7][:, 0:CHUNK]))
-            if c == 0:
-                first_product(ahead + 1, 1, steps[2:4], closes=True)
-            elif c < last:
-                whole_half(ahead + 1, 1)
+            first_passes(ahead[to_early_tiles:])
         second_product(last, (2, 3), (banks[0][:, 0:CHUNK], banks[1][:, 0:CHUNK]))
 
         order = [(c, t, 1) for c in range(CHUNKS) for t in range(N_TILES) if c < last - 1 or t < N_TILES - 1]

@@ -25,7 +25,7 @@ ALIGN = 64
 PIECE = 512
 PAD = 16
 STEPS = (0, 2, 3, 1)
-CUTS = ((2, 2, 10), (1, 4, 12), (3, 6, 12), (0, 0, 0))
+CUTS = ((2, 2, 10), (3, 6, 12), (3, 6, 12), (0, 0, 0))
 
 
 def tile_list_msg_none_none_kernel(
@@ -45,7 +45,7 @@ def tile_list_msg_none_none_kernel(
         wt = [keep.tile([P, R // 2], I32, name="wt%d" % a, align_bytes=ALIGN) for a in range(2)]
         wt_sc = keep.tile([P, 2, R // 4], I32, align_bytes=ALIGN)
         ws_sc = keep.tile([P, R // 4], I32, align_bytes=ALIGN)
-        wd_sc = shared.tile([P, 2, N // 4], I32, name="wd_sc", offset=10240 + 512, align_bytes=ALIGN)
+        wd_sc = keep.tile([P, 2, N // 4], I32, align_bytes=ALIGN)
         src_sc = [
             keep.tile([P, J // 2], U8, name="src_sc0", align_bytes=ALIGN),
             shared.tile([P, J // 2], U8, name="src_sc1", offset=0, align_bytes=ALIGN),
@@ -55,8 +55,8 @@ def tile_list_msg_none_none_kernel(
             shared.tile([P, J // 2], U8, name="dst_sc1", offset=4096, align_bytes=ALIGN),
         ]
         moved_sc = [keep.tile([P, J // 8], I32, name="moved_sc%d" % half, align_bytes=ALIGN) for half in range(2)]
-        wd = shared.tile([P, 2, N // 2], I32, name="wd", offset=10240 - 1536, align_bytes=ALIGN)
-        weight = shared.tile([P, J], F32, name="weight", offset=10240 + 1536, align_bytes=ALIGN)
+        wd = shared.tile([P, 2, N // 2], I32, name="wd", offset=10240 - 1024, align_bytes=ALIGN)
+        weight = shared.tile([P, J], F32, name="weight", offset=10240 + 1024, align_bytes=ALIGN)
         reused = {(0, 0): 4096, (0, 1): 5120, (1, 1): 6144, (2, 0): 5120, (2, 1): 6144}
         h_rows = [
             [
@@ -152,7 +152,7 @@ def tile_list_msg_none_none_kernel(
             if b == 1 and blk < BLOCKS:
                 return (0, 2, 1, 3)
             if blk == BLOCKS:
-                return (0, 1, 2, 3)
+                return (0, 2, 1, 3)
             return STEPS
 
         def first_passes(passes):
@@ -233,6 +233,7 @@ def tile_list_msg_none_none_kernel(
         make_identity(nc, ident_made[:])
         nc.scalar.copy(out=ident[:], in_=ident_made[:])
         nc.gpsimd.memset(moved_sc[1][:], 0)
+        nc.gpsimd.memset(wd_sc[:], 0)
         for t in range(1, N_TILES):
             for col in range(0, T, PIECE):
                 nc.gpsimd.memset(placed[t][:, col : col + PIECE].bitcast(I32), 0)
@@ -255,10 +256,8 @@ def tile_list_msg_none_none_kernel(
         gather_words(3, 3, 5)
         gather_words(1, 3, 5)
 
-        early = [(blk, b, STEPS[0]) for b in range(2) for blk in range(BLOCKS + 1)]
-        early.extend((blk, b, STEPS[1]) for b in range(2) for blk in range(BLOCKS))
+        early = [(blk, b, step) for step in STEPS[0:2] for b in range(2) for blk in range(BLOCKS + 1)]
         first_passes(early)
-        nc.gpsimd.memset(wd_sc[:], 0)
         for q in (0, 2, 1, 3):
             load_side_by_side(nc.sync, wd_sc, wd_scales, q)
         nc.sync.dma_start(out=wd[:], in_=wd_words.bitcast(I32).rearrange("a p c -> p a c"))
@@ -273,7 +272,8 @@ def tile_list_msg_none_none_kernel(
             if c > 0:
                 for b in range(2):
                     turn(c, b, banks[4 + b])
-                quantise(c, slice(0, 2))
+                quantise(c, slice(0, 1))
+                quantise(c, slice(1, 2))
             else:
                 turn(c, 0, banks[6])
                 turn(c, 1, banks[7], range(0, 1))

@@ -23,6 +23,7 @@ BLOCKS = CHUNK // P
 N_TILES = N // P
 ALIGN = 64
 PIECE = 512
+SC_FIRST = 5
 PAD = 16
 STEPS = (0, 2, 3, 1)
 CUTS = ((2, 2, 10), (3, 6, 12), (3, 6, 12), (0, 0, 0))
@@ -47,14 +48,17 @@ def tile_list_msg_none_none_kernel(
         ws_sc = keep.tile([P, R // 4], I32, align_bytes=ALIGN)
         wd_sc = keep.tile([P, 2, N // 4], I32, align_bytes=ALIGN)
         src_sc = [
-            keep.tile([P, J // 2], U8, name="src_sc0", align_bytes=ALIGN),
-            shared.tile([P, J // 2], U8, name="src_sc1", offset=0, align_bytes=ALIGN),
+            keep.tile([P, SC_FIRST * P], U8, name="src_sc0", align_bytes=ALIGN),
+            shared.tile([P, J - SC_FIRST * P], U8, name="src_sc1", offset=0, align_bytes=ALIGN),
         ]
         dst_sc = [
-            keep.tile([P, J // 2], U8, name="dst_sc0", align_bytes=ALIGN),
-            shared.tile([P, J // 2], U8, name="dst_sc1", offset=4096, align_bytes=ALIGN),
+            keep.tile([P, SC_FIRST * P], U8, name="dst_sc0", align_bytes=ALIGN),
+            shared.tile([P, J - SC_FIRST * P], U8, name="dst_sc1", offset=4096, align_bytes=ALIGN),
         ]
-        moved_sc = [keep.tile([P, J // 8], I32, name="moved_sc%d" % half, align_bytes=ALIGN) for half in range(2)]
+        moved_sc = [
+            keep.tile([P, part.shape[1] // 4], I32, name="moved_sc%d" % i, align_bytes=ALIGN)
+            for i, part in enumerate(dst_sc)
+        ]
         wd = shared.tile([P, 2, N // 2], I32, name="wd", offset=10240 - 1024, align_bytes=ALIGN)
         weight = shared.tile([P, J], F32, name="weight", offset=10240 + 1024, align_bytes=ALIGN)
         reused = {(0, 0): 4096, (0, 1): 5120, (1, 1): 6144, (2, 0): 5120, (2, 1): 6144}
@@ -110,8 +114,10 @@ def tile_list_msg_none_none_kernel(
         nc.sync.dma_start(out=ws[0][0][:], in_=words8(ws_words, 0)[:, 0:BANK])
         for q in (0, 2, 1, 3):
             load_packed(nc.sync, tab_sc, 0, tab_scales, q)
+        for q in (0, 2):
+            load_side_by_side(nc.sync, wt_sc, wt_scales, q)
         nc.sync.dma_start(out=tab[:, 0:T], in_=words8(tab_words, 0))
-        for q in (0, 2, 1, 3):
+        for q in (1, 3):
             load_side_by_side(nc.sync, wt_sc, wt_scales, q)
         nc.sync.dma_start(out=wt[0][:], in_=wt_words[0].bitcast(I32))
         nc.sync.dma_start(out=tab[:, T : 2 * T], in_=words8(tab_words, 1))
@@ -157,15 +163,16 @@ def tile_list_msg_none_none_kernel(
 
         def first_passes(passes):
             for blk, b, step in passes:
-                within = slice(blk % 4 * P, (blk % 4 + 1) * P)
+                part, at = (0, blk) if blk < SC_FIRST else (1, blk - SC_FIRST)
+                within = slice(at * P, (at + 1) * P)
                 acc = banks[2 * (2 if blk == BLOCKS else blk % 2) + b]
                 a = step % 2
                 if step < 2:
-                    lhsT_scale = dst_sc[blk // 4][:, within] if a == 0 else moved_sc[blk // 4][:].bitcast(U8)[:, within]
+                    lhsT_scale = dst_sc[part][:, within] if a == 0 else moved_sc[part][:].bitcast(U8)[:, within]
                     rhs = wt[a][:].bitcast(U8)[:, 2 * BANK * b : 2 * BANK * (b + 1)].bitcast(FP4X4)
                     rhs_scale = wt_sc[:, a, :].bitcast(U8)[:, BANK * b : BANK * (b + 1)]
                 else:
-                    lhsT_scale = src_sc[blk // 4][4 * a : P, within]
+                    lhsT_scale = src_sc[part][4 * a : P, within]
                     rhs = ws[a][b][:].bitcast(FP8X4)
                     rhs_scale = ws_sc[:].bitcast(U8)[8 + 4 * a : P, BANK * b : BANK * (b + 1)]
                 nc.tensor.matmul_mx(
@@ -227,9 +234,9 @@ def tile_list_msg_none_none_kernel(
                 out=moved_sc[half][0:112, :], in_=dst_sc[half][4:116, :].bitcast(I32)
             )
 
-        gather_scales(dst_sc[0], dst_list, 0, 4)
+        gather_scales(dst_sc[0], dst_list, 0, SC_FIRST)
         move_plane(nc.gpsimd, 0)
-        gather_scales(src_sc[0], src_list, 0, 4)
+        gather_scales(src_sc[0], src_list, 0, SC_FIRST)
         make_identity(nc, ident_made[:])
         nc.scalar.copy(out=ident[:], in_=ident_made[:])
         nc.gpsimd.memset(moved_sc[1][:], 0)
@@ -278,11 +285,11 @@ def tile_list_msg_none_none_kernel(
                 turn(c, 0, banks[6])
                 turn(c, 1, banks[7], range(0, 1))
                 turn(c, 1, banks[0], range(1, 2))
-                gather_scales(dst_sc[1], dst_list, 4, 4)
+                gather_scales(dst_sc[1], dst_list, SC_FIRST, 8 - SC_FIRST)
                 move_plane(nc.sync, 1)
                 quantise(c, slice(0, 1))
                 quantise(c, slice(1, 2))
-                gather_scales(src_sc[1], src_list, 4, 4)
+                gather_scales(src_sc[1], src_list, SC_FIRST, 8 - SC_FIRST)
                 gather_words(0, 6, 2)
             first_passes(ahead[to_turn:to_late_tiles])
             if c > 0:

@@ -1,7 +1,6 @@
 from contextlib import ExitStack
 
 import concourse.mybir as mybir
-from concourse.masks import make_identity
 
 K, R, N, T, J = 1024, 1024, 512, 2048, 1024
 FLOPS = 2 * (2 * K * R * J + R * N * J)
@@ -19,77 +18,76 @@ P = 128
 BANK = 512
 CHUNK = 256
 CHUNKS = J // CHUNK
-BLOCKS = CHUNK // P
 N_TILES = N // P
 ALIGN = 64
 PIECE = 512
-SC_FIRST = 5
-PAD = 16
-STEPS = (0, 2, 3, 1)
-CUTS = ((2, 2, 10), (3, 6, 12), (3, 6, 12), (0, 0, 0))
+RING = 7
+LATE = (0, 3)
 
 
 def tile_list_msg_none_none_kernel(
     tc, tab_words, tab_scales, ws_words, ws_scales, wt_words, wt_scales, wd_words, wd_scales, wgo, offs, offs2, out
 ):
     nc = tc.nc
+    last = CHUNKS - 1
     with ExitStack() as ctx:
         keep = ctx.enter_context(tc.tile_pool(name="keep", bufs=1))
         shared = ctx.enter_context(tc.tile_pool(name="shared", bufs=1))
         psum = ctx.enter_context(tc.psum_pool(name="psum", bufs=1))
 
+        def kept(name, shape, dtype):
+            return keep.tile(shape, dtype, name=name, align_bytes=ALIGN)
+
         src_list = keep.tile([P, J // 16], U16)
         dst_list = keep.tile([P, J // 16], U16)
-        tab = keep.tile([P, 2 * T], I32, align_bytes=ALIGN)
-        tab_sc = keep.tile([P, T // 4], I32, align_bytes=ALIGN)
-        ws = [[keep.tile([P, BANK], I32, name="ws%d%d" % (a, b), align_bytes=ALIGN) for b in range(2)] for a in range(2)]
-        wt = [keep.tile([P, R // 2], I32, name="wt%d" % a, align_bytes=ALIGN) for a in range(2)]
-        wt_sc = keep.tile([P, 2, R // 4], I32, align_bytes=ALIGN)
-        ws_sc = keep.tile([P, R // 4], I32, align_bytes=ALIGN)
-        wd_sc = keep.tile([P, 2, N // 4], I32, align_bytes=ALIGN)
-        src_sc = [
-            keep.tile([P, SC_FIRST * P], U8, name="src_sc0", align_bytes=ALIGN),
-            shared.tile([P, J - SC_FIRST * P], U8, name="src_sc1", offset=0, align_bytes=ALIGN),
+        tab = kept("tab", [P, 2 * T], I32)
+        tab_sc = kept("tab_sc", [P, T // 4], I32)
+        ws_in = [
+            shared.tile([P, 2 * BANK], I32, name="ws_in0", offset=12288, align_bytes=ALIGN),
+            kept("ws_in1", [P, 2 * BANK], I32),
         ]
+        wt_in = [
+            shared.tile([P, R // 2], I32, name="wt_in0", offset=6144, align_bytes=ALIGN),
+            kept("wt_in1", [P, R // 2], I32),
+        ]
+        w_sc_in = shared.tile([P, 2 * R // 4], I32, name="w_sc_in", offset=16384 + 7168, align_bytes=ALIGN)
+        ws = [[kept("ws%d%d" % (a, b), [P, BANK], U32) for b in range(2)] for a in range(2)]
+        wt = [[kept("wt%d%d" % (a, b), [P, BANK], U16) for b in range(2)] for a in range(2)]
+        w_sc = [kept("w_sc%d" % a, [P, R], U8) for a in range(2)]
+        wd = shared.tile([P, 2, N // 2], I32, name="wd", offset=6144 - 1024, align_bytes=ALIGN)
+        wd_sc = shared.tile([P, 2, N // 4], I32, name="wd_sc", offset=12288, align_bytes=ALIGN)
+        weight = shared.tile([P, J], F32, name="weight", offset=6144 + 1024, align_bytes=ALIGN)
+        src_sc = kept("src_sc", [P, J], U8)
         dst_sc = [
-            keep.tile([P, SC_FIRST * P], U8, name="dst_sc0", align_bytes=ALIGN),
-            shared.tile([P, J - SC_FIRST * P], U8, name="dst_sc1", offset=4096, align_bytes=ALIGN),
+            kept("dst_sc0", [P, J // 2], U8),
+            shared.tile([P, J // 2], U8, name="dst_sc1", offset=0, align_bytes=ALIGN),
         ]
-        moved_sc = [
-            keep.tile([P, part.shape[1] // 4], I32, name="moved_sc%d" % i, align_bytes=ALIGN)
-            for i, part in enumerate(dst_sc)
+        moved_sc = [kept("moved_sc%d" % i, [P, J // 8], I32) for i in range(2)]
+        early = [kept("early%d" % s, [P, last * CHUNK if s in LATE else J], U32) for s in range(4)]
+        late = {
+            s: shared.tile([P, CHUNK], U32, name="late%d" % s, offset=2048 + 1024 * i, align_bytes=ALIGN)
+            for i, s in enumerate(LATE)
+        }
+        grouped0 = [
+            shared.tile([P, CHUNK * 4], BF16, name="grouped0%d" % b, offset=2048 * b, align_bytes=ALIGN)
+            for b in range(2)
         ]
-        wd = shared.tile([P, 2, N // 2], I32, name="wd", offset=10240 - 1024, align_bytes=ALIGN)
-        weight = shared.tile([P, J], F32, name="weight", offset=10240 + 1024, align_bytes=ALIGN)
-        reused = {(0, 0): 4096, (0, 1): 5120, (1, 1): 6144, (2, 0): 5120, (2, 1): 6144}
-        h_rows = [
-            [
-                shared.tile([P, BANK], BF16, name="h_rows%d%d" % (blk, b), offset=reused[blk, b])
-                if (blk, b) in reused
-                else keep.tile([P, BANK], BF16, name="h_rows%d%d" % (blk, b))
-                for b in range(2)
-            ]
-            for blk in range(CHUNKS * BLOCKS)
-        ]
-        grouped = [keep.tile([P, 2, CHUNK, 2], F32, name="grouped%d" % c, align_bytes=ALIGN) for c in range(1, CHUNKS)]
-        grouped.insert(0, shared.tile([P, 2, CHUNK, 2], F32, name="grouped0", offset=0, align_bytes=ALIGN))
-        late = shared.tile([P, CHUNK], U32, name="late", offset=1024, align_bytes=ALIGN)
-        h_codes = keep.tile([P, CHUNKS, 2, CHUNK], U32, align_bytes=ALIGN)
-        h_sc = keep.tile([P, CHUNKS, 2, CHUNK], U8, align_bytes=ALIGN)
+        grouped = [None] + [kept("grouped%d" % c, [P, 2 * CHUNK * 4], BF16) for c in range(1, CHUNKS)]
+        h_codes = [kept("h_codes%d" % c, [P, 2 * CHUNK], U32) for c in range(CHUNKS)]
+        h_sc = [kept("h_sc%d" % c, [P, 2 * CHUNK], U8) for c in range(CHUNKS)]
         banks = [psum.tile([P, BANK], F32, name="bank%d" % i) for i in range(8)]
-        ident = keep.tile([P, P], F32)
-        ident_made = keep.tile([P, P], F32)
-        y_sb = [keep.tile([P, J], F32, name="y%d" % t) for t in range(N_TILES)]
-        placed = [keep.tile([P, T], F32, name="placed%d" % t) for t in range(N_TILES)]
+        y_sb = [kept("y%d" % t, [P, J], F32) for t in range(N_TILES)]
+        placed = [kept("placed%d" % t, [P, T], F32) for t in range(2)] + [
+            shared.tile([P, T], F32, name="placed%d" % t, offset=16384 + 8192 * (t - 2), align_bytes=ALIGN)
+            for t in (2, 3)
+        ]
 
-        def load_packed(queue, plane, first, scales, q):
-            queue.dma_start(
-                out=plane[32 * q + first : 32 * q + first + 8, :], in_=scales.bitcast(I32)[:, 4 * q : 4 * q + 4, :]
-            )
+        def load_packed(queue, plane, scales, q):
+            queue.dma_start(out=plane[32 * q : 32 * q + 8, :], in_=scales.bitcast(I32)[:, 4 * q : 4 * q + 4, :])
 
-        def load_side_by_side(queue, plane, scales, q):
+        def load_side_by_side(queue, plane, first, scales, q):
             queue.dma_start(
-                out=plane[32 * q : 32 * q + 4, :, :],
+                out=plane[32 * q + first : 32 * q + first + 4, :, :],
                 in_=scales.bitcast(I32)[:, 4 * q : 4 * q + 4, :].rearrange("a r n -> r a n"),
             )
 
@@ -101,210 +99,197 @@ def tile_list_msg_none_none_kernel(
             nc.vector.memset(words[:, 0 : width // 2 + 1], 0)
             nc.vector.memset(words[:, width // 2 + 1 : width], 0)
 
+        w_sc_rows = w_sc_in[:].rearrange("p (a n) -> p a n", a=2)
         nc.gpsimd.memset(tab_sc[:], 0)
-        clear_on_vector(ws_sc[:])
-        for q in (0, 2):
-            load_packed(nc.gpsimd, ws_sc, 8, ws_scales, q)
-        clear_on_vector(wt_sc[:].rearrange("p a n -> p (a n)"))
+        clear_on_vector(w_sc_in[:])
         clear_on_vector(moved_sc[0][:])
         clear_on_vector(placed[0][:].bitcast(I32))
 
         nc.sync.dma_start(dst_list[:], offs2)
         nc.sync.dma_start(src_list[:], offs)
-        nc.sync.dma_start(out=ws[0][0][:], in_=words8(ws_words, 0)[:, 0:BANK])
+        nc.sync.dma_start(out=wt_in[0][:], in_=wt_words[0].bitcast(I32))
         for q in (0, 2, 1, 3):
-            load_packed(nc.sync, tab_sc, 0, tab_scales, q)
+            load_packed(nc.sync, tab_sc, tab_scales, q)
         for q in (0, 2):
-            load_side_by_side(nc.sync, wt_sc, wt_scales, q)
+            load_side_by_side(nc.sync, w_sc_rows, 0, wt_scales, q)
         nc.sync.dma_start(out=tab[:, 0:T], in_=words8(tab_words, 0))
         for q in (1, 3):
-            load_side_by_side(nc.sync, wt_sc, wt_scales, q)
-        nc.sync.dma_start(out=wt[0][:], in_=wt_words[0].bitcast(I32))
+            load_side_by_side(nc.sync, w_sc_rows, 0, wt_scales, q)
+        for q in (0, 2, 1, 3):
+            load_side_by_side(nc.sync, w_sc_rows, 4, ws_scales, q)
         nc.sync.dma_start(out=tab[:, T : 2 * T], in_=words8(tab_words, 1))
-        for q in (1, 3):
-            load_packed(nc.sync, ws_sc, 8, ws_scales, q)
-        nc.sync.dma_start(out=ws[0][1][:], in_=words8(ws_words, 0)[:, BANK:R])
-        nc.sync.dma_start(out=ws[1][0][:], in_=words8(ws_words, 1)[:, 0:BANK])
-        nc.sync.dma_start(out=wt[1][:], in_=wt_words[1].bitcast(I32))
-        nc.sync.dma_start(out=ws[1][1][:], in_=words8(ws_words, 1)[:, BANK:R])
+        nc.sync.dma_start(out=wt_in[1][:], in_=wt_words[1].bitcast(I32))
+        ws_rows = ws_words.rearrange("a p c i -> p a (c i)").bitcast(I32)
+        for b in range(2):
+            nc.sync.dma_start(
+                out=ws_in[b][:].rearrange("p (a c) -> p a c", a=2), in_=ws_rows[:, :, b * BANK : (b + 1) * BANK]
+            )
 
-        last = CHUNKS - 1
-        picked = {}
+        def deal(dealt, columns, run):
+            nc.scalar.copy(
+                out=dealt.rearrange("p (i g m) -> p g i m", i=4, m=run),
+                in_=columns.rearrange("p (g m i) -> p g i m", i=4, m=run),
+            )
 
         def listed(offsets, first, count):
-            return offsets[:, first * P // 16 : (first + count) * P // 16]
+            return offsets[:, first * CHUNK // 16 : (first + count) * CHUNK // 16]
 
-        def gather_words(step, first, count, spare=0):
-            offsets = dst_list if step < 2 else src_list
-            a = step % 2
-            if count % 2:
-                shape, name = [P, count, P + PAD], "picked%d%d" % (step, first)
-                if (step, first) == (0, 0):
-                    rows = shared.tile(shape, U32, name=name, offset=10240, align_bytes=ALIGN)
+        def picked(s, first, count=1):
+            if first == last and s in LATE:
+                return late[s][:]
+            return early[s][:, first * CHUNK : (first + count) * CHUNK]
+
+        def gather_words(s, first, count, spare=0):
+            offsets = src_list if s // 2 else dst_list
+            window = tab[:, s % 2 * T : (s % 2 + 1) * T + spare]
+            nc.vector.tensor_copy(picked(s, first, count), window.bitcast(U32).indirect(listed(offsets, first, count)))
+
+        def gather_scales(plane, offsets):
+            nc.vector.tensor_copy(plane[:], tab_sc[:].bitcast(U8).indirect(offsets))
+
+        def ring_bank(c, b, pair):
+            return banks[(4 * max(c - 1, 0) + 2 * b + pair) % RING]
+
+        def first_pass(c, b, pair, s):
+            a = s % 2
+            acc = ring_bank(c, b, pair)
+            slots = 4 if c == 0 else 2
+            width = BANK // slots
+            edges = slice(pair * width, (pair + 1) * width) if c == 0 else slice(0, CHUNK)
+            within = slice(c * CHUNK + edges.start, c * CHUNK + edges.stop)
+            for e in range(slots):
+                i = e if c == 0 else 2 * pair + e
+                cols = slice(i * P, (i + 1) * P)
+                sc_cols = slice(b * BANK + i * P, b * BANK + (i + 1) * P)
+                if s // 2:
+                    lhsT = ws[a][b][:, cols].bitcast(FP8X4)
+                    lhsT_scale = w_sc[a][4:P, sc_cols]
+                    rhs_scale = src_sc[4 * a : P, within]
                 else:
-                    rows = keep.tile(shape, U32, name=name, align_bytes=ALIGN)
-                target = rows[:, :, 0:P]
-                for i in range(count):
-                    picked[step, first + i] = rows[:, i, 0:P]
-            else:
-                target = late[:]
-                for i in range(count):
-                    picked[step, first + i] = target[:, i * P : (i + 1) * P]
-            nc.vector.tensor_copy(
-                target, tab[:, a * T : (a + 1) * T + spare].bitcast(U32).indirect(listed(offsets, first, count))
-            )
-
-        def steps_of(blk, b):
-            if b == 1 and blk < BLOCKS:
-                return (0, 2, 1, 3)
-            if blk == BLOCKS:
-                return (0, 2, 1, 3)
-            return STEPS
-
-        def first_passes(passes):
-            for blk, b, step in passes:
-                part, at = (0, blk) if blk < SC_FIRST else (1, blk - SC_FIRST)
-                within = slice(at * P, (at + 1) * P)
-                acc = banks[2 * (2 if blk == BLOCKS else blk % 2) + b]
-                a = step % 2
-                if step < 2:
-                    lhsT_scale = dst_sc[part][:, within] if a == 0 else moved_sc[part][:].bitcast(U8)[:, within]
-                    rhs = wt[a][:].bitcast(U8)[:, 2 * BANK * b : 2 * BANK * (b + 1)].bitcast(FP4X4)
-                    rhs_scale = wt_sc[:, a, :].bitcast(U8)[:, BANK * b : BANK * (b + 1)]
-                else:
-                    lhsT_scale = src_sc[part][4 * a : P, within]
-                    rhs = ws[a][b][:].bitcast(FP8X4)
-                    rhs_scale = ws_sc[:].bitcast(U8)[8 + 4 * a : P, BANK * b : BANK * (b + 1)]
+                    lhsT = wt[a][b][:, cols].bitcast(FP4X4)
+                    lhsT_scale = w_sc[a][:, sc_cols]
+                    plane = moved_sc[c // 2][:].bitcast(U8) if a else dst_sc[c // 2][:]
+                    rhs_scale = plane[:, within.start % BANK : within.start % BANK + width]
                 nc.tensor.matmul_mx(
-                    out=acc[:],
-                    lhsT=picked[step, blk].bitcast(FP8X4),
+                    out=acc[:, e * width : (e + 1) * width],
+                    lhsT=lhsT,
                     lhsT_scale=lhsT_scale,
-                    rhs=rhs,
+                    rhs=picked(s, c)[:, edges].bitcast(FP8X4),
                     rhs_scale=rhs_scale,
-                    start=(step == STEPS[0]),
-                    stop=(step == steps_of(blk, b)[-1]),
+                    start=(s == 0 and e == 0),
+                    stop=(s == 3 and e == slots - 1),
                 )
-                if step == steps_of(blk, b)[-1]:
-                    nc.scalar.copy(
-                        out=h_rows[blk][b][:].rearrange("j (u p e) -> j u p e", u=2, e=2),
-                        in_=acc[:].rearrange("j (p u e) -> j u p e", u=2, e=2),
-                    )
+            if s == 3 and c == 0:
+                nc.scalar.copy(
+                    out=grouped0[b][:, pair * BANK : (pair + 1) * BANK].rearrange("p (j i) -> p j i", i=4),
+                    in_=acc[:].rearrange("p (i j) -> p j i", i=4),
+                )
+            elif s == 3:
+                rows = grouped[c][:, b * 4 * CHUNK : (b + 1) * 4 * CHUNK].rearrange("p (j i) -> p j i", i=4)
+                nc.scalar.copy(
+                    out=rows[:, :, 2 * pair : 2 * pair + 2], in_=acc[:].rearrange("p (e j) -> p j e", e=2)
+                )
 
-        def turn(c, b, bank, blocks=range(BLOCKS)):
-            turned = bank[:].rearrange("p (i u j) -> p i u j", i=2, u=2)
-            for i in blocks:
-                words = h_rows[c * BLOCKS + i][b][:].bitcast(F32)
-                for u in range(2):
-                    nc.tensor.transpose(turned[:, i, u, :], words[:, u * P : (u + 1) * P], ident[:])
-            within = slice(blocks.start, blocks.stop)
-            nc.scalar.copy(
-                out=grouped[c][:, b, :, :].rearrange("p (i j) u -> p i j u", i=2)[:, within],
-                in_=turned.rearrange("p i u j -> p i j u")[:, within],
-            )
+        def first_product(c, b):
+            for pair in range(2):
+                for s in range(4):
+                    first_pass(c, b, pair, s)
 
-        def quantise(c, halves):
+        def quantise(c, first, count):
             nc.vector.quantize_mx(
-                out=h_codes[:, c, halves, :].rearrange("p b j -> p (b j)").bitcast(FP8X4),
-                scales=h_sc[:, c, halves, :].rearrange("p b j -> p (b j)"),
-                in_=grouped[c][:, halves, :, :].rearrange("p b j u -> p (b j u)").bitcast(BF16),
+                out=h_codes[c][:, first * CHUNK : (first + count) * CHUNK].bitcast(FP8X4),
+                scales=h_sc[c][:, first * CHUNK : (first + count) * CHUNK],
+                in_=grouped0[first][:] if c == 0 else grouped[c][:],
             )
 
-        def second_product(c, tiles, accs):
-            for t, acc in zip(tiles, accs):
-                for blk in range(BLOCKS):
-                    cols = slice(blk * P, (blk + 1) * P)
-                    for b in range(2):
-                        nc.tensor.matmul_mx(
-                            out=acc[:, cols],
-                            lhsT=wd[:, b, :].bitcast(U8)[:, 2 * P * t : 2 * P * (t + 1)].bitcast(FP4X4),
-                            lhsT_scale=wd_sc[:, b, :].bitcast(U8)[:, P * t : P * (t + 1)],
-                            rhs=h_codes[:, c, b, cols].bitcast(FP8X4),
-                            rhs_scale=h_sc[:, c, b, cols],
-                            start=(b == 0),
-                            stop=(b == 1),
-                        )
-            for t, acc in zip(tiles, accs):
-                nc.scalar.copy(out=y_sb[t][:, c * CHUNK : (c + 1) * CHUNK], in_=acc)
+        def second_product(pieces, bank):
+            for e, (c, t) in enumerate(pieces):
+                for b in range(2):
+                    cols = slice(b * CHUNK, (b + 1) * CHUNK)
+                    nc.tensor.matmul_mx(
+                        out=bank[:, e * CHUNK : (e + 1) * CHUNK],
+                        lhsT=wd[:, b, :].bitcast(U8)[:, 2 * P * t : 2 * P * (t + 1)].bitcast(FP4X4),
+                        lhsT_scale=wd_sc[:, b, :].bitcast(U8)[:, P * t : P * (t + 1)],
+                        rhs=h_codes[c][:, cols].bitcast(FP8X4),
+                        rhs_scale=h_sc[c][:, cols],
+                        start=(b == 0),
+                        stop=(b == 1),
+                    )
+            for e, (c, t) in enumerate(pieces):
+                nc.scalar.copy(out=y_sb[t][:, c * CHUNK : (c + 1) * CHUNK], in_=bank[:, e * CHUNK : (e + 1) * CHUNK])
 
-        def gather_scales(plane, offsets, first, count):
-            nc.vector.tensor_copy(plane[:], tab_sc[:].bitcast(U8).indirect(listed(offsets, first, count)))
+        for a in range(2):
+            for b in range(2):
+                deal(wt[a][b][:], wt_in[a][:].bitcast(U16)[:, b * BANK : (b + 1) * BANK], 8)
+        for b in range(2):
+            for a in range(2):
+                deal(ws[a][b][:], ws_in[b][:].bitcast(U32)[:, a * BANK : (a + 1) * BANK], 4)
+
+        def deal_scales(a):
+            nc.gpsimd.tensor_copy(
+                out=w_sc[a][:].rearrange("p (b i m) -> p b i m", b=2, i=4),
+                in_=w_sc_in[:].bitcast(U8)[:, a * R : (a + 1) * R].rearrange("p (b m i) -> p b i m", b=2, i=4),
+            )
 
         def move_plane(queue, half):
-            queue.dma_start(
-                out=moved_sc[half][0:112, :], in_=dst_sc[half][4:116, :].bitcast(I32)
-            )
+            queue.dma_start(out=moved_sc[half][0:112, :], in_=dst_sc[half][4:116, :].bitcast(I32))
 
-        gather_scales(dst_sc[0], dst_list, 0, SC_FIRST)
+        gather_scales(dst_sc[0], listed(dst_list, 0, 2))
         move_plane(nc.gpsimd, 0)
-        gather_scales(src_sc[0], src_list, 0, SC_FIRST)
-        make_identity(nc, ident_made[:])
-        nc.scalar.copy(out=ident[:], in_=ident_made[:])
+        deal_scales(0)
+        deal_scales(1)
+        gather_scales(src_sc, src_list[:])
+        gather_words(0, 0, 1)
+        gather_words(2, 0, 1)
+        gather_words(0, 1, 2)
+        gather_words(1, 0, 1)
+        gather_words(3, 0, 1)
+        gather_words(1, 1, 3)
+        gather_words(2, 1, 3, spare=8)
+        gather_words(3, 1, 2)
         nc.gpsimd.memset(moved_sc[1][:], 0)
         nc.gpsimd.memset(wd_sc[:], 0)
-        for t in range(1, N_TILES):
+        for t in (1, 2, 3):
             for col in range(0, T, PIECE):
                 nc.gpsimd.memset(placed[t][:, col : col + PIECE].bitcast(I32), 0)
-        for plane in 3 * [tab_sc[:].bitcast(U8)] + 2 * [src_sc[0][:]]:
-            nc.tensor.matmul_mx(
-                out=banks[6][:],
-                lhsT=ws[0][0][:, 0:P].bitcast(FP8X4),
-                lhsT_scale=plane[:, 0:P],
-                rhs=ws[0][0][:].bitcast(FP8X4),
-                rhs_scale=plane[:, 0:BANK],
-                start=True,
-                stop=True,
-            )
-        gather_words(0, 0, 3)
-        gather_words(2, 0, 3)
-        gather_words(0, 3, 3)
-        gather_words(3, 0, 3)
-        gather_words(1, 0, 3)
-        gather_words(2, 3, 5, spare=8)
-        gather_words(3, 3, 5)
-        gather_words(1, 3, 5)
 
-        early = [(blk, b, step) for step in STEPS[0:2] for b in range(2) for blk in range(BLOCKS + 1)]
-        first_passes(early)
         for q in (0, 2, 1, 3):
-            load_side_by_side(nc.sync, wd_sc, wd_scales, q)
+            load_side_by_side(nc.sync, wd_sc, 0, wd_scales, q)
         nc.sync.dma_start(out=wd[:], in_=wd_words.bitcast(I32).rearrange("a p c -> p a c"))
         nc.sync.dma_start(out=weight[:], in_=wgo)
-        first_passes([(blk, b, step) for b in range(2) for step in steps_of(0, b)[2:4] for blk in range(BLOCKS)])
-        for c in range(CHUNKS):
-            blocks_ahead = range((c + 1) * BLOCKS, (c + 2) * BLOCKS) if c < last else ()
-            ahead = [(blk, b, step) for blk in blocks_ahead for b in range(2) for step in steps_of(blk, b)]
-            ahead = [one for one in ahead if one not in early]
-            to_turn, to_late_tiles, to_early_tiles = CUTS[c]
-            first_passes(ahead[0:to_turn])
-            if c > 0:
-                for b in range(2):
-                    turn(c, b, banks[4 + b])
-                quantise(c, slice(0, 1))
-                quantise(c, slice(1, 2))
-            else:
-                turn(c, 0, banks[6])
-                turn(c, 1, banks[7], range(0, 1))
-                turn(c, 1, banks[0], range(1, 2))
-                gather_scales(dst_sc[1], dst_list, SC_FIRST, 8 - SC_FIRST)
-                move_plane(nc.sync, 1)
-                quantise(c, slice(0, 1))
-                quantise(c, slice(1, 2))
-                gather_scales(src_sc[1], src_list, SC_FIRST, 8 - SC_FIRST)
-                gather_words(0, 6, 2)
-            first_passes(ahead[to_turn:to_late_tiles])
-            if c > 0:
-                second_product(c - 1, (2, 3), (banks[4][:, 0:CHUNK], banks[4][:, CHUNK:BANK]))
-            first_passes(ahead[to_late_tiles:to_early_tiles])
-            second_product(c, (0, 1), (banks[6][:, 0:CHUNK], banks[7][:, 0:CHUNK]))
-            first_passes(ahead[to_early_tiles:])
-        second_product(last, (2, 3), (banks[0][:, 0:CHUNK], banks[1][:, 0:CHUNK]))
 
-        order = [(c, t, 1) for c in range(CHUNKS) for t in range(N_TILES) if c < last - 1 or t < N_TILES - 1]
-        order.append((last - 1, N_TILES - 1, 2))
+        for s in range(2):
+            for b in range(2):
+                for pair in range(2):
+                    first_pass(0, b, pair, s)
+        for b in range(2):
+            for s in range(2, 4):
+                for pair in range(2):
+                    first_pass(0, b, pair, s)
+        quantise(0, 0, 1)
+        quantise(0, 1, 1)
+        gather_scales(dst_sc[1], listed(dst_list, 2, 2))
+        move_plane(nc.sync, 1)
+        for s in LATE:
+            gather_words(s, last, 1)
+        for c in range(last):
+            ahead = (0, 1) if c < last - 1 else (0,)
+            behind = (2, 3) if c < last - 1 else (1,)
+            first_product(c + 1, 0)
+            second_product([(c, t) for t in ahead], banks[RING])
+            first_product(c + 1, 1)
+            quantise(c + 1, 0, 2)
+            second_product([(c, t) for t in behind], ring_bank(c + 1, 1, 1))
+        second_product([(last, 0), (last, 1)], banks[RING])
+        for t in (2, 3):
+            second_product([(last - 1, t), (last, t)], banks[t + 3])
+
+        order = [(c, t, 1) for c in range(last - 1) for t in range(N_TILES)]
+        order = order + [(c, t, 1) for c in (last - 1, last) for t in (0, 1)] + [(last - 1, t, 2) for t in (2, 3)]
         for c, t, chunks in order:
             cols = slice(c * CHUNK, (c + chunks) * CHUNK)
             nc.vector.tensor_tensor(
-                placed[t][:].indirect(listed(dst_list, c * BLOCKS, chunks * BLOCKS)),
+                placed[t][:].indirect(listed(dst_list, c, chunks)),
                 y_sb[t][:, cols],
                 weight[:, cols],
                 mybir.AluOpType.mult,

@@ -21,8 +21,9 @@ CHUNKS = J // CHUNK
 N_TILES = N // P
 ALIGN = 64
 PIECE = 512
-RING = 7
-LATE = (0, 3)
+RING = 6
+LATE = (3,)
+AHEAD = (7, 11, 11)
 
 
 def tile_list_msg_none_none_kernel(
@@ -42,21 +43,16 @@ def tile_list_msg_none_none_kernel(
         dst_list = keep.tile([P, J // 16], U16)
         tab = kept("tab", [P, 2 * T], I32)
         tab_sc = kept("tab_sc", [P, T // 4], I32)
-        ws_in = [
-            shared.tile([P, 2 * BANK], I32, name="ws_in0", offset=12288, align_bytes=ALIGN),
-            kept("ws_in1", [P, 2 * BANK], I32),
-        ]
-        wt_in = [
-            shared.tile([P, R // 2], I32, name="wt_in0", offset=6144, align_bytes=ALIGN),
-            kept("wt_in1", [P, R // 2], I32),
-        ]
-        w_sc_in = shared.tile([P, 2 * R // 4], I32, name="w_sc_in", offset=16384 + 7168, align_bytes=ALIGN)
+        ws_in = {(a, b): kept("ws_in%d%d" % (a, b), [P, BANK], I32) for a, b in ((0, 0), (0, 1), (1, 1))}
+        ws_in[1, 0] = shared.tile([P, BANK], I32, name="ws_in10", offset=16384, align_bytes=ALIGN)
+        wt_in = [kept("wt_in%d" % a, [P, R // 2], I32) for a in range(2)]
+        w_sc_in = shared.tile([P, 2 * R // 4], I32, name="w_sc_in", offset=24576, align_bytes=ALIGN)
         ws = [[kept("ws%d%d" % (a, b), [P, BANK], U32) for b in range(2)] for a in range(2)]
         wt = [[kept("wt%d%d" % (a, b), [P, BANK], U16) for b in range(2)] for a in range(2)]
-        w_sc = [kept("w_sc%d" % a, [P, R], U8) for a in range(2)]
-        wd = shared.tile([P, 2, N // 2], I32, name="wd", offset=6144 - 1024, align_bytes=ALIGN)
-        wd_sc = shared.tile([P, 2, N // 4], I32, name="wd_sc", offset=12288, align_bytes=ALIGN)
-        weight = shared.tile([P, J], F32, name="weight", offset=6144 + 1024, align_bytes=ALIGN)
+        w_sc = [[kept("w_sc%d%d" % (a, b), [P, BANK], U8) for b in range(2)] for a in range(2)]
+        wd = shared.tile([P, 2, N // 2], I32, name="wd", offset=16384 - 1024, align_bytes=ALIGN)
+        wd_sc = shared.tile([P, 2, N // 4], I32, name="wd_sc", offset=24576 - 512, align_bytes=ALIGN)
+        weight = shared.tile([P, J], F32, name="weight", offset=16384 + 1024, align_bytes=ALIGN)
         src_sc = kept("src_sc", [P, J], U8)
         dst_sc = [
             kept("dst_sc0", [P, J // 2], U8),
@@ -65,21 +61,18 @@ def tile_list_msg_none_none_kernel(
         moved_sc = [kept("moved_sc%d" % i, [P, J // 8], I32) for i in range(2)]
         early = [kept("early%d" % s, [P, last * CHUNK if s in LATE else J], U32) for s in range(4)]
         late = {
-            s: shared.tile([P, CHUNK], U32, name="late%d" % s, offset=2048 + 1024 * i, align_bytes=ALIGN)
+            s: shared.tile([P, CHUNK], U32, name="late%d" % s, offset=1024 + 1024 * i, align_bytes=ALIGN)
             for i, s in enumerate(LATE)
         }
-        grouped0 = [
-            shared.tile([P, CHUNK * 4], BF16, name="grouped0%d" % b, offset=2048 * b, align_bytes=ALIGN)
-            for b in range(2)
-        ]
-        grouped = [None] + [kept("grouped%d" % c, [P, 2 * CHUNK * 4], BF16) for c in range(1, CHUNKS)]
+        grouped = [shared.tile([P, 2 * CHUNK * 4], BF16, name="grouped0", offset=0, align_bytes=ALIGN)]
+        grouped = grouped + [kept("grouped%d" % c, [P, 2 * CHUNK * 4], BF16) for c in range(1, CHUNKS)]
         h_codes = [kept("h_codes%d" % c, [P, 2 * CHUNK], U32) for c in range(CHUNKS)]
         h_sc = [kept("h_sc%d" % c, [P, 2 * CHUNK], U8) for c in range(CHUNKS)]
         banks = [psum.tile([P, BANK], F32, name="bank%d" % i) for i in range(8)]
         y_sb = [kept("y%d" % t, [P, J], F32) for t in range(N_TILES)]
         placed = [kept("placed%d" % t, [P, T], F32) for t in range(2)] + [
-            shared.tile([P, T], F32, name="placed%d" % t, offset=16384 + 8192 * (t - 2), align_bytes=ALIGN)
-            for t in (2, 3)
+            shared.tile([P, T], F32, name="placed%d" % t, offset=at, align_bytes=ALIGN)
+            for t, at in ((2, 24576 + 1024), (3, 3072))
         ]
 
         def load_packed(queue, plane, scales, q):
@@ -94,36 +87,42 @@ def tile_list_msg_none_none_kernel(
         def words8(w, a):
             return w[a].rearrange("p c i -> p (c i)").bitcast(I32)
 
+        def load_ws(a, b):
+            nc.sync.dma_start(out=ws_in[a, b][:], in_=words8(ws_words, a)[:, b * BANK : (b + 1) * BANK])
+
         def clear_on_vector(words):
             width = words.shape[1]
             nc.vector.memset(words[:, 0 : width // 2 + 1], 0)
             nc.vector.memset(words[:, width // 2 + 1 : width], 0)
 
+        def clear_on_gpsimd(window):
+            for col in range(0, T, PIECE):
+                nc.gpsimd.memset(window[:, col : col + PIECE].bitcast(I32), 0)
+
         w_sc_rows = w_sc_in[:].rearrange("p (a n) -> p a n", a=2)
         nc.gpsimd.memset(tab_sc[:], 0)
         clear_on_vector(w_sc_in[:])
+        load_side_by_side(nc.gpsimd, w_sc_rows, 4, ws_scales, 0)
         clear_on_vector(moved_sc[0][:])
         clear_on_vector(placed[0][:].bitcast(I32))
 
         nc.sync.dma_start(dst_list[:], offs2)
         nc.sync.dma_start(src_list[:], offs)
-        nc.sync.dma_start(out=wt_in[0][:], in_=wt_words[0].bitcast(I32))
-        for q in (0, 2, 1, 3):
+        load_ws(0, 0)
+        for q in (2, 3, 0, 1):
             load_packed(nc.sync, tab_sc, tab_scales, q)
-        for q in (0, 2):
-            load_side_by_side(nc.sync, w_sc_rows, 0, wt_scales, q)
+        nc.sync.dma_start(out=wt_in[0][:], in_=wt_words[0].bitcast(I32))
+        load_side_by_side(nc.sync, w_sc_rows, 0, wt_scales, 0)
         nc.sync.dma_start(out=tab[:, 0:T], in_=words8(tab_words, 0))
-        for q in (1, 3):
+        for q in (2, 1, 3):
             load_side_by_side(nc.sync, w_sc_rows, 0, wt_scales, q)
-        for q in (0, 2, 1, 3):
+        for q in (2, 1, 3):
             load_side_by_side(nc.sync, w_sc_rows, 4, ws_scales, q)
         nc.sync.dma_start(out=tab[:, T : 2 * T], in_=words8(tab_words, 1))
+        load_ws(1, 0)
         nc.sync.dma_start(out=wt_in[1][:], in_=wt_words[1].bitcast(I32))
-        ws_rows = ws_words.rearrange("a p c i -> p a (c i)").bitcast(I32)
-        for b in range(2):
-            nc.sync.dma_start(
-                out=ws_in[b][:].rearrange("p (a c) -> p a c", a=2), in_=ws_rows[:, :, b * BANK : (b + 1) * BANK]
-            )
+        load_ws(0, 1)
+        load_ws(1, 1)
 
         def deal(dealt, columns, run):
             nc.scalar.copy(
@@ -148,9 +147,9 @@ def tile_list_msg_none_none_kernel(
             nc.vector.tensor_copy(plane[:], tab_sc[:].bitcast(U8).indirect(offsets))
 
         def ring_bank(c, b, pair):
-            return banks[(4 * max(c - 1, 0) + 2 * b + pair) % RING]
+            return banks[(4 * c + 2 * (1 - b) + pair) % RING]
 
-        def first_pass(c, b, pair, s):
+        def first_pass(c, b, pair, s, opens, closes):
             a = s % 2
             acc = ring_bank(c, b, pair)
             slots = 4 if c == 0 else 2
@@ -160,14 +159,13 @@ def tile_list_msg_none_none_kernel(
             for e in range(slots):
                 i = e if c == 0 else 2 * pair + e
                 cols = slice(i * P, (i + 1) * P)
-                sc_cols = slice(b * BANK + i * P, b * BANK + (i + 1) * P)
                 if s // 2:
                     lhsT = ws[a][b][:, cols].bitcast(FP8X4)
-                    lhsT_scale = w_sc[a][4:P, sc_cols]
+                    lhsT_scale = w_sc[a][b][4:P, cols]
                     rhs_scale = src_sc[4 * a : P, within]
                 else:
                     lhsT = wt[a][b][:, cols].bitcast(FP4X4)
-                    lhsT_scale = w_sc[a][:, sc_cols]
+                    lhsT_scale = w_sc[a][b][:, cols]
                     plane = moved_sc[c // 2][:].bitcast(U8) if a else dst_sc[c // 2][:]
                     rhs_scale = plane[:, within.start % BANK : within.start % BANK + width]
                 nc.tensor.matmul_mx(
@@ -176,31 +174,27 @@ def tile_list_msg_none_none_kernel(
                     lhsT_scale=lhsT_scale,
                     rhs=picked(s, c)[:, edges].bitcast(FP8X4),
                     rhs_scale=rhs_scale,
-                    start=(s == 0 and e == 0),
-                    stop=(s == 3 and e == slots - 1),
+                    start=(opens and e == 0),
+                    stop=(closes and e == slots - 1),
                 )
-            if s == 3 and c == 0:
+            if closes and c == 0:
+                rows = grouped[0][:, (2 * b + pair) * BANK : (2 * b + pair + 1) * BANK]
                 nc.scalar.copy(
-                    out=grouped0[b][:, pair * BANK : (pair + 1) * BANK].rearrange("p (j i) -> p j i", i=4),
+                    out=rows.rearrange("p (j i) -> p j i", i=4),
                     in_=acc[:].rearrange("p (i j) -> p j i", i=4),
                 )
-            elif s == 3:
+            elif closes:
                 rows = grouped[c][:, b * 4 * CHUNK : (b + 1) * 4 * CHUNK].rearrange("p (j i) -> p j i", i=4)
                 nc.scalar.copy(
                     out=rows[:, :, 2 * pair : 2 * pair + 2], in_=acc[:].rearrange("p (e j) -> p j e", e=2)
                 )
 
-        def first_product(c, b):
-            for pair in range(2):
-                for s in range(4):
-                    first_pass(c, b, pair, s)
+        def first_product(c, steps):
+            for step in steps:
+                first_pass(c, 1 - step // 8, step // 4 % 2, 3 - step % 4, step % 4 == 0, step % 4 == 3)
 
-        def quantise(c, first, count):
-            nc.vector.quantize_mx(
-                out=h_codes[c][:, first * CHUNK : (first + count) * CHUNK].bitcast(FP8X4),
-                scales=h_sc[c][:, first * CHUNK : (first + count) * CHUNK],
-                in_=grouped0[first][:] if c == 0 else grouped[c][:],
-            )
+        def quantise(c):
+            nc.vector.quantize_mx(out=h_codes[c][:].bitcast(FP8X4), scales=h_sc[c][:], in_=grouped[c][:])
 
         def second_product(pieces, bank):
             for e, (c, t) in enumerate(pieces):
@@ -218,18 +212,26 @@ def tile_list_msg_none_none_kernel(
             for e, (c, t) in enumerate(pieces):
                 nc.scalar.copy(out=y_sb[t][:, c * CHUNK : (c + 1) * CHUNK], in_=bank[:, e * CHUNK : (e + 1) * CHUNK])
 
-        for a in range(2):
+        def deal_ws(a, b):
+            deal(ws[a][b][:], ws_in[a, b][:].bitcast(U32), 4)
+
+        def deal_wt(a):
             for b in range(2):
                 deal(wt[a][b][:], wt_in[a][:].bitcast(U16)[:, b * BANK : (b + 1) * BANK], 8)
-        for b in range(2):
-            for a in range(2):
-                deal(ws[a][b][:], ws_in[b][:].bitcast(U32)[:, a * BANK : (a + 1) * BANK], 4)
+
+        deal_ws(0, 0)
+        deal_wt(0)
+        deal_ws(1, 0)
+        deal_wt(1)
+        deal_ws(0, 1)
+        deal_ws(1, 1)
 
         def deal_scales(a):
-            nc.gpsimd.tensor_copy(
-                out=w_sc[a][:].rearrange("p (b i m) -> p b i m", b=2, i=4),
-                in_=w_sc_in[:].bitcast(U8)[:, a * R : (a + 1) * R].rearrange("p (b m i) -> p b i m", b=2, i=4),
-            )
+            for b in range(2):
+                columns = w_sc_in[:].bitcast(U8)[:, a * R + b * BANK : a * R + (b + 1) * BANK]
+                nc.gpsimd.tensor_copy(
+                    out=w_sc[a][b][:].rearrange("p (i m) -> p i m", i=4), in_=columns.rearrange("p (m i) -> p i m", i=4)
+                )
 
         def move_plane(queue, half):
             queue.dma_start(out=moved_sc[half][0:112, :], in_=dst_sc[half][4:116, :].bitcast(I32))
@@ -239,50 +241,58 @@ def tile_list_msg_none_none_kernel(
         deal_scales(0)
         deal_scales(1)
         gather_scales(src_sc, src_list[:])
+        for plane in 2 * [dst_sc[0]] + 3 * [src_sc]:
+            nc.tensor.matmul_mx(
+                out=banks[RING][:],
+                lhsT=ws_in[0, 0][:, 0:P].bitcast(FP8X4),
+                lhsT_scale=plane[:, 0:P],
+                rhs=ws_in[0, 0][:].bitcast(FP8X4),
+                rhs_scale=plane[:, 0:BANK],
+                start=True,
+                stop=True,
+            )
         gather_words(0, 0, 1)
-        gather_words(2, 0, 1)
-        gather_words(0, 1, 2)
-        gather_words(1, 0, 1)
+        gather_words(2, 0, 2)
+        gather_words(0, 1, 1)
         gather_words(3, 0, 1)
-        gather_words(1, 1, 3)
-        gather_words(2, 1, 3, spare=8)
-        gather_words(3, 1, 2)
+        gather_words(1, 0, 2)
+        gather_words(3, 1, 1)
+        gather_words(0, 2, 2, spare=8)
+        gather_words(1, 2, 2)
+        gather_words(2, 2, 2, spare=8)
+        gather_words(3, 2, 1)
         nc.gpsimd.memset(moved_sc[1][:], 0)
         nc.gpsimd.memset(wd_sc[:], 0)
-        for t in (1, 2, 3):
-            for col in range(0, T, PIECE):
-                nc.gpsimd.memset(placed[t][:, col : col + PIECE].bitcast(I32), 0)
+        clear_on_gpsimd(placed[1])
+        clear_on_gpsimd(placed[2])
 
         for q in (0, 2, 1, 3):
             load_side_by_side(nc.sync, wd_sc, 0, wd_scales, q)
         nc.sync.dma_start(out=wd[:], in_=wd_words.bitcast(I32).rearrange("a p c -> p a c"))
         nc.sync.dma_start(out=weight[:], in_=wgo)
 
-        for s in range(2):
-            for b in range(2):
-                for pair in range(2):
-                    first_pass(0, b, pair, s)
-        for b in range(2):
-            for s in range(2, 4):
-                for pair in range(2):
-                    first_pass(0, b, pair, s)
-        quantise(0, 0, 1)
-        quantise(0, 1, 1)
+        for b, s in ((0, 0), (0, 2), (1, 0), (0, 3), (0, 1), (1, 1), (1, 2), (1, 3)):
+            for pair in range(2):
+                first_pass(0, b, pair, s, s == 0, s == (1, 3)[b])
+        quantise(0)
+        clear_on_gpsimd(placed[3])
         gather_scales(dst_sc[1], listed(dst_list, 2, 2))
         move_plane(nc.sync, 1)
         for s in LATE:
             gather_words(s, last, 1)
         for c in range(last):
-            ahead = (0, 1) if c < last - 1 else (0,)
-            behind = (2, 3) if c < last - 1 else (1,)
-            first_product(c + 1, 0)
-            second_product([(c, t) for t in ahead], banks[RING])
-            first_product(c + 1, 1)
-            quantise(c + 1, 0, 2)
-            second_product([(c, t) for t in behind], ring_bank(c + 1, 1, 1))
-        second_product([(last, 0), (last, 1)], banks[RING])
+            ahead = range(0, last - c)
+            behind = range(last - c, N_TILES if c < last - 1 else 2)
+            first_product(c + 1, range(0, AHEAD[c]))
+            for t in ahead:
+                second_product([(c, t)], banks[RING + t % 2])
+            first_product(c + 1, range(AHEAD[c], 16))
+            quantise(c + 1)
+            second_product([(c, t) for t in behind], ring_bank(c + 1, 0, 1))
+        for t in (0, 1):
+            second_product([(last, t)], banks[RING + t])
         for t in (2, 3):
-            second_product([(last - 1, t), (last, t)], banks[t + 3])
+            second_product([(last - 1, t), (last, t)], banks[t + 2])
 
         order = [(c, t, 1) for c in range(last - 1) for t in range(N_TILES)]
         order = order + [(c, t, 1) for c in (last - 1, last) for t in (0, 1)] + [(last - 1, t, 2) for t in (2, 3)]

@@ -22,7 +22,7 @@ N_TILES = N // P
 ALIGN = 64
 PIECE = 512
 RING = 6
-LATE = (3,)
+LATE = (0,)
 AHEAD = (7, 11, 11)
 
 
@@ -109,15 +109,16 @@ def tile_list_msg_none_none_kernel(
         nc.sync.dma_start(dst_list[:], offs2)
         nc.sync.dma_start(src_list[:], offs)
         load_ws(0, 0)
-        for q in (2, 3, 0, 1):
+        for q in (0, 2, 1, 3):
             load_packed(nc.sync, tab_sc, tab_scales, q)
-        nc.sync.dma_start(out=wt_in[0][:], in_=wt_words[0].bitcast(I32))
-        load_side_by_side(nc.sync, w_sc_rows, 0, wt_scales, 0)
+        for q in (0, 2):
+            load_side_by_side(nc.sync, w_sc_rows, 0, wt_scales, q)
         nc.sync.dma_start(out=tab[:, 0:T], in_=words8(tab_words, 0))
-        for q in (2, 1, 3):
+        for q in (1, 3):
             load_side_by_side(nc.sync, w_sc_rows, 0, wt_scales, q)
         for q in (2, 1, 3):
             load_side_by_side(nc.sync, w_sc_rows, 4, ws_scales, q)
+        nc.sync.dma_start(out=wt_in[0][:], in_=wt_words[0].bitcast(I32))
         nc.sync.dma_start(out=tab[:, T : 2 * T], in_=words8(tab_words, 1))
         load_ws(1, 0)
         nc.sync.dma_start(out=wt_in[1][:], in_=wt_words[1].bitcast(I32))
@@ -251,16 +252,16 @@ def tile_list_msg_none_none_kernel(
                 start=True,
                 stop=True,
             )
+        gather_words(2, 0, 1)
         gather_words(0, 0, 1)
-        gather_words(2, 0, 2)
-        gather_words(0, 1, 1)
+        gather_words(2, 1, 1)
+        gather_words(0, 1, 2)
         gather_words(3, 0, 1)
-        gather_words(1, 0, 2)
+        gather_words(1, 0, 1)
         gather_words(3, 1, 1)
-        gather_words(0, 2, 2, spare=8)
-        gather_words(1, 2, 2)
+        gather_words(1, 1, 3)
         gather_words(2, 2, 2, spare=8)
-        gather_words(3, 2, 1)
+        gather_words(3, 2, 2)
         nc.gpsimd.memset(moved_sc[1][:], 0)
         nc.gpsimd.memset(wd_sc[:], 0)
         clear_on_gpsimd(placed[1])
@@ -271,9 +272,9 @@ def tile_list_msg_none_none_kernel(
         nc.sync.dma_start(out=wd[:], in_=wd_words.bitcast(I32).rearrange("a p c -> p a c"))
         nc.sync.dma_start(out=weight[:], in_=wgo)
 
-        for b, s in ((0, 0), (0, 2), (1, 0), (0, 3), (0, 1), (1, 1), (1, 2), (1, 3)):
+        for b, s in ((0, 2), (0, 0), (1, 0), (0, 3), (0, 1), (1, 1), (1, 2), (1, 3)):
             for pair in range(2):
-                first_pass(0, b, pair, s, s == 0, s == (1, 3)[b])
+                first_pass(0, b, pair, s, s == (2, 0)[b], s == (1, 3)[b])
         quantise(0)
         clear_on_gpsimd(placed[3])
         gather_scales(dst_sc[1], listed(dst_list, 2, 2))

@@ -51,7 +51,7 @@ def tile_list_msg_none_none_kernel(
         wt = [[kept("wt%d%d" % (a, b), [P, BANK], U16) for b in range(2)] for a in range(2)]
         w_sc = [[kept("w_sc%d%d" % (a, b), [P, BANK], U8) for b in range(2)] for a in range(2)]
         wd = shared.tile([P, 2, N // 2], I32, name="wd", offset=16384 - 1024, align_bytes=ALIGN)
-        wd_sc = shared.tile([P, 2, N // 4], I32, name="wd_sc", offset=24576 - 512, align_bytes=ALIGN)
+        wd_sc = kept("wd_sc", [P, 2, N // 4], I32)
         weight = shared.tile([P, J], F32, name="weight", offset=16384 + 1024, align_bytes=ALIGN)
         src_sc = kept("src_sc", [P, J], U8)
         dst_sc = [
@@ -90,21 +90,18 @@ def tile_list_msg_none_none_kernel(
         def load_ws(a, b):
             nc.sync.dma_start(out=ws_in[a, b][:], in_=words8(ws_words, a)[:, b * BANK : (b + 1) * BANK])
 
-        def clear_on_vector(words):
-            width = words.shape[1]
-            nc.vector.memset(words[:, 0 : width // 2 + 1], 0)
-            nc.vector.memset(words[:, width // 2 + 1 : width], 0)
-
         def clear_on_gpsimd(window):
             for col in range(0, T, PIECE):
                 nc.gpsimd.memset(window[:, col : col + PIECE].bitcast(I32), 0)
 
         w_sc_rows = w_sc_in[:].rearrange("p (a n) -> p a n", a=2)
         nc.gpsimd.memset(tab_sc[:], 0)
-        clear_on_vector(w_sc_in[:])
+        nc.vector.memset(w_sc_in[:], 0)
         load_side_by_side(nc.gpsimd, w_sc_rows, 4, ws_scales, 0)
-        clear_on_vector(moved_sc[0][:])
-        clear_on_vector(placed[0][:].bitcast(I32))
+        for plane in (moved_sc[0], moved_sc[1], wd_sc):
+            nc.vector.memset(plane[:], 0)
+        for t in range(2):
+            nc.vector.memset(placed[t][:].bitcast(I32), 0)
 
         nc.sync.dma_start(dst_list[:], offs2)
         nc.sync.dma_start(src_list[:], offs)
@@ -262,9 +259,6 @@ def tile_list_msg_none_none_kernel(
         gather_words(1, 1, 3)
         gather_words(2, 2, 2, spare=8)
         gather_words(3, 2, 2)
-        nc.gpsimd.memset(moved_sc[1][:], 0)
-        nc.gpsimd.memset(wd_sc[:], 0)
-        clear_on_gpsimd(placed[1])
         clear_on_gpsimd(placed[2])
 
         for q in (0, 2, 1, 3):

@@ -21,8 +21,8 @@ CHUNKS = J // CHUNK
 N_TILES = N // P
 ALIGN = 64
 PIECE = 512
-RING = 6
-LATE = (0,)
+LATE = (0, 2)
+PAD = 32
 AHEAD = (7, 11, 11)
 
 
@@ -41,12 +41,12 @@ def tile_list_msg_none_none_kernel(
 
         src_list = keep.tile([P, J // 16], U16)
         dst_list = keep.tile([P, J // 16], U16)
-        tab = kept("tab", [P, 2 * T], I32)
+        tab = [kept("tab%d" % a, [P, T], I32) for a in range(2)]
         tab_sc = kept("tab_sc", [P, T // 4], I32)
         ws_in = {(a, b): kept("ws_in%d%d" % (a, b), [P, BANK], I32) for a, b in ((0, 0), (0, 1), (1, 1))}
         ws_in[1, 0] = shared.tile([P, BANK], I32, name="ws_in10", offset=16384, align_bytes=ALIGN)
         wt_in = [kept("wt_in%d" % a, [P, R // 2], I32) for a in range(2)]
-        w_sc_in = shared.tile([P, 2 * R // 4], I32, name="w_sc_in", offset=24576, align_bytes=ALIGN)
+        w_sc_in = shared.tile([P, 2 * R // 4], I32, name="w_sc_in", offset=32768, align_bytes=ALIGN)
         ws = [[kept("ws%d%d" % (a, b), [P, BANK], U32) for b in range(2)] for a in range(2)]
         wt = [[kept("wt%d%d" % (a, b), [P, BANK], U16) for b in range(2)] for a in range(2)]
         w_sc = [[kept("w_sc%d%d" % (a, b), [P, BANK], U8) for b in range(2)] for a in range(2)]
@@ -55,24 +55,28 @@ def tile_list_msg_none_none_kernel(
         weight = shared.tile([P, J], F32, name="weight", offset=16384 + 1024, align_bytes=ALIGN)
         src_sc = kept("src_sc", [P, J], U8)
         dst_sc = [
-            kept("dst_sc0", [P, J // 2], U8),
-            shared.tile([P, J // 2], U8, name="dst_sc1", offset=0, align_bytes=ALIGN),
+            kept("dst_sc0", [P, CHUNK], U8),
+            kept("dst_sc1", [P, CHUNK], U8),
+            shared.tile([P, 2 * CHUNK], U8, name="dst_sc2", offset=0, align_bytes=ALIGN),
         ]
-        moved_sc = [kept("moved_sc%d" % i, [P, J // 8], I32) for i in range(2)]
+        moved_sc = kept("moved_sc", [P, J // 4], I32)
         early = [kept("early%d" % s, [P, last * CHUNK if s in LATE else J], U32) for s in range(4)]
         late = {
-            s: shared.tile([P, CHUNK], U32, name="late%d" % s, offset=1024 + 1024 * i, align_bytes=ALIGN)
+            s: shared.tile([P, CHUNK], U32, name="late%d" % s, offset=2048 + 1024 * i, align_bytes=ALIGN)
             for i, s in enumerate(LATE)
         }
-        grouped = [shared.tile([P, 2 * CHUNK * 4], BF16, name="grouped0", offset=0, align_bytes=ALIGN)]
-        grouped = grouped + [kept("grouped%d" % c, [P, 2 * CHUNK * 4], BF16) for c in range(1, CHUNKS)]
+        first_h = [
+            shared.tile([P, CHUNK * 4 + PAD * b], BF16, name="first_h%d" % b, offset=2048 * b, align_bytes=ALIGN)
+            for b in range(2)
+        ]
+        grouped = {c: kept("grouped%d" % c, [P, 2 * CHUNK * 4], BF16) for c in range(1, CHUNKS)}
         h_codes = [kept("h_codes%d" % c, [P, 2 * CHUNK], U32) for c in range(CHUNKS)]
         h_sc = [kept("h_sc%d" % c, [P, 2 * CHUNK], U8) for c in range(CHUNKS)]
         banks = [psum.tile([P, BANK], F32, name="bank%d" % i) for i in range(8)]
         y_sb = [kept("y%d" % t, [P, J], F32) for t in range(N_TILES)]
-        placed = [kept("placed%d" % t, [P, T], F32) for t in range(2)] + [
+        placed = [kept("placed0", [P, T], F32)] + [
             shared.tile([P, T], F32, name="placed%d" % t, offset=at, align_bytes=ALIGN)
-            for t, at in ((2, 24576 + 1024), (3, 3072))
+            for t, at in ((1, 32768 - 8192 + 64), (2, 32768 + 1024), (3, 4096))
         ]
 
         def load_packed(queue, plane, scales, q):
@@ -90,37 +94,40 @@ def tile_list_msg_none_none_kernel(
         def load_ws(a, b):
             nc.sync.dma_start(out=ws_in[a, b][:], in_=words8(ws_words, a)[:, b * BANK : (b + 1) * BANK])
 
+        def clear_on_vector(words):
+            width = words.shape[1]
+            nc.vector.memset(words[:, 0 : width // 2 + 1], 0)
+            nc.vector.memset(words[:, width // 2 + 1 : width], 0)
+
         def clear_on_gpsimd(window):
             for col in range(0, T, PIECE):
                 nc.gpsimd.memset(window[:, col : col + PIECE].bitcast(I32), 0)
 
         w_sc_rows = w_sc_in[:].rearrange("p (a n) -> p a n", a=2)
         nc.gpsimd.memset(tab_sc[:], 0)
-        nc.vector.memset(w_sc_in[:], 0)
+        nc.gpsimd.memset(wd_sc[:], 0)
+        clear_on_vector(w_sc_in[:])
         load_side_by_side(nc.gpsimd, w_sc_rows, 4, ws_scales, 0)
-        for plane in (moved_sc[0], moved_sc[1], wd_sc):
-            nc.vector.memset(plane[:], 0)
-        for t in range(2):
-            nc.vector.memset(placed[t][:].bitcast(I32), 0)
+        clear_on_vector(moved_sc[:])
+        clear_on_vector(placed[0][:].bitcast(I32))
 
         nc.sync.dma_start(dst_list[:], offs2)
         nc.sync.dma_start(src_list[:], offs)
         load_ws(0, 0)
         for q in (0, 2, 1, 3):
             load_packed(nc.sync, tab_sc, tab_scales, q)
-        for q in (0, 2):
-            load_side_by_side(nc.sync, w_sc_rows, 0, wt_scales, q)
-        nc.sync.dma_start(out=tab[:, 0:T], in_=words8(tab_words, 0))
-        for q in (1, 3):
+        nc.sync.dma_start(out=wt_in[0][:], in_=wt_words[0].bitcast(I32))
+        load_side_by_side(nc.sync, w_sc_rows, 0, wt_scales, 0)
+        nc.sync.dma_start(out=tab[0][:], in_=words8(tab_words, 0))
+        for q in (2, 1, 3):
             load_side_by_side(nc.sync, w_sc_rows, 0, wt_scales, q)
         for q in (2, 1, 3):
             load_side_by_side(nc.sync, w_sc_rows, 4, ws_scales, q)
-        nc.sync.dma_start(out=wt_in[0][:], in_=wt_words[0].bitcast(I32))
-        nc.sync.dma_start(out=tab[:, T : 2 * T], in_=words8(tab_words, 1))
+        nc.sync.dma_start(out=tab[1][:], in_=words8(tab_words, 1))
         load_ws(1, 0)
-        nc.sync.dma_start(out=wt_in[1][:], in_=wt_words[1].bitcast(I32))
         load_ws(0, 1)
         load_ws(1, 1)
+        nc.sync.dma_start(out=wt_in[1][:], in_=wt_words[1].bitcast(I32))
 
         def deal(dealt, columns, run):
             nc.scalar.copy(
@@ -136,20 +143,17 @@ def tile_list_msg_none_none_kernel(
                 return late[s][:]
             return early[s][:, first * CHUNK : (first + count) * CHUNK]
 
-        def gather_words(s, first, count, spare=0):
+        def gather_words(s, first, count):
             offsets = src_list if s // 2 else dst_list
-            window = tab[:, s % 2 * T : (s % 2 + 1) * T + spare]
-            nc.vector.tensor_copy(picked(s, first, count), window.bitcast(U32).indirect(listed(offsets, first, count)))
+            nc.vector.tensor_copy(picked(s, first, count), tab[s % 2][:].bitcast(U32).indirect(listed(offsets, first, count)))
 
         def gather_scales(plane, offsets):
             nc.vector.tensor_copy(plane[:], tab_sc[:].bitcast(U8).indirect(offsets))
 
-        def ring_bank(c, b, pair):
-            return banks[(4 * c + 2 * (1 - b) + pair) % RING]
 
         def first_pass(c, b, pair, s, opens, closes):
             a = s % 2
-            acc = ring_bank(c, b, pair)
+            acc = banks[2 * b + pair]
             slots = 4 if c == 0 else 2
             width = BANK // slots
             edges = slice(pair * width, (pair + 1) * width) if c == 0 else slice(0, CHUNK)
@@ -164,8 +168,8 @@ def tile_list_msg_none_none_kernel(
                 else:
                     lhsT = wt[a][b][:, cols].bitcast(FP4X4)
                     lhsT_scale = w_sc[a][b][:, cols]
-                    plane = moved_sc[c // 2][:].bitcast(U8) if a else dst_sc[c // 2][:]
-                    rhs_scale = plane[:, within.start % BANK : within.start % BANK + width]
+                    at = within.start - min(c, 2) * CHUNK
+                    rhs_scale = moved_sc[:].bitcast(U8)[:, within] if a else dst_sc[min(c, 2)][:, at : at + width]
                 nc.tensor.matmul_mx(
                     out=acc[:, e * width : (e + 1) * width],
                     lhsT=lhsT,
@@ -176,7 +180,7 @@ def tile_list_msg_none_none_kernel(
                     stop=(closes and e == slots - 1),
                 )
             if closes and c == 0:
-                rows = grouped[0][:, (2 * b + pair) * BANK : (2 * b + pair + 1) * BANK]
+                rows = first_h[b][:, pair * BANK : (pair + 1) * BANK]
                 nc.scalar.copy(
                     out=rows.rearrange("p (j i) -> p j i", i=4),
                     in_=acc[:].rearrange("p (i j) -> p j i", i=4),
@@ -189,10 +193,16 @@ def tile_list_msg_none_none_kernel(
 
         def first_product(c, steps):
             for step in steps:
-                first_pass(c, 1 - step // 8, step // 4 % 2, 3 - step % 4, step % 4 == 0, step % 4 == 3)
+                first_pass(c, step // 8, step // 4 % 2, (0, 2, 3, 1)[step % 4], step % 4 == 0, step % 4 == 3)
 
         def quantise(c):
             nc.vector.quantize_mx(out=h_codes[c][:].bitcast(FP8X4), scales=h_sc[c][:], in_=grouped[c][:])
+
+        def quantise_first(b):
+            cols = slice(b * CHUNK, (b + 1) * CHUNK)
+            nc.vector.quantize_mx(
+                out=h_codes[0][:, cols].bitcast(FP8X4), scales=h_sc[0][:, cols], in_=first_h[b][:, 0 : 4 * CHUNK]
+            )
 
         def second_product(pieces, bank):
             for e, (c, t) in enumerate(pieces):
@@ -220,9 +230,9 @@ def tile_list_msg_none_none_kernel(
         deal_ws(0, 0)
         deal_wt(0)
         deal_ws(1, 0)
-        deal_wt(1)
         deal_ws(0, 1)
         deal_ws(1, 1)
+        deal_wt(1)
 
         def deal_scales(a):
             for b in range(2):
@@ -231,17 +241,20 @@ def tile_list_msg_none_none_kernel(
                     out=w_sc[a][b][:].rearrange("p (i m) -> p i m", i=4), in_=columns.rearrange("p (m i) -> p i m", i=4)
                 )
 
-        def move_plane(queue, half):
-            queue.dma_start(out=moved_sc[half][0:112, :], in_=dst_sc[half][4:116, :].bitcast(I32))
+        def move_plane(queue, part):
+            rows = dst_sc[part][4:116, :].bitcast(I32)
+            first = part * CHUNK // 4
+            queue.dma_start(out=moved_sc[0:112, first : first + rows.shape[1]], in_=rows)
 
-        gather_scales(dst_sc[0], listed(dst_list, 0, 2))
-        move_plane(nc.gpsimd, 0)
+        for c in range(2):
+            gather_scales(dst_sc[c], listed(dst_list, c, 1))
+            move_plane(nc.gpsimd, c)
         deal_scales(0)
         deal_scales(1)
         gather_scales(src_sc, src_list[:])
-        for plane in 2 * [dst_sc[0]] + 3 * [src_sc]:
+        for plane in 3 * [src_sc]:
             nc.tensor.matmul_mx(
-                out=banks[RING][:],
+                out=banks[6][:],
                 lhsT=ws_in[0, 0][:, 0:P].bitcast(FP8X4),
                 lhsT_scale=plane[:, 0:P],
                 rhs=ws_in[0, 0][:].bitcast(FP8X4),
@@ -251,14 +264,14 @@ def tile_list_msg_none_none_kernel(
             )
         gather_words(2, 0, 1)
         gather_words(0, 0, 1)
-        gather_words(2, 1, 1)
+        gather_words(2, 1, 2)
         gather_words(0, 1, 2)
         gather_words(3, 0, 1)
         gather_words(1, 0, 1)
         gather_words(3, 1, 1)
         gather_words(1, 1, 3)
-        gather_words(2, 2, 2, spare=8)
         gather_words(3, 2, 2)
+        clear_on_gpsimd(placed[1])
         clear_on_gpsimd(placed[2])
 
         for q in (0, 2, 1, 3):
@@ -266,13 +279,14 @@ def tile_list_msg_none_none_kernel(
         nc.sync.dma_start(out=wd[:], in_=wd_words.bitcast(I32).rearrange("a p c -> p a c"))
         nc.sync.dma_start(out=weight[:], in_=wgo)
 
-        for b, s in ((0, 2), (0, 0), (1, 0), (0, 3), (0, 1), (1, 1), (1, 2), (1, 3)):
+        for b, s in ((0, 2), (0, 0), (1, 0), (0, 3), (1, 2), (1, 3), (0, 1), (1, 1)):
             for pair in range(2):
-                first_pass(0, b, pair, s, s == (2, 0)[b], s == (1, 3)[b])
-        quantise(0)
+                first_pass(0, b, pair, s, s == (2, 0)[b], s == 1)
+        quantise_first(0)
+        gather_scales(dst_sc[2], listed(dst_list, 2, 2))
+        move_plane(nc.sync, 2)
+        quantise_first(1)
         clear_on_gpsimd(placed[3])
-        gather_scales(dst_sc[1], listed(dst_list, 2, 2))
-        move_plane(nc.sync, 1)
         for s in LATE:
             gather_words(s, last, 1)
         for c in range(last):
@@ -280,12 +294,12 @@ def tile_list_msg_none_none_kernel(
             behind = range(last - c, N_TILES if c < last - 1 else 2)
             first_product(c + 1, range(0, AHEAD[c]))
             for t in ahead:
-                second_product([(c, t)], banks[RING + t % 2])
+                second_product([(c, t)], banks[6 + t % 2])
             first_product(c + 1, range(AHEAD[c], 16))
             quantise(c + 1)
-            second_product([(c, t) for t in behind], ring_bank(c + 1, 0, 1))
+            second_product([(c, t) for t in behind], banks[3])
         for t in (0, 1):
-            second_product([(last, t)], banks[RING + t])
+            second_product([(last, t)], banks[6 + t])
         for t in (2, 3):
             second_product([(last - 1, t), (last, t)], banks[t + 2])
 

@@ -116,13 +116,14 @@ def tile_list_msg_none_none_kernel(
         load_ws(0, 0)
         for q in (0, 2, 1, 3):
             load_packed(nc.sync, tab_sc, tab_scales, q)
-        nc.sync.dma_start(out=wt_in[0][:], in_=wt_words[0].bitcast(I32))
-        load_side_by_side(nc.sync, w_sc_rows, 0, wt_scales, 0)
+        for q in (0, 2):
+            load_side_by_side(nc.sync, w_sc_rows, 0, wt_scales, q)
         nc.sync.dma_start(out=tab[0][:], in_=words8(tab_words, 0))
-        for q in (2, 1, 3):
+        for q in (1, 3):
             load_side_by_side(nc.sync, w_sc_rows, 0, wt_scales, q)
         for q in (2, 1, 3):
             load_side_by_side(nc.sync, w_sc_rows, 4, ws_scales, q)
+        nc.sync.dma_start(out=wt_in[0][:], in_=wt_words[0].bitcast(I32))
         nc.sync.dma_start(out=tab[1][:], in_=words8(tab_words, 1))
         load_ws(1, 0)
         load_ws(0, 1)

@@ -21,9 +21,8 @@ CHUNKS = J // CHUNK
 N_TILES = N // P
 ALIGN = 64
 PIECE = 512
-LATE = (0, 2)
 PAD = 32
-AHEAD = (7, 11, 11)
+AHEAD = 11
 
 
 def tile_list_msg_none_none_kernel(
@@ -41,7 +40,7 @@ def tile_list_msg_none_none_kernel(
 
         src_list = keep.tile([P, J // 16], U16)
         dst_list = keep.tile([P, J // 16], U16)
-        tab = [kept("tab%d" % a, [P, T], I32) for a in range(2)]
+        tab = kept("tab", [P, 2 * T], I32)
         tab_sc = kept("tab_sc", [P, T // 4], I32)
         ws_in = {(a, b): kept("ws_in%d%d" % (a, b), [P, BANK], I32) for a, b in ((0, 0), (0, 1), (1, 1))}
         ws_in[1, 0] = shared.tile([P, BANK], I32, name="ws_in10", offset=16384, align_bytes=ALIGN)
@@ -53,17 +52,12 @@ def tile_list_msg_none_none_kernel(
         wd = shared.tile([P, 2, N // 2], I32, name="wd", offset=16384 - 1024, align_bytes=ALIGN)
         wd_sc = kept("wd_sc", [P, 2, N // 4], I32)
         weight = shared.tile([P, J], F32, name="weight", offset=16384 + 1024, align_bytes=ALIGN)
-        src_sc = kept("src_sc", [P, J], U8)
-        dst_sc = [
-            kept("dst_sc0", [P, CHUNK], U8),
-            kept("dst_sc1", [P, CHUNK], U8),
-            shared.tile([P, 2 * CHUNK], U8, name="dst_sc2", offset=0, align_bytes=ALIGN),
-        ]
-        moved_sc = kept("moved_sc", [P, J // 4], I32)
-        early = [kept("early%d" % s, [P, last * CHUNK if s in LATE else J], U32) for s in range(4)]
+        picked_sc = [kept("picked_sc0", [P, 2 * CHUNK], U8), kept("picked_sc1", [P, 2 * last * CHUNK], U8)]
+        moved_sc = [kept("moved_sc%d" % i, [P, part.shape[1] // 4], I32) for i, part in enumerate(picked_sc)]
+        early = [kept("early%d" % s, [P, 2 * CHUNK if s % 2 else J], U32) for s in range(4)]
         late = {
-            s: shared.tile([P, CHUNK], U32, name="late%d" % s, offset=2048 + 1024 * i, align_bytes=ALIGN)
-            for i, s in enumerate(LATE)
+            s: shared.tile([P, 2 * CHUNK], U32, name="late%d" % s, offset=2048 * (s // 2), align_bytes=ALIGN)
+            for s in (1, 3)
         }
         first_h = [
             shared.tile([P, CHUNK * 4 + PAD * b], BF16, name="first_h%d" % b, offset=2048 * b, align_bytes=ALIGN)
@@ -79,14 +73,11 @@ def tile_list_msg_none_none_kernel(
             for t, at in ((1, 32768 - 8192 + 64), (2, 32768 + 1024), (3, 4096))
         ]
 
-        def load_packed(queue, plane, scales, q):
-            queue.dma_start(out=plane[32 * q : 32 * q + 8, :], in_=scales.bitcast(I32)[:, 4 * q : 4 * q + 4, :])
+        def rows_of(scales, r):
+            return scales.bitcast(I32)[:, r:16:4, :].rearrange("a q n -> q a n")
 
-        def load_side_by_side(queue, plane, first, scales, q):
-            queue.dma_start(
-                out=plane[32 * q + first : 32 * q + first + 4, :, :],
-                in_=scales.bitcast(I32)[:, 4 * q : 4 * q + 4, :].rearrange("a r n -> r a n"),
-            )
+        def load_side_by_side(queue, plane, first, scales, r):
+            queue.dma_start(out=plane[first + r : P : 32, :, :], in_=rows_of(scales, r))
 
         def words8(w, a):
             return w[a].rearrange("p c i -> p (c i)").bitcast(I32)
@@ -94,39 +85,35 @@ def tile_list_msg_none_none_kernel(
         def load_ws(a, b):
             nc.sync.dma_start(out=ws_in[a, b][:], in_=words8(ws_words, a)[:, b * BANK : (b + 1) * BANK])
 
-        def clear_on_vector(words):
-            width = words.shape[1]
-            nc.vector.memset(words[:, 0 : width // 2 + 1], 0)
-            nc.vector.memset(words[:, width // 2 + 1 : width], 0)
-
         def clear_on_gpsimd(window):
             for col in range(0, T, PIECE):
                 nc.gpsimd.memset(window[:, col : col + PIECE].bitcast(I32), 0)
 
         w_sc_rows = w_sc_in[:].rearrange("p (a n) -> p a n", a=2)
         nc.gpsimd.memset(tab_sc[:], 0)
-        nc.gpsimd.memset(wd_sc[:], 0)
-        clear_on_vector(w_sc_in[:])
+        nc.vector.memset(w_sc_in[:], 0)
         load_side_by_side(nc.gpsimd, w_sc_rows, 4, ws_scales, 0)
-        clear_on_vector(moved_sc[:])
-        clear_on_vector(placed[0][:].bitcast(I32))
+        for plane in moved_sc + [wd_sc]:
+            nc.vector.memset(plane[:], 0)
+        for cols in (slice(0, T // 2 + 1), slice(T // 2 + 1, T)):
+            nc.vector.memset(placed[0][:, cols].bitcast(I32), 0)
 
         nc.sync.dma_start(dst_list[:], offs2)
         nc.sync.dma_start(src_list[:], offs)
         load_ws(0, 0)
-        for q in (0, 2, 1, 3):
-            load_packed(nc.sync, tab_sc, tab_scales, q)
+        for r in range(4):
+            nc.sync.dma_start(out=tab_sc[r:P:16, :], in_=rows_of(tab_scales, r))
         for q in (0, 2):
             load_side_by_side(nc.sync, w_sc_rows, 0, wt_scales, q)
-        nc.sync.dma_start(out=tab[0][:], in_=words8(tab_words, 0))
+        nc.sync.dma_start(out=tab[:, 0:T], in_=words8(tab_words, 0))
         for q in (1, 3):
             load_side_by_side(nc.sync, w_sc_rows, 0, wt_scales, q)
         for q in (2, 1, 3):
             load_side_by_side(nc.sync, w_sc_rows, 4, ws_scales, q)
         nc.sync.dma_start(out=wt_in[0][:], in_=wt_words[0].bitcast(I32))
-        nc.sync.dma_start(out=tab[1][:], in_=words8(tab_words, 1))
-        load_ws(1, 0)
+        nc.sync.dma_start(out=tab[:, T : 2 * T], in_=words8(tab_words, 1))
         load_ws(0, 1)
+        load_ws(1, 0)
         load_ws(1, 1)
         nc.sync.dma_start(out=wt_in[1][:], in_=wt_words[1].bitcast(I32))
 
@@ -140,16 +127,21 @@ def tile_list_msg_none_none_kernel(
             return offsets[:, first * CHUNK // 16 : (first + count) * CHUNK // 16]
 
         def picked(s, first, count=1):
-            if first == last and s in LATE:
-                return late[s][:]
+            if first >= 2 and s in late:
+                return late[s][:, (first - 2) * CHUNK : (first - 2 + count) * CHUNK]
             return early[s][:, first * CHUNK : (first + count) * CHUNK]
 
-        def gather_words(s, first, count):
+        def gather_words(s, first, count, spare=0):
             offsets = src_list if s // 2 else dst_list
-            nc.vector.tensor_copy(picked(s, first, count), tab[s % 2][:].bitcast(U32).indirect(listed(offsets, first, count)))
+            window = tab[:, s % 2 * T : (s % 2 + 1) * T + spare].bitcast(U32)
+            nc.vector.tensor_copy(picked(s, first, count), window.indirect(listed(offsets, first, count)))
 
-        def gather_scales(plane, offsets):
-            nc.vector.tensor_copy(plane[:], tab_sc[:].bitcast(U8).indirect(offsets))
+        def gather_scales(part, first, count):
+            for i, offsets in enumerate((dst_list, src_list)):
+                nc.vector.tensor_copy(
+                    picked_sc[part][:, i * count * CHUNK : (i + 1) * count * CHUNK],
+                    tab_sc[:].bitcast(U8).indirect(listed(offsets, first, count)),
+                )
 
 
         def first_pass(c, b, pair, s, opens, closes):
@@ -158,25 +150,24 @@ def tile_list_msg_none_none_kernel(
             slots = 4 if c == 0 else 2
             width = BANK // slots
             edges = slice(pair * width, (pair + 1) * width) if c == 0 else slice(0, CHUNK)
-            within = slice(c * CHUNK + edges.start, c * CHUNK + edges.stop)
+            part = min(c, 1)
+            plane = moved_sc[part][:].bitcast(U8) if a else picked_sc[part][:]
+            at = s // 2 * plane.shape[1] // 2 + (c - part) * CHUNK + edges.start
             for e in range(slots):
                 i = e if c == 0 else 2 * pair + e
                 cols = slice(i * P, (i + 1) * P)
                 if s // 2:
                     lhsT = ws[a][b][:, cols].bitcast(FP8X4)
                     lhsT_scale = w_sc[a][b][4:P, cols]
-                    rhs_scale = src_sc[4 * a : P, within]
                 else:
                     lhsT = wt[a][b][:, cols].bitcast(FP4X4)
                     lhsT_scale = w_sc[a][b][:, cols]
-                    at = within.start - min(c, 2) * CHUNK
-                    rhs_scale = moved_sc[:].bitcast(U8)[:, within] if a else dst_sc[min(c, 2)][:, at : at + width]
                 nc.tensor.matmul_mx(
                     out=acc[:, e * width : (e + 1) * width],
                     lhsT=lhsT,
                     lhsT_scale=lhsT_scale,
                     rhs=picked(s, c)[:, edges].bitcast(FP8X4),
-                    rhs_scale=rhs_scale,
+                    rhs_scale=plane[:, at : at + width],
                     start=(opens and e == 0),
                     stop=(closes and e == slots - 1),
                 )
@@ -230,8 +221,8 @@ def tile_list_msg_none_none_kernel(
 
         deal_ws(0, 0)
         deal_wt(0)
-        deal_ws(1, 0)
         deal_ws(0, 1)
+        deal_ws(1, 0)
         deal_ws(1, 1)
         deal_wt(1)
 
@@ -243,17 +234,14 @@ def tile_list_msg_none_none_kernel(
                 )
 
         def move_plane(queue, part):
-            rows = dst_sc[part][4:116, :].bitcast(I32)
-            first = part * CHUNK // 4
-            queue.dma_start(out=moved_sc[0:112, first : first + rows.shape[1]], in_=rows)
+            queue.dma_start(out=moved_sc[part][0:112, :], in_=picked_sc[part][16:P, :].bitcast(I32))
 
-        for c in range(2):
-            gather_scales(dst_sc[c], listed(dst_list, c, 1))
-            move_plane(nc.gpsimd, c)
+        gather_scales(0, 0, 1)
+        move_plane(nc.gpsimd, 0)
         deal_scales(0)
         deal_scales(1)
-        gather_scales(src_sc, src_list[:])
-        for plane in 3 * [src_sc]:
+        gather_scales(1, 1, last)
+        for plane in 3 * [picked_sc[1]]:
             nc.tensor.matmul_mx(
                 out=banks[6][:],
                 lhsT=ws_in[0, 0][:, 0:P].bitcast(FP8X4),
@@ -263,15 +251,13 @@ def tile_list_msg_none_none_kernel(
                 start=True,
                 stop=True,
             )
-        gather_words(2, 0, 1)
-        gather_words(0, 0, 1)
-        gather_words(2, 1, 2)
-        gather_words(0, 1, 2)
-        gather_words(3, 0, 1)
-        gather_words(1, 0, 1)
-        gather_words(3, 1, 1)
-        gather_words(1, 1, 3)
-        gather_words(3, 2, 2)
+        for steps in ((2, 0), (3, 1)):
+            for c in range(2):
+                for s in steps:
+                    gather_words(s, c, 1)
+        gather_words(2, 2, 2, spare=8)
+        gather_words(0, 2, 2, spare=8)
+        move_plane(nc.sync, 1)
         clear_on_gpsimd(placed[1])
         clear_on_gpsimd(placed[2])
 
@@ -280,23 +266,20 @@ def tile_list_msg_none_none_kernel(
         nc.sync.dma_start(out=wd[:], in_=wd_words.bitcast(I32).rearrange("a p c -> p a c"))
         nc.sync.dma_start(out=weight[:], in_=wgo)
 
-        for b, s in ((0, 2), (0, 0), (1, 0), (0, 3), (1, 2), (1, 3), (0, 1), (1, 1)):
+        for b, s in ((0, 2), (0, 0), (1, 0), (1, 2), (0, 3), (1, 3), (0, 1), (1, 1)):
             for pair in range(2):
                 first_pass(0, b, pair, s, s == (2, 0)[b], s == 1)
-        quantise_first(0)
-        gather_scales(dst_sc[2], listed(dst_list, 2, 2))
-        move_plane(nc.sync, 2)
-        quantise_first(1)
+        for b in range(2):
+            quantise_first(b)
+            gather_words(2 * b + 1, 2, 2)
         clear_on_gpsimd(placed[3])
-        for s in LATE:
-            gather_words(s, last, 1)
         for c in range(last):
             ahead = range(0, last - c)
             behind = range(last - c, N_TILES if c < last - 1 else 2)
-            first_product(c + 1, range(0, AHEAD[c]))
+            first_product(c + 1, range(0, AHEAD))
             for t in ahead:
                 second_product([(c, t)], banks[6 + t % 2])
-            first_product(c + 1, range(AHEAD[c], 16))
+            first_product(c + 1, range(AHEAD, 16))
             quantise(c + 1)
             second_product([(c, t) for t in behind], banks[3])
         for t in (0, 1):

@@ -91,12 +91,12 @@ def tile_list_msg_none_none_kernel(
 
         w_sc_rows = w_sc_in[:].rearrange("p (a n) -> p a n", a=2)
         nc.gpsimd.memset(tab_sc[:], 0)
-        nc.vector.memset(w_sc_in[:], 0)
+        for cols in (slice(0, R // 4 + 1), slice(R // 4 + 1, R // 2)):
+            nc.vector.memset(w_sc_in[:, cols], 0)
         load_side_by_side(nc.gpsimd, w_sc_rows, 4, ws_scales, 0)
         for plane in moved_sc + [wd_sc]:
             nc.vector.memset(plane[:], 0)
-        for cols in (slice(0, T // 2 + 1), slice(T // 2 + 1, T)):
-            nc.vector.memset(placed[0][:, cols].bitcast(I32), 0)
+        nc.vector.memset(placed[0][:].bitcast(I32), 0)
 
         nc.sync.dma_start(dst_list[:], offs2)
         nc.sync.dma_start(src_list[:], offs)

@@ -241,16 +241,6 @@ def tile_list_msg_none_none_kernel(
         deal_scales(0)
         deal_scales(1)
         gather_scales(1, 1, last)
-        for plane in 3 * [picked_sc[1]]:
-            nc.tensor.matmul_mx(
-                out=banks[6][:],
-                lhsT=ws_in[0, 0][:, 0:P].bitcast(FP8X4),
-                lhsT_scale=plane[:, 0:P],
-                rhs=ws_in[0, 0][:].bitcast(FP8X4),
-                rhs_scale=plane[:, 0:BANK],
-                start=True,
-                stop=True,
-            )
         for steps in ((2, 0), (3, 1)):
             for c in range(2):
                 for s in steps:

@@ -21,8 +21,11 @@ CHUNKS = J // CHUNK
 N_TILES = N // P
 ALIGN = 64
 PIECE = 512
+SPARE = 8
 PAD = 32
-AHEAD = 11
+AHEAD = (7, 12, 12)
+TILES_AHEAD = (2, 2, 1)
+SRC, DST = 0, 1
 
 
 def tile_list_msg_none_none_kernel(
@@ -38,39 +41,40 @@ def tile_list_msg_none_none_kernel(
         def kept(name, shape, dtype):
             return keep.tile(shape, dtype, name=name, align_bytes=ALIGN)
 
-        src_list = keep.tile([P, J // 16], U16)
-        dst_list = keep.tile([P, J // 16], U16)
+        def laid(name, shape, dtype, at):
+            return shared.tile(shape, dtype, name=name, offset=at, align_bytes=ALIGN)
+
+        lists = [keep.tile([P, J // 16], U16, name="list%d" % side) for side in (SRC, DST)]
         tab = kept("tab", [P, 2 * T], I32)
         tab_sc = kept("tab_sc", [P, T // 4], I32)
-        ws_in = {(a, b): kept("ws_in%d%d" % (a, b), [P, BANK], I32) for a, b in ((0, 0), (0, 1), (1, 1))}
-        ws_in[1, 0] = shared.tile([P, BANK], I32, name="ws_in10", offset=16384, align_bytes=ALIGN)
+        ws_in = [kept("ws_in0", [P, R], I32), laid("ws_in1", [P, R], I32, 16384)]
         wt_in = [kept("wt_in%d" % a, [P, R // 2], I32) for a in range(2)]
-        w_sc_in = shared.tile([P, 2 * R // 4], I32, name="w_sc_in", offset=32768, align_bytes=ALIGN)
+        w_sc_in = laid("w_sc_in", [P, 2 * R // 4], I32, 32768)
         ws = [[kept("ws%d%d" % (a, b), [P, BANK], U32) for b in range(2)] for a in range(2)]
         wt = [[kept("wt%d%d" % (a, b), [P, BANK], U16) for b in range(2)] for a in range(2)]
         w_sc = [[kept("w_sc%d%d" % (a, b), [P, BANK], U8) for b in range(2)] for a in range(2)]
-        wd = shared.tile([P, 2, N // 2], I32, name="wd", offset=16384 - 1024, align_bytes=ALIGN)
+        wd = laid("wd", [P, 2, N // 2], I32, 16384 - 1024)
         wd_sc = kept("wd_sc", [P, 2, N // 4], I32)
-        weight = shared.tile([P, J], F32, name="weight", offset=16384 + 1024, align_bytes=ALIGN)
+        weight = laid("weight", [P, J], F32, 16384 + 1024)
         picked_sc = [kept("picked_sc0", [P, 2 * CHUNK], U8), kept("picked_sc1", [P, 2 * last * CHUNK], U8)]
         moved_sc = [kept("moved_sc%d" % i, [P, part.shape[1] // 4], I32) for i, part in enumerate(picked_sc)]
-        early = [kept("early%d" % s, [P, 2 * CHUNK if s % 2 else J], U32) for s in range(4)]
-        late = {
-            s: shared.tile([P, 2 * CHUNK], U32, name="late%d" % s, offset=2048 * (s // 2), align_bytes=ALIGN)
-            for s in (1, 3)
+        early = {
+            (side, a): kept("early%d%d" % (side, a), [P, 2 * CHUNK if a else J], U32)
+            for side in (SRC, DST)
+            for a in range(2)
         }
-        first_h = [
-            shared.tile([P, CHUNK * 4 + PAD * b], BF16, name="first_h%d" % b, offset=2048 * b, align_bytes=ALIGN)
-            for b in range(2)
-        ]
-        grouped = {c: kept("grouped%d" % c, [P, 2 * CHUNK * 4], BF16) for c in range(1, CHUNKS)}
+        first_h = laid("first_h", [P, 2 * CHUNK * 4 + PAD], BF16, 0)
+        late = {side: laid("late%d" % side, [P, 2 * CHUNK], U32, 2048 * side) for side in (SRC, DST)}
+        grouped = [first_h] + [kept("grouped%d" % c, [P, 2 * CHUNK * 4], BF16) for c in range(1, CHUNKS)]
         h_codes = [kept("h_codes%d" % c, [P, 2 * CHUNK], U32) for c in range(CHUNKS)]
         h_sc = [kept("h_sc%d" % c, [P, 2 * CHUNK], U8) for c in range(CHUNKS)]
         banks = [psum.tile([P, BANK], F32, name="bank%d" % i) for i in range(8)]
         y_sb = [kept("y%d" % t, [P, J], F32) for t in range(N_TILES)]
-        placed = [kept("placed0", [P, T], F32)] + [
-            shared.tile([P, T], F32, name="placed%d" % t, offset=at, align_bytes=ALIGN)
-            for t, at in ((1, 32768 - 8192 + 64), (2, 32768 + 1024), (3, 4096))
+        placed = [
+            kept("placed0", [P, T], F32),
+            laid("placed1", [P, T], F32, 32768 - 8192 + 64),
+            laid("placed2", [P, T], F32, 32768 + 1024),
+            laid("placed3", [P, T], F32, 4096),
         ]
 
         def rows_of(scales, r):
@@ -82,39 +86,38 @@ def tile_list_msg_none_none_kernel(
         def words8(w, a):
             return w[a].rearrange("p c i -> p (c i)").bitcast(I32)
 
-        def load_ws(a, b):
-            nc.sync.dma_start(out=ws_in[a, b][:], in_=words8(ws_words, a)[:, b * BANK : (b + 1) * BANK])
+        def clear_odd(tile):
+            cut = tile.shape[1] // 2 + 1
+            nc.vector.memset(tile[:, 0:cut], 0)
+            nc.vector.memset(tile[:, cut : tile.shape[1]], 0)
 
         def clear_on_gpsimd(window):
             for col in range(0, T, PIECE):
                 nc.gpsimd.memset(window[:, col : col + PIECE].bitcast(I32), 0)
 
         w_sc_rows = w_sc_in[:].rearrange("p (a n) -> p a n", a=2)
-        nc.gpsimd.memset(tab_sc[:], 0)
-        for cols in (slice(0, R // 4 + 1), slice(R // 4 + 1, R // 2)):
-            nc.vector.memset(w_sc_in[:, cols], 0)
-        load_side_by_side(nc.gpsimd, w_sc_rows, 4, ws_scales, 0)
-        for plane in moved_sc + [wd_sc]:
-            nc.vector.memset(plane[:], 0)
+        nc.vector.memset(w_sc_in[:], 0)
+        for r in (0, 2):
+            load_side_by_side(nc.gpsimd, w_sc_rows, 4, ws_scales, r)
+        clear_odd(tab_sc)
+        clear_odd(moved_sc[1])
+        nc.vector.memset(moved_sc[0][:], 0)
+        nc.vector.memset(wd_sc[:], 0)
         nc.vector.memset(placed[0][:].bitcast(I32), 0)
 
-        nc.sync.dma_start(dst_list[:], offs2)
-        nc.sync.dma_start(src_list[:], offs)
-        load_ws(0, 0)
+        nc.sync.dma_start(lists[SRC][:], offs)
+        nc.sync.dma_start(lists[DST][:], offs2)
+        nc.sync.dma_start(out=tab[:, 0:T], in_=words8(tab_words, 0))
+        for r in range(4):
+            load_side_by_side(nc.sync, w_sc_rows, 0, wt_scales, r)
+        for r in (1, 3):
+            load_side_by_side(nc.sync, w_sc_rows, 4, ws_scales, r)
+        nc.sync.dma_start(out=ws_in[0][:], in_=words8(ws_words, 0))
         for r in range(4):
             nc.sync.dma_start(out=tab_sc[r:P:16, :], in_=rows_of(tab_scales, r))
-        for q in (0, 2):
-            load_side_by_side(nc.sync, w_sc_rows, 0, wt_scales, q)
-        nc.sync.dma_start(out=tab[:, 0:T], in_=words8(tab_words, 0))
-        for q in (1, 3):
-            load_side_by_side(nc.sync, w_sc_rows, 0, wt_scales, q)
-        for q in (2, 1, 3):
-            load_side_by_side(nc.sync, w_sc_rows, 4, ws_scales, q)
         nc.sync.dma_start(out=wt_in[0][:], in_=wt_words[0].bitcast(I32))
         nc.sync.dma_start(out=tab[:, T : 2 * T], in_=words8(tab_words, 1))
-        load_ws(0, 1)
-        load_ws(1, 0)
-        load_ws(1, 1)
+        nc.sync.dma_start(out=ws_in[1][:], in_=words8(ws_words, 1))
         nc.sync.dma_start(out=wt_in[1][:], in_=wt_words[1].bitcast(I32))
 
         def deal(dealt, columns, run):
@@ -123,40 +126,54 @@ def tile_list_msg_none_none_kernel(
                 in_=columns.rearrange("p (g m i) -> p g i m", i=4, m=run),
             )
 
-        def listed(offsets, first, count):
-            return offsets[:, first * CHUNK // 16 : (first + count) * CHUNK // 16]
+        for a in range(2):
+            for b in range(2):
+                deal(ws[a][b][:], ws_in[a][:, b * BANK : (b + 1) * BANK].bitcast(U32), 4)
+            for b in range(2):
+                deal(wt[a][b][:], wt_in[a][:].bitcast(U16)[:, b * BANK : (b + 1) * BANK], 8)
+        for a in range(2):
+            for b in range(2):
+                columns = w_sc_in[:].bitcast(U8)[:, a * R + b * BANK : a * R + (b + 1) * BANK]
+                nc.gpsimd.tensor_copy(
+                    out=w_sc[a][b][:].rearrange("p (i m) -> p i m", i=4), in_=columns.rearrange("p (m i) -> p i m", i=4)
+                )
+        clear_on_gpsimd(placed[1])
+        clear_on_gpsimd(placed[2])
 
-        def picked(s, first, count=1):
-            if first >= 2 and s in late:
-                return late[s][:, (first - 2) * CHUNK : (first - 2 + count) * CHUNK]
-            return early[s][:, first * CHUNK : (first + count) * CHUNK]
+        def listed(side, first, count):
+            return lists[side][:, first * CHUNK // 16 : (first + count) * CHUNK // 16]
 
-        def gather_words(s, first, count, spare=0):
-            offsets = src_list if s // 2 else dst_list
-            window = tab[:, s % 2 * T : (s % 2 + 1) * T + spare].bitcast(U32)
-            nc.vector.tensor_copy(picked(s, first, count), window.indirect(listed(offsets, first, count)))
+        def picked(side, a, first, count=1):
+            if first >= 2 and a:
+                return late[side][:, (first - 2) * CHUNK : (first - 2 + count) * CHUNK]
+            return early[side, a][:, first * CHUNK : (first + count) * CHUNK]
+
+        def gather_words(side, a, first, count, spare=0):
+            window = tab[:, a * T : (a + 1) * T + spare].bitcast(U32)
+            nc.vector.tensor_copy(picked(side, a, first, count), window.indirect(listed(side, first, count)))
 
         def gather_scales(part, first, count):
-            for i, offsets in enumerate((dst_list, src_list)):
+            for side in (SRC, DST):
                 nc.vector.tensor_copy(
-                    picked_sc[part][:, i * count * CHUNK : (i + 1) * count * CHUNK],
-                    tab_sc[:].bitcast(U8).indirect(listed(offsets, first, count)),
+                    picked_sc[part][:, side * count * CHUNK : (side + 1) * count * CHUNK],
+                    tab_sc[:].bitcast(U8).indirect(listed(side, first, count)),
                 )
 
+        def move_plane(part):
+            nc.sync.dma_start(out=moved_sc[part][0:112, :], in_=picked_sc[part][16:P, :].bitcast(I32))
 
-        def first_pass(c, b, pair, s, opens, closes):
-            a = s % 2
+        def first_pass(c, b, pair, side, a, opens, closes):
             acc = banks[2 * b + pair]
             slots = 4 if c == 0 else 2
             width = BANK // slots
             edges = slice(pair * width, (pair + 1) * width) if c == 0 else slice(0, CHUNK)
             part = min(c, 1)
             plane = moved_sc[part][:].bitcast(U8) if a else picked_sc[part][:]
-            at = s // 2 * plane.shape[1] // 2 + (c - part) * CHUNK + edges.start
+            at = side * plane.shape[1] // 2 + (c - part) * CHUNK + edges.start
             for e in range(slots):
                 i = e if c == 0 else 2 * pair + e
                 cols = slice(i * P, (i + 1) * P)
-                if s // 2:
+                if side == SRC:
                     lhsT = ws[a][b][:, cols].bitcast(FP8X4)
                     lhsT_scale = w_sc[a][b][4:P, cols]
                 else:
@@ -166,35 +183,32 @@ def tile_list_msg_none_none_kernel(
                     out=acc[:, e * width : (e + 1) * width],
                     lhsT=lhsT,
                     lhsT_scale=lhsT_scale,
-                    rhs=picked(s, c)[:, edges].bitcast(FP8X4),
+                    rhs=picked(side, a, c)[:, edges].bitcast(FP8X4),
                     rhs_scale=plane[:, at : at + width],
                     start=(opens and e == 0),
                     stop=(closes and e == slots - 1),
                 )
+            rows = grouped[c][:, b * 4 * CHUNK : (b + 1) * 4 * CHUNK]
             if closes and c == 0:
-                rows = first_h[b][:, pair * BANK : (pair + 1) * BANK]
                 nc.scalar.copy(
-                    out=rows.rearrange("p (j i) -> p j i", i=4),
+                    out=rows[:, pair * BANK : (pair + 1) * BANK].rearrange("p (j i) -> p j i", i=4),
                     in_=acc[:].rearrange("p (i j) -> p j i", i=4),
                 )
             elif closes:
-                rows = grouped[c][:, b * 4 * CHUNK : (b + 1) * 4 * CHUNK].rearrange("p (j i) -> p j i", i=4)
                 nc.scalar.copy(
-                    out=rows[:, :, 2 * pair : 2 * pair + 2], in_=acc[:].rearrange("p (e j) -> p j e", e=2)
+                    out=rows.rearrange("p (j i) -> p j i", i=4)[:, :, 2 * pair : 2 * pair + 2],
+                    in_=acc[:].rearrange("p (e j) -> p j e", e=2),
                 )
+
+        terms = ((SRC, 0), (DST, 0), (SRC, 1), (DST, 1))
 
         def first_product(c, steps):
             for step in steps:
-                first_pass(c, step // 8, step // 4 % 2, (0, 2, 3, 1)[step % 4], step % 4 == 0, step % 4 == 3)
+                side, a = terms[step % 4]
+                first_pass(c, step // 8, step // 4 % 2, side, a, step % 4 == 0, step % 4 == 3)
 
         def quantise(c):
-            nc.vector.quantize_mx(out=h_codes[c][:].bitcast(FP8X4), scales=h_sc[c][:], in_=grouped[c][:])
-
-        def quantise_first(b):
-            cols = slice(b * CHUNK, (b + 1) * CHUNK)
-            nc.vector.quantize_mx(
-                out=h_codes[0][:, cols].bitcast(FP8X4), scales=h_sc[0][:, cols], in_=first_h[b][:, 0 : 4 * CHUNK]
-            )
+            nc.vector.quantize_mx(out=h_codes[c][:].bitcast(FP8X4), scales=h_sc[c][:], in_=grouped[c][:, 0 : 2 * CHUNK * 4])
 
         def second_product(pieces, bank):
             for e, (c, t) in enumerate(pieces):
@@ -212,66 +226,38 @@ def tile_list_msg_none_none_kernel(
             for e, (c, t) in enumerate(pieces):
                 nc.scalar.copy(out=y_sb[t][:, c * CHUNK : (c + 1) * CHUNK], in_=bank[:, e * CHUNK : (e + 1) * CHUNK])
 
-        def deal_ws(a, b):
-            deal(ws[a][b][:], ws_in[a, b][:].bitcast(U32), 4)
-
-        def deal_wt(a):
-            for b in range(2):
-                deal(wt[a][b][:], wt_in[a][:].bitcast(U16)[:, b * BANK : (b + 1) * BANK], 8)
-
-        deal_ws(0, 0)
-        deal_wt(0)
-        deal_ws(0, 1)
-        deal_ws(1, 0)
-        deal_ws(1, 1)
-        deal_wt(1)
-
-        def deal_scales(a):
-            for b in range(2):
-                columns = w_sc_in[:].bitcast(U8)[:, a * R + b * BANK : a * R + (b + 1) * BANK]
-                nc.gpsimd.tensor_copy(
-                    out=w_sc[a][b][:].rearrange("p (i m) -> p i m", i=4), in_=columns.rearrange("p (m i) -> p i m", i=4)
-                )
-
-        def move_plane(queue, part):
-            queue.dma_start(out=moved_sc[part][0:112, :], in_=picked_sc[part][16:P, :].bitcast(I32))
-
+        for side in (SRC, DST):
+            gather_words(side, 0, 0, 2)
         gather_scales(0, 0, 1)
-        move_plane(nc.gpsimd, 0)
-        deal_scales(0)
-        deal_scales(1)
+        move_plane(0)
         gather_scales(1, 1, last)
-        for steps in ((2, 0), (3, 1)):
-            for c in range(2):
-                for s in steps:
-                    gather_words(s, c, 1)
-        gather_words(2, 2, 2, spare=8)
-        gather_words(0, 2, 2, spare=8)
-        move_plane(nc.sync, 1)
-        clear_on_gpsimd(placed[1])
-        clear_on_gpsimd(placed[2])
-
-        for q in (0, 2, 1, 3):
-            load_side_by_side(nc.sync, wd_sc, 0, wd_scales, q)
+        for c in range(2):
+            for side in (SRC, DST):
+                gather_words(side, 1, c, 1)
+        for side in (SRC, DST):
+            gather_words(side, 0, 2, 2, spare=SPARE)
+        for r in range(4):
+            load_side_by_side(nc.sync, wd_sc, 0, wd_scales, r)
+        move_plane(1)
         nc.sync.dma_start(out=wd[:], in_=wd_words.bitcast(I32).rearrange("a p c -> p a c"))
         nc.sync.dma_start(out=weight[:], in_=wgo)
 
-        for b, s in ((0, 2), (0, 0), (1, 0), (1, 2), (0, 3), (1, 3), (0, 1), (1, 1)):
-            for pair in range(2):
-                first_pass(0, b, pair, s, s == (2, 0)[b], s == 1)
-        for b in range(2):
-            quantise_first(b)
-            gather_words(2 * b + 1, 2, 2)
+        for a in range(2):
+            for side in (SRC, DST):
+                for b in range(2):
+                    for pair in range(2):
+                        first_pass(0, b, pair, side, a, (side, a) == terms[0], (side, a) == terms[3])
+        quantise(0)
+        for side in (SRC, DST):
+            gather_words(side, 1, 2, 2)
         clear_on_gpsimd(placed[3])
         for c in range(last):
-            ahead = range(0, last - c)
-            behind = range(last - c, N_TILES if c < last - 1 else 2)
-            first_product(c + 1, range(0, AHEAD))
-            for t in ahead:
+            first_product(c + 1, range(0, AHEAD[c]))
+            for t in range(TILES_AHEAD[c]):
                 second_product([(c, t)], banks[6 + t % 2])
-            first_product(c + 1, range(AHEAD, 16))
+            first_product(c + 1, range(AHEAD[c], 16))
             quantise(c + 1)
-            second_product([(c, t) for t in behind], banks[3])
+            second_product([(c, t) for t in range(TILES_AHEAD[c], N_TILES if c < last - 1 else 2)], banks[3])
         for t in (0, 1):
             second_product([(last, t)], banks[6 + t])
         for t in (2, 3):
@@ -282,7 +268,7 @@ def tile_list_msg_none_none_kernel(
         for c, t, chunks in order:
             cols = slice(c * CHUNK, (c + chunks) * CHUNK)
             nc.vector.tensor_tensor(
-                placed[t][:].indirect(listed(dst_list, c, chunks)),
+                placed[t][:].indirect(listed(DST, c, chunks)),
                 y_sb[t][:, cols],
                 weight[:, cols],
                 mybir.AluOpType.mult,

@@ -22,7 +22,7 @@ N_TILES = N // P
 ALIGN = 64
 PIECE = 512
 SPARE = 8
-PAD = 32
+PAD = 64
 AHEAD = (7, 12, 12)
 TILES_AHEAD = (2, 2, 1)
 SRC, DST = 0, 1
@@ -54,7 +54,8 @@ def tile_list_msg_none_none_kernel(
         wt = [[kept("wt%d%d" % (a, b), [P, BANK], U16) for b in range(2)] for a in range(2)]
         w_sc = [[kept("w_sc%d%d" % (a, b), [P, BANK], U8) for b in range(2)] for a in range(2)]
         wd = laid("wd", [P, 2, N // 2], I32, 16384 - 1024)
-        wd_sc = kept("wd_sc", [P, 2, N // 4], I32)
+        wd_sc_flat = kept("wd_sc", [P, N // 2], I32)
+        wd_sc = wd_sc_flat[:].rearrange("p (a n) -> p a n", a=2)
         weight = laid("weight", [P, J], F32, 16384 + 1024)
         picked_sc = [kept("picked_sc0", [P, 2 * CHUNK], U8), kept("picked_sc1", [P, 2 * last * CHUNK], U8)]
         moved_sc = [kept("moved_sc%d" % i, [P, part.shape[1] // 4], I32) for i, part in enumerate(picked_sc)]
@@ -63,9 +64,10 @@ def tile_list_msg_none_none_kernel(
             for side in (SRC, DST)
             for a in range(2)
         }
-        first_h = laid("first_h", [P, 2 * CHUNK * 4 + PAD], BF16, 0)
-        late = {side: laid("late%d" % side, [P, 2 * CHUNK], U32, 2048 * side) for side in (SRC, DST)}
-        grouped = [first_h] + [kept("grouped%d" % c, [P, 2 * CHUNK * 4], BF16) for c in range(1, CHUNKS)]
+        first_h = [laid("first_h%d" % b, [P, CHUNK * 4 + PAD * b], BF16, 2048 * b) for b in range(2)]
+        late_src = [laid("late_src%d" % i, [P, CHUNK], U32, (1024 + 64) * i) for i in range(2)]
+        late_dst = laid("late_dst", [P, 2 * CHUNK], U32, 2048 + 64)
+        grouped = {c: kept("grouped%d" % c, [P, 2 * CHUNK * 4], BF16) for c in range(1, CHUNKS)}
         h_codes = [kept("h_codes%d" % c, [P, 2 * CHUNK], U32) for c in range(CHUNKS)]
         h_sc = [kept("h_sc%d" % c, [P, 2 * CHUNK], U8) for c in range(CHUNKS)]
         banks = [psum.tile([P, BANK], F32, name="bank%d" % i) for i in range(8)]
@@ -74,7 +76,7 @@ def tile_list_msg_none_none_kernel(
             kept("placed0", [P, T], F32),
             laid("placed1", [P, T], F32, 32768 - 8192 + 64),
             laid("placed2", [P, T], F32, 32768 + 1024),
-            laid("placed3", [P, T], F32, 4096),
+            laid("placed3", [P, T], F32, 4096 + 64),
         ]
 
         def rows_of(scales, r):
@@ -96,29 +98,32 @@ def tile_list_msg_none_none_kernel(
                 nc.gpsimd.memset(window[:, col : col + PIECE].bitcast(I32), 0)
 
         w_sc_rows = w_sc_in[:].rearrange("p (a n) -> p a n", a=2)
+        nc.vector.memset(tab_sc[:], 0)
         nc.vector.memset(w_sc_in[:], 0)
-        for r in (0, 2):
-            load_side_by_side(nc.gpsimd, w_sc_rows, 4, ws_scales, r)
-        clear_odd(tab_sc)
+        load_side_by_side(nc.gpsimd, w_sc_rows, 4, ws_scales, 0)
         clear_odd(moved_sc[1])
-        nc.vector.memset(moved_sc[0][:], 0)
-        nc.vector.memset(wd_sc[:], 0)
+        clear_odd(wd_sc_flat)
+        clear_odd(moved_sc[0])
         nc.vector.memset(placed[0][:].bitcast(I32), 0)
 
-        nc.sync.dma_start(lists[SRC][:], offs)
         nc.sync.dma_start(lists[DST][:], offs2)
-        nc.sync.dma_start(out=tab[:, 0:T], in_=words8(tab_words, 0))
-        for r in range(4):
-            load_side_by_side(nc.sync, w_sc_rows, 0, wt_scales, r)
-        for r in (1, 3):
-            load_side_by_side(nc.sync, w_sc_rows, 4, ws_scales, r)
-        nc.sync.dma_start(out=ws_in[0][:], in_=words8(ws_words, 0))
+        nc.sync.dma_start(lists[SRC][:], offs)
         for r in range(4):
             nc.sync.dma_start(out=tab_sc[r:P:16, :], in_=rows_of(tab_scales, r))
+        for r in (0, 2):
+            load_side_by_side(nc.sync, w_sc_rows, 0, wt_scales, r)
+        nc.sync.dma_start(out=tab[:, 0:T], in_=words8(tab_words, 0))
+        nc.sync.dma_start(out=ws_in[0][:], in_=words8(ws_words, 0))
+        for r in (1, 3):
+            load_side_by_side(nc.sync, w_sc_rows, 0, wt_scales, r)
+        for r in (2, 1, 3):
+            load_side_by_side(nc.sync, w_sc_rows, 4, ws_scales, r)
         nc.sync.dma_start(out=wt_in[0][:], in_=wt_words[0].bitcast(I32))
         nc.sync.dma_start(out=tab[:, T : 2 * T], in_=words8(tab_words, 1))
-        nc.sync.dma_start(out=ws_in[1][:], in_=words8(ws_words, 1))
         nc.sync.dma_start(out=wt_in[1][:], in_=wt_words[1].bitcast(I32))
+        for b in range(2):
+            cols = slice(b * BANK, (b + 1) * BANK)
+            nc.sync.dma_start(out=ws_in[1][:, cols], in_=words8(ws_words, 1)[:, cols])
 
         def deal(dealt, columns, run):
             nc.scalar.copy(
@@ -126,11 +131,13 @@ def tile_list_msg_none_none_kernel(
                 in_=columns.rearrange("p (g m i) -> p g i m", i=4, m=run),
             )
 
-        for a in range(2):
+        terms = ((SRC, 0), (DST, 0), (DST, 1), (SRC, 1))
+        for side, a in terms:
             for b in range(2):
-                deal(ws[a][b][:], ws_in[a][:, b * BANK : (b + 1) * BANK].bitcast(U32), 4)
-            for b in range(2):
-                deal(wt[a][b][:], wt_in[a][:].bitcast(U16)[:, b * BANK : (b + 1) * BANK], 8)
+                if side == SRC:
+                    deal(ws[a][b][:], ws_in[a][:, b * BANK : (b + 1) * BANK].bitcast(U32), 4)
+                else:
+                    deal(wt[a][b][:], wt_in[a][:].bitcast(U16)[:, b * BANK : (b + 1) * BANK], 8)
         for a in range(2):
             for b in range(2):
                 columns = w_sc_in[:].bitcast(U8)[:, a * R + b * BANK : a * R + (b + 1) * BANK]
@@ -144,8 +151,10 @@ def tile_list_msg_none_none_kernel(
             return lists[side][:, first * CHUNK // 16 : (first + count) * CHUNK // 16]
 
         def picked(side, a, first, count=1):
+            if first >= 2 and a and side == SRC:
+                return late_src[first - 2][:]
             if first >= 2 and a:
-                return late[side][:, (first - 2) * CHUNK : (first - 2 + count) * CHUNK]
+                return late_dst[:, (first - 2) * CHUNK : (first - 2 + count) * CHUNK]
             return early[side, a][:, first * CHUNK : (first + count) * CHUNK]
 
         def gather_words(side, a, first, count, spare=0):
@@ -188,19 +197,17 @@ def tile_list_msg_none_none_kernel(
                     start=(opens and e == 0),
                     stop=(closes and e == slots - 1),
                 )
-            rows = grouped[c][:, b * 4 * CHUNK : (b + 1) * 4 * CHUNK]
             if closes and c == 0:
                 nc.scalar.copy(
-                    out=rows[:, pair * BANK : (pair + 1) * BANK].rearrange("p (j i) -> p j i", i=4),
+                    out=first_h[b][:, pair * BANK : (pair + 1) * BANK].rearrange("p (j i) -> p j i", i=4),
                     in_=acc[:].rearrange("p (i j) -> p j i", i=4),
                 )
             elif closes:
+                rows = grouped[c][:, b * 4 * CHUNK : (b + 1) * 4 * CHUNK]
                 nc.scalar.copy(
                     out=rows.rearrange("p (j i) -> p j i", i=4)[:, :, 2 * pair : 2 * pair + 2],
                     in_=acc[:].rearrange("p (e j) -> p j e", e=2),
                 )
-
-        terms = ((SRC, 0), (DST, 0), (SRC, 1), (DST, 1))
 
         def first_product(c, steps):
             for step in steps:
@@ -208,7 +215,13 @@ def tile_list_msg_none_none_kernel(
                 first_pass(c, step // 8, step // 4 % 2, side, a, step % 4 == 0, step % 4 == 3)
 
         def quantise(c):
-            nc.vector.quantize_mx(out=h_codes[c][:].bitcast(FP8X4), scales=h_sc[c][:], in_=grouped[c][:, 0 : 2 * CHUNK * 4])
+            nc.vector.quantize_mx(out=h_codes[c][:].bitcast(FP8X4), scales=h_sc[c][:], in_=grouped[c][:])
+
+        def quantise_first(b):
+            cols = slice(b * CHUNK, (b + 1) * CHUNK)
+            nc.vector.quantize_mx(
+                out=h_codes[0][:, cols].bitcast(FP8X4), scales=h_sc[0][:, cols], in_=first_h[b][:, 0 : 4 * CHUNK]
+            )
 
         def second_product(pieces, bank):
             for e, (c, t) in enumerate(pieces):
@@ -226,14 +239,13 @@ def tile_list_msg_none_none_kernel(
             for e, (c, t) in enumerate(pieces):
                 nc.scalar.copy(out=y_sb[t][:, c * CHUNK : (c + 1) * CHUNK], in_=bank[:, e * CHUNK : (e + 1) * CHUNK])
 
-        for side in (SRC, DST):
-            gather_words(side, 0, 0, 2)
         gather_scales(0, 0, 1)
         move_plane(0)
         gather_scales(1, 1, last)
-        for c in range(2):
-            for side in (SRC, DST):
-                gather_words(side, 1, c, 1)
+        for pass_terms in (terms[:2], terms[2:]):
+            for c in range(2):
+                for side, a in pass_terms:
+                    gather_words(side, a, c, 1)
         for side in (SRC, DST):
             gather_words(side, 0, 2, 2, spare=SPARE)
         for r in range(4):
@@ -242,14 +254,15 @@ def tile_list_msg_none_none_kernel(
         nc.sync.dma_start(out=wd[:], in_=wd_words.bitcast(I32).rearrange("a p c -> p a c"))
         nc.sync.dma_start(out=weight[:], in_=wgo)
 
-        for a in range(2):
-            for side in (SRC, DST):
-                for b in range(2):
-                    for pair in range(2):
-                        first_pass(0, b, pair, side, a, (side, a) == terms[0], (side, a) == terms[3])
-        quantise(0)
-        for side in (SRC, DST):
-            gather_words(side, 1, 2, 2)
+        for side, a in terms:
+            for b in range(2):
+                for pair in range(2):
+                    first_pass(0, b, pair, side, a, (side, a) == terms[0], (side, a) == terms[3])
+        quantise_first(0)
+        gather_words(SRC, 1, 2, 1)
+        quantise_first(1)
+        gather_words(DST, 1, 2, 2)
+        gather_words(SRC, 1, 3, 1)
         clear_on_gpsimd(placed[3])
         for c in range(last):
             first_product(c + 1, range(0, AHEAD[c]))

from contextlib import ExitStack

import concourse.mybir as mybir

K, R, N, T, J = 1024, 1024, 512, 2048, 1024
FLOPS = 2 * (2 * K * R * J + R * N * J)

F32 = mybir.dt.float32
BF16 = mybir.dt.bfloat16
I32 = mybir.dt.int32
U32 = mybir.dt.uint32
U16 = mybir.dt.uint16
U8 = mybir.dt.uint8
FP8X4 = mybir.dt.float8_e4m3fn_x4
FP4X4 = mybir.dt.float4_e2m1fn_x4

P = 128
BANK = 512
CHUNK = 256
CHUNKS = J // CHUNK
N_TILES = N // P
ALIGN = 64
PIECE = 512
SPARE = 8
PAD = 64
AHEAD = (7, 12, 12)
TILES_AHEAD = (2, 2, 1)
SRC, DST = 0, 1


def tile_list_msg_none_none_kernel(
    tc, tab_words, tab_scales, ws_words, ws_scales, wt_words, wt_scales, wd_words, wd_scales, wgo, offs, offs2, out
):
    nc = tc.nc
    last = CHUNKS - 1
    with ExitStack() as ctx:
        keep = ctx.enter_context(tc.tile_pool(name="keep", bufs=1))
        shared = ctx.enter_context(tc.tile_pool(name="shared", bufs=1))
        psum = ctx.enter_context(tc.psum_pool(name="psum", bufs=1))

        def kept(name, shape, dtype):
            return keep.tile(shape, dtype, name=name, align_bytes=ALIGN)

        def laid(name, shape, dtype, at):
            return shared.tile(shape, dtype, name=name, offset=at, align_bytes=ALIGN)

        lists = [keep.tile([P, J // 16], U16, name="list%d" % side) for side in (SRC, DST)]
        tab = kept("tab", [P, 2 * T], I32)
        tab_sc = kept("tab_sc", [P, T // 4], I32)
        ws_in = [kept("ws_in0", [P, R], I32), laid("ws_in1", [P, R], I32, 16384)]
        wt_in = [kept("wt_in%d" % a, [P, R // 2], I32) for a in range(2)]
        w_sc_in = laid("w_sc_in", [P, 2 * R // 4], I32, 32768)
        ws = [[kept("ws%d%d" % (a, b), [P, BANK], U32) for b in range(2)] for a in range(2)]
        wt = [[kept("wt%d%d" % (a, b), [P, BANK], U16) for b in range(2)] for a in range(2)]
        w_sc = [[kept("w_sc%d%d" % (a, b), [P, BANK], U8) for b in range(2)] for a in range(2)]
        wd = laid("wd", [P, 2, N // 2], I32, 16384 - 1024)
        wd_sc_flat = kept("wd_sc", [P, N // 2], I32)
        wd_sc = wd_sc_flat[:].rearrange("p (a n) -> p a n", a=2)
        weight = laid("weight", [P, J], F32, 16384 + 1024)
        picked_sc = [kept("picked_sc0", [P, 2 * CHUNK], U8), kept("picked_sc1", [P, 2 * last * CHUNK], U8)]
        moved_sc = [kept("moved_sc%d" % i, [P, part.shape[1] // 4], I32) for i, part in enumerate(picked_sc)]
        early = {
            (side, a): kept("early%d%d" % (side, a), [P, 2 * CHUNK if a else J], U32)
            for side in (SRC, DST)
            for a in range(2)
        }
        first_h = [laid("first_h%d" % b, [P, CHUNK * 4 + PAD * b], BF16, 2048 * b) for b in range(2)]
        late_src = [laid("late_src%d" % i, [P, CHUNK], U32, (1024 + 64) * i) for i in range(2)]
        late_dst = laid("late_dst", [P, 2 * CHUNK], U32, 2048 + 64)
        grouped = {c: kept("grouped%d" % c, [P, 2 * CHUNK * 4], BF16) for c in range(1, CHUNKS)}
        h_codes = [kept("h_codes%d" % c, [P, 2 * CHUNK], U32) for c in range(CHUNKS)]
        h_sc = [kept("h_sc%d" % c, [P, 2 * CHUNK], U8) for c in range(CHUNKS)]
        banks = [psum.tile([P, BANK], F32, name="bank%d" % i) for i in range(8)]
        y_sb = [kept("y%d" % t, [P, J], F32) for t in range(N_TILES)]
        placed = [
            kept("placed0", [P, T], F32),
            laid("placed1", [P, T], F32, 32768 - 8192 + 64),
            laid("placed2", [P, T], F32, 32768 + 1024),
            laid("placed3", [P, T], F32, 4096 + 64),
        ]

        def rows_of(scales, r):
            return scales.bitcast(I32)[:, r:16:4, :].rearrange("a q n -> q a n")

        def load_side_by_side(queue, plane, first, scales, r):
            queue.dma_start(out=plane[first + r : P : 32, :, :], in_=rows_of(scales, r))

        def words8(w, a):
            return w[a].rearrange("p c i -> p (c i)").bitcast(I32)

        def clear_odd(tile):
            cut = tile.shape[1] // 2 + 1
            nc.vector.memset(tile[:, 0:cut], 0)
            nc.vector.memset(tile[:, cut : tile.shape[1]], 0)

        def clear_on_gpsimd(window):
            for col in range(0, T, PIECE):
                nc.gpsimd.memset(window[:, col : col + PIECE].bitcast(I32), 0)

        w_sc_rows = w_sc_in[:].rearrange("p (a n) -> p a n", a=2)
        nc.vector.memset(tab_sc[:], 0)
        nc.vector.memset(w_sc_in[:], 0)
        load_side_by_side(nc.gpsimd, w_sc_rows, 4, ws_scales, 0)
        clear_odd(moved_sc[1])
        clear_odd(wd_sc_flat)
        clear_odd(moved_sc[0])
        nc.vector.memset(placed[0][:].bitcast(I32), 0)

        nc.sync.dma_start(lists[DST][:], offs2)
        nc.sync.dma_start(lists[SRC][:], offs)
        for r in range(4):
            nc.sync.dma_start(out=tab_sc[r:P:16, :], in_=rows_of(tab_scales, r))
        for r in (0, 2):
            load_side_by_side(nc.sync, w_sc_rows, 0, wt_scales, r)
        nc.sync.dma_start(out=tab[:, 0:T], in_=words8(tab_words, 0))
        nc.sync.dma_start(out=ws_in[0][:], in_=words8(ws_words, 0))
        for r in (1, 3):
            load_side_by_side(nc.sync, w_sc_rows, 0, wt_scales, r)
        for r in (2, 1, 3):
            load_side_by_side(nc.sync, w_sc_rows, 4, ws_scales, r)
        nc.sync.dma_start(out=wt_in[0][:], in_=wt_words[0].bitcast(I32))
        nc.sync.dma_start(out=tab[:, T : 2 * T], in_=words8(tab_words, 1))
        nc.sync.dma_start(out=wt_in[1][:], in_=wt_words[1].bitcast(I32))
        for b in range(2):
            cols = slice(b * BANK, (b + 1) * BANK)
            nc.sync.dma_start(out=ws_in[1][:, cols], in_=words8(ws_words, 1)[:, cols])

        def deal(dealt, columns, run):
            nc.scalar.copy(
                out=dealt.rearrange("p (i g m) -> p g i m", i=4, m=run),
                in_=columns.rearrange("p (g m i) -> p g i m", i=4, m=run),
            )

        terms = ((SRC, 0), (DST, 0), (DST, 1), (SRC, 1))
        for side, a in terms:
            for b in range(2):
                if side == SRC:
                    deal(ws[a][b][:], ws_in[a][:, b * BANK : (b + 1) * BANK].bitcast(U32), 4)
                else:
                    deal(wt[a][b][:], wt_in[a][:].bitcast(U16)[:, b * BANK : (b + 1) * BANK], 8)
        for a in range(2):
            for b in range(2):
                columns = w_sc_in[:].bitcast(U8)[:, a * R + b * BANK : a * R + (b + 1) * BANK]
                nc.gpsimd.tensor_copy(
                    out=w_sc[a][b][:].rearrange("p (i m) -> p i m", i=4), in_=columns.rearrange("p (m i) -> p i m", i=4)
                )
        clear_on_gpsimd(placed[1])
        clear_on_gpsimd(placed[2])

        def listed(side, first, count):
            return lists[side][:, first * CHUNK // 16 : (first + count) * CHUNK // 16]

        def picked(side, a, first, count=1):
            if first >= 2 and a and side == SRC:
                return late_src[first - 2][:]
            if first >= 2 and a:
                return late_dst[:, (first - 2) * CHUNK : (first - 2 + count) * CHUNK]
            return early[side, a][:, first * CHUNK : (first + count) * CHUNK]

        def gather_words(side, a, first, count, spare=0):
            window = tab[:, a * T : (a + 1) * T + spare].bitcast(U32)
            nc.vector.tensor_copy(picked(side, a, first, count), window.indirect(listed(side, first, count)))

        def gather_scales(part, first, count):
            for side in (SRC, DST):
                nc.vector.tensor_copy(
                    picked_sc[part][:, side * count * CHUNK : (side + 1) * count * CHUNK],
                    tab_sc[:].bitcast(U8).indirect(listed(side, first, count)),
                )

        def move_plane(part):
            nc.sync.dma_start(out=moved_sc[part][0:112, :], in_=picked_sc[part][16:P, :].bitcast(I32))

        def first_pass(c, b, pair, side, a, opens, closes):
            acc = banks[2 * b + pair]
            slots = 4 if c == 0 else 2
            width = BANK // slots
            edges = slice(pair * width, (pair + 1) * width) if c == 0 else slice(0, CHUNK)
            part = min(c, 1)
            plane = moved_sc[part][:].bitcast(U8) if a else picked_sc[part][:]
            at = side * plane.shape[1] // 2 + (c - part) * CHUNK + edges.start
            for e in range(slots):
                i = e if c == 0 else 2 * pair + e
                cols = slice(i * P, (i + 1) * P)
                if side == SRC:
                    lhsT = ws[a][b][:, cols].bitcast(FP8X4)
                    lhsT_scale = w_sc[a][b][4:P, cols]
                else:
                    lhsT = wt[a][b][:, cols].bitcast(FP4X4)
                    lhsT_scale = w_sc[a][b][:, cols]
                nc.tensor.matmul_mx(
                    out=acc[:, e * width : (e + 1) * width],
                    lhsT=lhsT,
                    lhsT_scale=lhsT_scale,
                    rhs=picked(side, a, c)[:, edges].bitcast(FP8X4),
                    rhs_scale=plane[:, at : at + width],
                    start=(opens and e == 0),
                    stop=(closes and e == slots - 1),
                )
            if closes and c == 0:
                nc.scalar.copy(
                    out=first_h[b][:, pair * BANK : (pair + 1) * BANK].rearrange("p (j i) -> p j i", i=4),
                    in_=acc[:].rearrange("p (i j) -> p j i", i=4),
                )
            elif closes:
                rows = grouped[c][:, b * 4 * CHUNK : (b + 1) * 4 * CHUNK]
                nc.scalar.copy(
                    out=rows.rearrange("p (j i) -> p j i", i=4)[:, :, 2 * pair : 2 * pair + 2],
                    in_=acc[:].rearrange("p (e j) -> p j e", e=2),
                )

        def first_product(c, steps):
            for step in steps:
                side, a = terms[step % 4]
                first_pass(c, step // 8, step // 4 % 2, side, a, step % 4 == 0, step % 4 == 3)

        def quantise(c):
            nc.vector.quantize_mx(out=h_codes[c][:].bitcast(FP8X4), scales=h_sc[c][:], in_=grouped[c][:])

        def quantise_first(b):
            cols = slice(b * CHUNK, (b + 1) * CHUNK)
            nc.vector.quantize_mx(
                out=h_codes[0][:, cols].bitcast(FP8X4), scales=h_sc[0][:, cols], in_=first_h[b][:, 0 : 4 * CHUNK]
            )

        def second_product(pieces, bank):
            for e, (c, t) in enumerate(pieces):
                for b in range(2):
                    cols = slice(b * CHUNK, (b + 1) * CHUNK)
                    nc.tensor.matmul_mx(
                        out=bank[:, e * CHUNK : (e + 1) * CHUNK],
                        lhsT=wd[:, b, :].bitcast(U8)[:, 2 * P * t : 2 * P * (t + 1)].bitcast(FP4X4),
                        lhsT_scale=wd_sc[:, b, :].bitcast(U8)[:, P * t : P * (t + 1)],
                        rhs=h_codes[c][:, cols].bitcast(FP8X4),
                        rhs_scale=h_sc[c][:, cols],
                        start=(b == 0),
                        stop=(b == 1),
                    )
            for e, (c, t) in enumerate(pieces):
                nc.scalar.copy(out=y_sb[t][:, c * CHUNK : (c + 1) * CHUNK], in_=bank[:, e * CHUNK : (e + 1) * CHUNK])

        gather_scales(0, 0, 1)
        move_plane(0)
        gather_scales(1, 1, last)
        for pass_terms in (terms[:2], terms[2:]):
            for c in range(2):
                for side, a in pass_terms:
                    gather_words(side, a, c, 1)
        for side in (SRC, DST):
            gather_words(side, 0, 2, 2, spare=SPARE)
        for r in range(4):
            load_side_by_side(nc.sync, wd_sc, 0, wd_scales, r)
        move_plane(1)
        nc.sync.dma_start(out=wd[:], in_=wd_words.bitcast(I32).rearrange("a p c -> p a c"))
        nc.sync.dma_start(out=weight[:], in_=wgo)

        for side, a in terms:
            for b in range(2):
                for pair in range(2):
                    first_pass(0, b, pair, side, a, (side, a) == terms[0], (side, a) == terms[3])
        quantise_first(0)
        gather_words(SRC, 1, 2, 1)
        quantise_first(1)
        gather_words(DST, 1, 2, 2)
        gather_words(SRC, 1, 3, 1)
        clear_on_gpsimd(placed[3])
        for c in range(last):
            first_product(c + 1, range(0, AHEAD[c]))
            for t in range(TILES_AHEAD[c]):
                second_product([(c, t)], banks[6 + t % 2])
            first_product(c + 1, range(AHEAD[c], 16))
            quantise(c + 1)
            second_product([(c, t) for t in range(TILES_AHEAD[c], N_TILES if c < last - 1 else 2)], banks[3])
        for t in (0, 1):
            second_product([(last, t)], banks[6 + t])
        for t in (2, 3):
            second_product([(last - 1, t), (last, t)], banks[t + 2])

        order = [(c, t, 1) for c in range(last - 1) for t in range(N_TILES)]
        order = order + [(c, t, 1) for c in (last - 1, last) for t in (0, 1)] + [(last - 1, t, 2) for t in (2, 3)]
        for c, t, chunks in order:
            cols = slice(c * CHUNK, (c + chunks) * CHUNK)
            nc.vector.tensor_tensor(
                placed[t][:].indirect(listed(DST, c, chunks)),
                y_sb[t][:, cols],
                weight[:, cols],
                mybir.AluOpType.mult,
            )
            if c + chunks == CHUNKS:
                nc.sync.dma_start(out=out[t * P : (t + 1) * P, :], in_=placed[t][:])
